import numpy as np, ml_dtypes
CORES = [3,11,19,27,35,43,51,59]
N = 8
import mx_ref
BF = ml_dtypes.bfloat16
def gcols(t, e):
    v = np.concatenate([t.reshape(8, 16, -1, 4), np.zeros((8, 16, 1, 4), BF)], axis=2)
    return np.ascontiguousarray(np.stack([v[g][:, e[g]] for g in range(8)])).reshape(128, -1)
def tile(rs):
    return np.stack(rs, axis=2).reshape(128, -1).astype(BF)
def pick(q, e):
    c = np.concatenate([q[0].reshape(128, -1, 4), np.zeros((128, 1, 4), np.uint8)], axis=1); s = np.concatenate([q[1], np.ones((16, 1), np.uint8)], axis=1)
    return (np.ascontiguousarray(c[:, e].reshape(128, -1)), np.ascontiguousarray(s[:, e]))
def join(*qs):
    return (np.concatenate([q[0] for q in qs], axis=1), np.concatenate([q[1] for q in qs], axis=1))
def put(q, e, v):
    c, s = q[0].reshape(128, -1, 4).copy(), q[1].copy(); c[:, e] = v[0].reshape(128, -1, 4); s[:, e] = v[1]
    return (c.reshape(128, -1), s)
def pk(c, s):
    return (np.ascontiguousarray(c), mx_ref.live(s))
def emit(q):
    return q[0], q[1]
def packed(v, rng):
    q = [mx_ref.quantize(np.ascontiguousarray(v[r])) for r in range(N)]
    return np.stack([a for a, b in q]), np.stack([mx_ref.plane(b, rng) for a, b in q])
def values_of_codes():
    e, c = np.zeros((128, 128, 4), np.float32), np.zeros((128, 2, 4), np.uint8)
    e[np.arange(128), np.arange(128), 0] = 1
    c[:127, :, 0] = np.arange(256).reshape(2, 128).T[:127]
    return mx_ref.matmul(mx_ref.quantize(e.reshape(128, 512).astype(BF)), (c.reshape(128, 8), np.full((16, 2), 127, np.uint8))).T.reshape(-1).astype(np.float64)
CODE_VALUE, SCALE_VALUE = values_of_codes(), 2.0 ** (np.arange(256) - 127.0)
def decode(q):
    return (CODE_VALUE[q[0]].reshape(16, 8, -1, 4) * SCALE_VALUE[q[1]][:, None, :, None] + 0.0).reshape(128, -1).astype(np.float32)
def f(rng, *shape):
    return mx_ref.flush((rng.standard_normal(shape, dtype=np.float32) * np.exp2(rng.integers(-2, 3, shape[:-1] + (1,)))).astype(BF))
def wide(rng, *shape, cols=0):
    v = rng.standard_normal(shape, dtype=np.float32) * np.exp2(rng.integers(-12, 13, shape)).astype(np.float32)
    if cols: v *= np.repeat(np.exp2(rng.integers(-cols, cols + 1, shape[:-2] + (1, shape[-1] // 4))) * (rng.random(shape[:-2] + (1, shape[-1] // 4)) > 0.0625), 4, axis=-1).astype(np.float32)
    return mx_ref.flush(v.astype(BF))
C, E = 384, 8
def big(v):
    v = v.astype(np.float32)
    v[np.abs(v) < np.float32(2.0 ** -16)] = 0
    return v.astype(BF)
def numbers_of(rng):
    return big(f(rng, N, 128, 4 * C)), big(f(rng, N, 128, 128)), np.array(f(rng, N, 128, 512)), np.array(f(rng, N, 128, 512))
def layers(rng):
    return big(f(rng, N, 128, 2048)).reshape(N, 8, 16, 4, 8, 16, 4)
def some(rng, k):
    return np.argsort(np.argsort(rng.random((8, 32)), axis=1), axis=1) < k
def flags(rng):
    k = np.where(some(rng, E // 2), -1.0, rng.random((N, 8, 32)))
    fl = np.ones((N, 8, 32), np.int32)
    np.put_along_axis(fl, np.argsort(k, axis=2)[:, :, :E], 0, axis=2)
    return fl
def relabels(rng):
    return np.argsort(rng.random((N, 7, 32, 32)), axis=3)
def drawn(rng, x, tr, u, v, fl, w, ti=None):
    t = tr.astype(np.float32).reshape(N, 8, 16, 32, 4).copy()
    t[np.broadcast_to((fl == 0)[:, :, None, :, None], t.shape)] = 0
    if ti is None: ti = relabels(rng)
    c, p = packed(np.ascontiguousarray(w).reshape(N, 128, 2048), rng)
    return {"x": np.ascontiguousarray(x).reshape(N, 128, 4 * C).astype(BF), "tr": t.reshape(N, 128, 128).astype(BF), "u": np.ascontiguousarray(u).reshape(N, 128, 512), "v": v, "fl": fl, "ti": ti.reshape(N, 7, 1024).astype(np.int32), "wc": c, "ws": p}
def setup_inputs(rng):
    x, tr, u, v = numbers_of(rng)
    return drawn(rng, x, tr, u, v, flags(rng), layers(rng))
def setup_inputs_ties(rng):
    x, tr, u, v = numbers_of(rng)
    o = rng.permutation(N)
    x = x.reshape(N, 8, 16, C, 4)
    for r in range(N):
        a = x[r][:, :8, :24].copy()
        a[:, :, 23] = 0
        k = rng.permutation(C) % 24
        if r == o[0]: k = np.zeros(C, int)
        if r == o[1]: k = np.full(C, 23)
        x[r][:, :8] = a[:, :, k]
    u = u.reshape(N, 8, 16, 128, 4)
    for i in range(5): u[:, :, 8:, i::16] = 0
    w = layers(rng)
    w[:, :, :, :, :, :8] = 0
    return drawn(rng, x, tr, u, v, flags(rng), w)
def setup_inputs_near(rng):
    x, tr, u, v = numbers_of(rng)
    fl, ti = flags(rng), relabels(rng)
    a = int(rng.integers(N))
    fl[(a + 1) % N] = fl[a]
    o = rng.permutation(N) % 2
    x = x.astype(np.float32).reshape(N, 8, 16, C, 4)
    tr = tr.astype(np.float32).reshape(N, 8, 16, 32, 4)
    x[:, :, :8] = 0
    tr[:, :, :8] = 0
    u = u.reshape(N, 128, 128, 4)
    for i in range(5): u[:, :, i::16] = 0
    for r in range(N):
        k = 2.0 ** -30 if o[r] == 0 else 1.0
        x[r, :, :5, :, 0] = k * rng.integers(-1, 2, (8, 5, C))
        tr[r, :, :5, :, 0] = k * rng.integers(-1, 2, (8, 5, 32))
        for g in rng.permutation(8)[:4]: x[r, g, :5, rng.integers(C), 0] = 2.0 ** 27 * rng.choice([-1.0, 1.0], 5)
        for h in range(0, 128, 16):
            for i in range(5): u[r, h + i, h + i, 0] = k
    hole = np.stack([np.flatnonzero(fl[a, g] == 0) for g in range(8)])
    held = np.stack([np.flatnonzero(fl[a, g] == 1) for g in range(8)])
    n = np.arange(8 * E)
    b = held[np.arange(8)[:, None], rng.integers(0, 32 - E, (8, 8 * E))]
    b[n // E, n] = hole[n // E, n % E]
    back = np.argsort(ti[a], axis=2)
    e = b.copy()
    for g in range(8):
        for h in range(g - 1, -1, -1): e[g] = back[h, b[h], e[g]]
    bit = (e[:, None] >> np.arange(4, -1, -1)[:, None]) & 1
    j = rng.permutation(C)[:8 * E]
    s = x[a, :, :5, :, 0]
    m = np.abs(s[:, :, j])
    s[:, :, j] = np.where(bit == 1, np.maximum(m, 2.0 ** -30 if o[a] == 0 else 1.0), 0.0 - m)
    x[a, :, :5, :, 0] = s
    w = layers(rng)
    w[:, :, :8] = 0
    w[:, :, :, :, :, :8] = 0
    return drawn(rng, x, tr, u, v, fl, w, ti)
def setup_inputs_deep(rng):
    x, tr, u, v = numbers_of(rng)
    x = (rng.integers(0, 2, x.shape) * 2.0 - 1.0) * (0.8 + 0.2 * rng.random(x.shape)) * 2.0 ** 26
    tr = (rng.integers(0, 2, tr.shape) * 2.0 - 1.0) * (0.8 + 0.2 * rng.random(tr.shape)) * 2.0 ** 26
    u = (rng.integers(0, 2, u.shape) * 2.0 - 1.0) * (0.9 + 0.1 * rng.random(u.shape)) * 2.0 ** 30
    o = rng.permutation(N)
    m = some(rng, E)
    fl = np.ones((N, 8, 32), np.int32)
    for r in range(N):
        if r == o[1]: fl[r, 7][m[7]] = 0
        elif r == o[2]: fl[r, 0][m[0]] = 0
        elif r != o[0]: fl[r][m] = 0
    w = (layers(rng).astype(np.float32) * np.float32(0.0625)).astype(BF)
    return drawn(rng, x.astype(np.float32), tr.astype(np.float32), u.astype(np.float32).astype(BF), v, fl, w)
def setup_inputs_odd(rng):
    x, tr, u, v = numbers_of(rng)
    x = (1.125 + 0.25 * rng.integers(0, 4, (N, 16, 8, C, 4))) * np.exp2(-rng.integers(8, 15, (N, 16, 8, C, 4)).astype(np.float32))
    x[:, :, 0, :, 0] = 1.96875
    x = x * (rng.integers(0, 2, x.shape) * 2.0 - 1.0) * np.exp2(rng.integers(-2, 3, (N, 16, 1, C, 1)).astype(np.float32))
    return drawn(rng, x.astype(np.float32), tr, u, v, flags(rng), layers(rng))
def setup_inputs_spread(rng):
    x, tr, u, v = numbers_of(rng)
    return drawn(rng, big(wide(rng, N, 128, 4 * C, cols=6)), big(wide(rng, N, 128, 128)), u, v, flags(rng), layers(rng))
def check_inputs(d):
    b = []
    for k in ("x", "tr", "u", "v"):
        a = np.abs(d[k].astype(np.float32))
        if not (np.isfinite(a).all() and ((a == 0) | (a >= 2.0 ** -30) & (a <= 2.0 ** 30)).all()): b.append("a value of " + k)
    fl = d["fl"]
    if not ((fl == 0) | (fl == 1)).all(): b.append("a flag of fl")
    if (np.sum(fl == 0, axis=2) > E).any(): b.append("too many empty slots in a level")
    if ((d["tr"].astype(np.float32).reshape(N, 8, 16, 32, 4) != 0) & (fl == 0)[:, :, None, :, None]).any(): b.append("tr isn't zero at an empty slot")
    if (np.sort(d["ti"].reshape(N, 7, 32, 32), axis=3) != np.arange(32)).any(): b.append("ti: not the points in some order")
    none, least, most = [emit(mx_ref.quantize(np.full((128, 16), k, np.float32).astype(BF)))[1][0, 0] for k in (0.0, 2.0 ** -30, 2.0 ** 30)]
    for r in range(N):
        if ((d["wc"][r] == 0x7F) | (d["wc"][r] == 0xFF)).any(): b.append("wc: a code that is no number")
        s = mx_ref.live(d["ws"][r])
        if ((s != none) & ((s < least) | (s > most))).any(): b.append("ws: a scale out of range")
    return b
def reference(x, tr, u, v, fl, ti, wc, ws):
    qu = [mx_ref.quantize(u[r]) for r in range(N)]
    lay = [pk(wc[r], ws[r]) for r in range(N)]
    now = [x[r] for r in range(N)]
    slot = [decode(mx_ref.quantize(tr[r])).astype(BF) for r in range(N)]
    full = fl > 0
    way = np.zeros((N, 8, C), np.int64)
    for t in range(3):
        claim, came = [], []
        for r in range(N):
            q = mx_ref.quantize(now[r])
            own = decode(q)
            s = mx_ref.matmul(qu[r], q)
            e = 16 * (s[0::16] > 0) + 8 * (s[1::16] > 0) + 4 * (s[2::16] > 0) + 2 * (s[3::16] > 0) + (s[4::16] > 0)
            fail = np.full(C, 8)
            for g in range(8):
                going = fail == 8
                way[r, g] = np.where(going, e[g], -1)
                fail = np.where(going & ~full[r, g][e[g]], g, fail)
                if g < 7: e[g + 1:] = ti[r, g][32 * e[g] + e[g + 1:]]
            passed = np.where(np.arange(8)[:, None] < fail, way[r], -1)
            z = (own - gcols(slot[r], passed).astype(np.float32)).astype(BF)
            q = mx_ref.quantize(z)
            c = np.full((8, 32), C)
            j = np.flatnonzero(fail < 8)
            np.minimum.at(c, (fail[j], way[r][fail[j], j]), j)
            claim.append(c < C)
            came.append(gcols(decode(q).astype(BF), np.where(c < C, c, -1)))
            now[r] = tile([mx_ref.matmul(pick(lay[r], np.arange(128 * b, 128 * b + 128)), q) * np.float32(0.015625) + z[:, b::4].astype(np.float32) for b in range(4)])
        for r in range(N):
            take = claim[(r - 1) % N] & ~full[r]
            slot[r] = gcols(np.concatenate([slot[r], came[(r - 1) % N]], axis=1), np.arange(32) + 32 * take)
            full[r] = full[r] | take
    y, bp, rt = np.zeros((N, 128, C), np.float32), np.zeros((N, 8, C + 32), np.float32), np.zeros((N, 128, 128), np.float32)
    oc, osc = np.zeros((N, 128, 4 * C), np.uint8), np.zeros((N, 16, C), np.uint8)
    for r in range(N):
        q = mx_ref.quantize(now[r])
        y[r] = mx_ref.matmul(mx_ref.quantize(v[r]), q)
        bp[r] = np.concatenate([way[r], full[r]], axis=1)
        rt[r] = slot[r].astype(np.float32)
        oc[r], osc[r] = emit(q)
    return {"y": y, "bp": bp, "rt": rt, "oc": oc, "osc": osc}

@@ -1,0 +1,538 @@
+import math
+from concourse.bass import DstId, RemoteDMATransfer
+from concourse.mybir import dt, AluOpType, AxisListType, ActivationFunctionType
+
+ROUNDS, C = 3, 384
+SHARE, FSL, NZ = (3, 3, 2, 2, 1, 1, 0), (3, 4), 1
+KIND = {"f": "float32", "b": "bfloat16", "i": "int32", "h": "uint16", "s": "uint8", "c": "float8_e4m3fn_x4"}
+SPEC = """b xt 1536 ut 512 vt 512 trt 512 et 2048 ent 2048 ct 512 bt 512 win 7168 tab 64 tat 64 res 1792 trb 1792 ow 768
+b ores 512 otr 512 fp 32 lf 32 gt 768 zt 1536 zp 1600 mw 256 mm 768 pr 768 jnk 384 lim 64 ctl 512 zero 512 lw 64 tw 2304
+b bw 128 me 4 nx 4
+c qxc 384 quc 128 qvc 128 qtc 128 wq 512 ec 512 enc 512 ctc 128 bc 128 qzc 384 qcc0 128 qcc1 128 qcc2 128 lc0 160 lc1 160 lc2 160
+s qxs 384 qus 128 qvs 128 qts 128 wp 512 es 512 ens 512 cts 128 bs 128 qzs 384 qcs0 128 qcs1 128 qcs2 128 ls0 160 ls1 160 ls2 160
+i tia 32 tib 32 pidx 1 pint 2 flw 2
+h occ 32 lu 32 ol 24 clu 2 tl 4 tlf 4 of0 28 of1 28 of2 28 of3 28 of4 28 of5 28 of6 28
+f ones 128 idn 128 fs 768 cnt 2 tk 2 rtt 128 yt 384 bpt 384 full 2 pf 2 hrow 7 s16 2 l16 2 i128 128 w5 8 mh 8"""
+PSUM = ("ps", "pe", "pf0", "pf1", "pf2", "pf3", "pd0", "pd1")
+SCRATCH = {"tdr": ("dram", [160, 32], "bfloat16")}
+for _n in ("fo", "fd0", "fd1"):
+    SCRATCH[_n] = ("dram", [2, 128, 2], "bfloat16")
+for _l in SPEC.split("\n"):
+    _w = _l.split()
+    for _k in range(1, len(_w), 2):
+        SCRATCH[_w[_k]] = ("sbuf", [128, int(_w[_k + 1])], KIND[_w[0]])
+for _n in PSUM:
+    SCRATCH[_n] = ("psum", [128, 512], "float32")
+DMAS = "dx du dti dtr dw dfl dfo dow0 dv dw0 dw1 dtd dw2 dw4 dl0 dl1 dl2 dlr0 dlr1 dlw0 dlw1 dout".split()
+SEMAPHORES = "cv ca ct_ cp loc rn rf0 rf1 rf2 rc0 rc1 rc2 rs0 rs1 rs2".split() + DMAS
+
+ADD, SUB, MUL, MAX, MIN = AluOpType.add, AluOpType.subtract, AluOpType.mult, AluOpType.max, AluOpType.min
+EQ, NE, GT, GE = AluOpType.is_equal, AluOpType.not_equal, AluOpType.is_gt, AluOpType.is_ge
+COPY = ActivationFunctionType.Copy
+
+
+def rank_program(g, core, T, topo):
+    rank = T.rank_of(core)
+    if rank is None:
+        return
+    nxt, prv = T.cores[(rank + 1) % len(T.cores)], T.cores[(rank - 1) % len(T.cores)]
+    eng = {"V": g.vector, "A": g.scalar, "T": g.tensor, "S": g.sync, "P": g}
+    semof = {"V": "cv", "A": "ca", "T": "ct_", "P": "cp"}
+    total = {}
+    known = {q: {} for q in eng}
+    clock = {}
+    wr, rd = {}, {}
+
+    def hit(a, b):
+        return a[0] < b[1] and b[0] < a[1] and a[2] < b[3] and b[2] < a[3] and (a[2] - b[2]) % math.gcd(a[4], b[4]) == 0
+
+    def covers(a, b):
+        return a[4] == 1 and a[0] <= b[0] and b[1] <= a[1] and a[2] <= b[2] and b[3] <= a[3]
+
+    def learn(q, sem, val):
+        k = known[q]
+        if k.get(sem, 0) >= val:
+            return
+        if sem in DMAS:
+            val = total[sem]
+        eng[q].wait_ge(T.sem[sem], val)
+        k[sem] = val
+        for (s, x), c in clock.items():
+            if s == sem and x <= val and (sem in DMAS or x == val):
+                for s2, x2 in c.items():
+                    if k.get(s2, 0) < x2:
+                        k[s2] = x2
+
+    def need(q, outs, ins):
+        toks = {}
+
+        def add(e):
+            toks[e[2]] = max(toks.get(e[2], 0), e[3])
+        for name, reg in ins:
+            for e in wr.get(name, []):
+                if hit(reg, e[0]):
+                    add(e)
+            if name in PSUM:
+                for e in rd.get(name, []):
+                    if e[1] != q:
+                        add(e)
+        for name, reg in outs:
+            for e in wr.get(name, []) + rd.get(name, []):
+                if name in PSUM or hit(reg, e[0]):
+                    add(e)
+        for s in sorted(toks):
+            learn(q, s, toks[s])
+
+    def note(q, outs, ins, sem, val):
+        for name, reg in outs:
+            wr[name] = [e for e in wr.get(name, []) if not covers(reg, e[0])] + [(reg, q, sem, val)]
+            rd[name] = [e for e in rd.get(name, []) if not covers(reg, e[0])]
+        for name, reg in ins:
+            rd.setdefault(name, []).append((reg, q, sem, val))
+
+    def regs(vs):
+        out = []
+        for e in vs:
+            out += e[1]
+        return out
+
+    def run(q, fn, outs, ins):
+        o, i = regs(outs), regs(ins)
+        need(q, o, i)
+        sem = semof[q]
+        total[sem] = total.get(sem, 0) + 1
+        clock[(sem, total[sem])] = dict(known[q])
+        fn().then_inc(T.sem[sem], 1)
+        note(q, o, i, sem, total[sem])
+
+    def dma(q, sem, out, in_):
+        o, i = regs([out]), regs([in_])
+        need(q, o, i)
+        total[sem] = total.get(sem, 0) + 16
+        clock[(sem, total[sem])] = dict(known[q])
+        eng[q].dma_start(out[0], in_[0]).then_inc(T.sem[sem], 16)
+        note(q, o, i, sem, total[sem])
+
+    def v(name, a, b, s=1, p=(0, 128)):
+        t = T[name]
+        return (t[p[0]:p[1], a:b:s] if s != 1 else t[p[0]:p[1], a:b], [(name, (p[0], p[1], a, b, s))])
+
+    def codes(name, a, b):
+        return (T[name][:, a:b].bitcast(dt.uint8), [(name, (0, 128, a, b, 1))])
+
+    def rows(name, a, b):
+        return (T[name][a:b, :], [(name, (a, b, 0, 32, 1))])
+
+    def slot(name, k=None):
+        return (T[name][:], [(name, (0, 2, 0, 256, 1))]) if k is None else (T[name][k], [(name, (k, k + 1, 0, 256, 1))])
+
+    def inp(ap):
+        return (ap, [])
+
+    def ind(win, off):
+        return (win[0].indirect(off[0]), win[1] + off[1])
+
+    def copy(out, in_):
+        run("V", lambda: g.vector.tensor_copy(out[0], in_[0]), [out], [in_])
+
+    def act(out, in_, scale=1.0):
+        run("A", lambda: g.scalar.activation(out[0], in_[0], COPY, scale=scale) if scale != 1.0 else g.scalar.activation(out[0], in_[0], COPY), [out], [in_])
+
+    def tt(out, a, b, op):
+        run("V", lambda: g.vector.tensor_tensor(out[0], a[0], b[0], op), [out], [a, b])
+
+    def ts(out, a, s1, op0, s2=None, op1=None):
+        ins = [a] + [s for s in (s1, s2) if isinstance(s, tuple)]
+        x1 = s1[0] if isinstance(s1, tuple) else s1
+        x2 = s2[0] if isinstance(s2, tuple) else s2
+        if op1 is None:
+            run("V", lambda: g.vector.tensor_scalar(out[0], a[0], x1, None, op0), [out], ins)
+        else:
+            run("V", lambda: g.vector.tensor_scalar(out[0], a[0], x1, x2, op0, op1), [out], ins)
+
+    def fill(out, c):
+        run("V", lambda: g.vector.memset(out[0], c), [out], [])
+
+    def quant(c, s, in_):
+        run("V", lambda: g.vector.quantize_mx(c[0], s[0], in_[0]), [c, s], [in_])
+
+    def mx(out, lc, ls, rc, rs):
+        run("T", lambda: g.tensor.matmul_mx(out[0], lc[0], ls[0], rc[0], rs[0], True, True), [out], [lc, ls, rc, rs])
+
+    def pair(c, s, a, b):
+        return v(c, a, b), v(s, a, b)
+
+    def turn(out, in_):
+        run("V", lambda: g.vector.transpose(out[0], in_[0]), [out], [in_])
+
+    def iota(out, pattern, base, cm):
+        run("P", lambda: g.iota(out[0], pattern, base, cm, allow_small_or_imprecise_dtypes=True), [out], [])
+
+    def one(G, k=1):
+        return (16 * G, 16 * G + k)
+
+    dma("S", "dti", v("tia", 0, 32), inp(T.ti[0:4, :]))
+    dma("A", "dti", v("tib", 0, 32, p=(0, 96)), inp(T.ti[4:7, :]))
+    dma("S", "dx", v("xt", 0, 1536), inp(T.x[:]))
+    dma("A", "du", v("ut", 0, 512), inp(T.u[:]))
+    dma("S", "dtr", v("trt", 0, 128), inp(T.tr[:]))
+    dma("S", "dfl", v("flw", 0, 2), inp(T.fl[:]))
+
+    fill(v("ones", 0, 128), 1.0)
+    iota(v("pidx", 0, 1), [[0, 1]], 0, 1)
+    run("P", lambda: g.affine_select(T.idn[:], T.ones[:], [[-1, 128]], EQ, 0.0, 0, 1), [v("idn", 0, 128)], [v("ones", 0, 128)])
+    iota(v("hrow", 0, 7), [[1, 7]], 1, 0)
+    iota(v("s16", 0, 2), [[16, 2]], 0, 0)
+    iota(v("win", 0, 1024), [[1, 32], [0, 32]], 0, 0)
+    iota(v("win", 2048, 3072), [[0, 32], [1, 32]], 0, 0)
+    iota(v("win", 6144, 7168), [[0, 32], [1, 32]], 0, 0)
+    iota(v("i128", 0, 128), [[1, 128]], -32, 0)
+    iota(v("ow", 0, 768), [[0, 768]], 0, 0)
+    iota(v("tw", 0, 2304), [[0, 2304]], 0, 0)
+    iota(v("bw", 0, 64), [[0, 2], [1, 2], [2, 16]], 0, 0)
+    fill(v("ent", 0, 2048), 0.0)
+    for b in range(4):
+        ts(v("ent", 512 * b + b, 512 * b + 512, 4), v("idn", 0, 128), -(2.0 ** -6), MUL)
+    fill(v("win", 1024, 2048), 0.0)
+    fill(v("ct", 0, 512), 0.0)
+    run("V", lambda: g.vector.tensor_scalar(T.pint[:, 0:1], T.pidx[:], 15, None, AluOpType.bitwise_and), [v("pint", 0, 1)], [v("pidx", 0, 1)])
+    run("V", lambda: g.vector.tensor_scalar(T.pint[:, 1:2], T.pidx[:], 4, None, AluOpType.arith_shift_right), [v("pint", 1, 2)], [v("pidx", 0, 1)])
+    copy(v("pf", 0, 2), v("pint", 0, 2))
+    i15, grp = v("pf", 0, 1), v("pf", 1, 2)
+    for k in range(5):
+        ts(v("w5", k, k + 1), i15, float(k), EQ, 2.0 ** (4 - k), MUL)
+    ts(v("w5", 6, 7), grp, 0.0, EQ, 32.0, MUL)
+    run("V", lambda: g.vector.tensor_reduce(T.w5[:, 5:6], T.w5[:, 0:5], AxisListType.X, ADD), [v("w5", 5, 6)], [v("w5", 0, 5)])
+    wcol = v("w5", 5, 6)
+    fill(v("bt", 384, 512), 0.0)
+    fill(v("trt", 128, 512), 0.0)
+    tt(v("w5", 7, 8), v("w5", 6, 7), wcol, MUL)
+    ts(v("mh", 0, 7), v("hrow", 0, 7), grp, EQ, wcol, MUL)
+    ts(v("l16", 0, 2), v("s16", 0, 2), i15, ADD)
+    for k in range(4):
+        ts(v("ct", 5 * k, 112, 16), v("mh", 0, 7), v("w5", 7, 8), ADD)
+    copy(v("tab", 0, 32), v("tia", 0, 32))
+    copy(v("tab", 32, 64, p=(0, 96)), v("tib", 0, 32, p=(0, 96)))
+    turn(v("tat", 0, 32), v("tab", 0, 32))
+    turn(v("tat", 32, 64, p=(0, 96)), v("tab", 32, 64, p=(0, 96)))
+    act(v("win", 3072, 4096), v("ent", 0, 1024), 0.0)
+    for G in range(6):
+        dma("SA"[G % 2], "dw0", v("win", 0, 1024, p=one(G)), v("tab", 0, 32, p=(0, 32)))
+    dma("S", "dtd", rows("tdr", 0, 64), v("tat", 0, 32, p=(64, 128)))
+    dma("A", "dtd", rows("tdr", 64, 160), v("tat", 32, 64, p=(0, 96)))
+    for G in range(6):
+        dma("SA"[G % 2], "dw1", v("win", 1024, 2048, p=one(G)), v("tat", 0, 32, p=(32, 64)))
+    act(v("win", 5120, 6144), v("ent", 0, 1024), 0.0)
+    act(v("win", 4096, 5120), v("win", 2048, 3072))
+    act(v("et", 0, 2048), v("ent", 0, 2048), -1.0)
+    for G in range(6):
+        dma("S", "dw2", v("win", 2048, 4096, p=one(G)), rows("tdr", 0, 64))
+    for G in range(6):
+        dma("S", "dw4", v("win", 4096, 7168, p=one(G)), rows("tdr", 64, 160))
+    dma("S", "dw", codes("wq", 0, 512), inp(T.wc[:]))
+    dma("S", "dw", v("wp", 0, 512), inp(T.ws[:]))
+    dma("S", "dv", v("vt", 0, 512), inp(T.v[:]))
+    quant(*pair("ctc", "cts", 0, 128), v("ct", 0, 512))
+    quant(*pair("quc", "qus", 0, 128), v("ut", 0, 512))
+
+    def slots_first():
+        ts(v("me", 2, 4), v("flw", 0, 2), -64.0, MUL, 64.0, ADD)
+        ts(v("tk", 0, 2), v("flw", 0, 2), -32.0, MUL, 32.0, ADD)
+        tt(v("me", 0, 2), v("tk", 0, 2), v("l16", 0, 2), ADD)
+        for k in range(2):
+            dma("S", "dfo", slot("fo", k), v("me", 2 * k, 2 * k + 2))
+        for G in range(6):
+            dma("S", "dow0", v("ow", 0, 256, p=one(G, 2)), slot("fo"))
+        copy(v("lw", 0, 2), v("me", 2, 4))
+
+    def first_rest():
+        for s in range(2):
+            ts(v("mw", 128 * s, 128 * s + 128), v("i128", 0, 128), v("l16", s, s + 1), NE)
+        fill(v("bw", 64, 128), -1.0)
+        for t in range(4):
+            fill(v("zp", 400 * t + 384, 400 * t + 400), 0.0)
+        fill(v("ctl", 128, 512), 0.0)
+        fill(v("zero", 0, 512), 0.0)
+        for k in range(3):
+            quant(*pair("lc%d" % k, "ls%d" % k, 32, 160), v("zero", 0, 512))
+
+    elist = topo.engines(core, nxt)
+    n = 1
+    while n * 2 <= len(elist) and n < 8:
+        n *= 2
+    elist = elist[:n]
+    full_mask = sum(1 << e for e in elist)
+    half = len(elist) // 2
+    halves = [sum(1 << e for e in elist[:half]), sum(1 << e for e in elist[half:])]
+    rid, pid, _ = topo.addr(nxt)
+
+    def send(ins, cnt, fn):
+        need("P", [], regs(ins))
+        total["loc"] = total.get("loc", 0) + cnt
+        fn()
+        note("P", [], regs(ins), "loc", total["loc"])
+
+    def arrived(where, sem, cnt=n):
+        total[sem] = cnt
+        note("R", where, [], sem, cnt)
+
+    def tell():
+        ridb, pidb, _b = topo.addr(prv)
+        maskb = sum(1 << e for e in topo.engines(core, prv)[:half])
+        send([v("me", 0, 4)], half, lambda: g.remote_dma(T.nx[:], T.me[:], T.sem.rn, T.sem.loc, pidb, ridb, maskb))
+        arrived([("nx", (0, 128, 0, 4, 1))], "rn", half)
+
+    def flags_out(r):
+        k, sem = 16 * r, "rf%d" % r
+        if r == ROUNDS - 1:
+            send([v("lim", k + 2, k + 4)], n, lambda: g.remote_dma(T.lw[:, k + 16:k + 18], T.lim[:, k + 2:k + 4], T.sem[sem], T.sem.loc, pid, rid, full_mask))
+            arrived([("lw", (0, 128, k + 16, k + 18, 1))], sem)
+        else:
+            fd = T["fd%d" % r]
+            tr = [RemoteDMATransfer(dst_ids=[DstId(rid=rid, pnc=pid)], dma_engine_mask=halves[e], remote_sem=T.sem[sem], src=T.lim[:, k + 2 * e:k + 2 * e + 2], dst=fd[e]) for e in range(2)]
+            send([v("lim", k, k + 4)], n, lambda: g.remote_dma_fused(tr, local_sem=T.sem.loc))
+            arrived([("fd%d" % r, (0, 2, 0, 256, 1))], sem)
+
+    def claims_out(r):
+        lc, ls, qc, qs = T["lc%d" % r], T["ls%d" % r], T["qcc%d" % r], T["qcs%d" % r]
+        send([v("qcc%d" % r, 0, 32)], n, lambda: g.remote_dma(lc[:, 0:32].bitcast(dt.uint8), qc[:, 0:32].bitcast(dt.uint8), T.sem["rc%d" % r], T.sem.loc, pid, rid, full_mask))
+        send([v("qcs%d" % r, 0, 32)], n, lambda: g.remote_dma(ls[:, 0:32], qs[:, 0:32], T.sem["rs%d" % r], T.sem.loc, pid, rid, full_mask))
+        arrived([("lc%d" % r, (0, 128, 0, 32, 1))], "rc%d" % r)
+        arrived([("ls%d" % r, (0, 128, 0, 32, 1))], "rs%d" % r)
+
+    def flags_in(r):
+        for G in range(6):
+            dma("S", "dlr%d" % r, v("ow", 256 * r + 256, 256 * r + 512, p=one(G, 2)), slot("fd%d" % r))
+        dma("S", "dlw%d" % r, v("lw", 16 * r + 16, 16 * r + 18), slot("fd%d" % r, 1))
+
+    def take_list(r):
+        k = 16 * r
+        tt(v("tk", 0, 2), v("lw", k, k + 2), v("lw", k + 16, k + 18), SUB)
+        for s in range(2):
+            o = v("tlf", 2 * s, 2 * s + 1) if r == ROUNDS - 1 else v("tl", 2 * r + s, 2 * r + s + 1)
+            ts(o, v("tk", s, s + 1), 2.0, MUL, v("l16", s, s + 1), ADD)
+
+    def unpack(r):
+        for t in range(4):
+            pd = "pd%d" % (t % 2)
+            mx(v(pd, 0, 128), *pair("enc", "ens", 128 * t, 128 * t + 128), *pair("lc%d" % r, "ls%d" % r, 0, 128))
+            a = 768 * r + 192 * t + 128
+            if t % 2 and r == ROUNDS - 1:
+                copy(v("tw", a, a + 32), v(pd, 0, 32))
+            else:
+                act(v("tw", a, a + 32), v(pd, 0, 32))
+
+    def new_slots(r):
+        for t in range(4):
+            a = 768 * r + 192 * t
+            act(v("tw", a + 768, a + 800), ind(v("tw", a, a + 160), v("tl", 2 * r, 2 * r + 2)))
+
+    def lists(r):
+        k = 16 * r
+        copy(v("clu", 0, 2), v("cnt", 0, 2))
+        ts(v("lim", k + 6, k + 8), v("cnt", 0, 2), float(C), GE, 128.0, MUL)
+        if r < ROUNDS - 1:
+            tt(v("lim", k + 4, k + 6), v("lim", k + 6, k + 8), v("l16", 0, 2), ADD)
+            old = v("nx", 0, 4) if r == 0 else v("lim", k - 16, k - 12)
+            tt(v("lim", k, k + 4), old, v("lim", k + 4, k + 8), MIN)
+        else:
+            tt(v("lim", k + 2, k + 4), v("lim", k - 14, k - 12), v("lim", k + 6, k + 8), MIN)
+        flags_out(r)
+        for t in range(4):
+            act(v("ctl", t, 128, 4), ind(v("zp", 400 * t, 400 * t + 400), v("clu", 0, 2)))
+
+    def pack(r):
+        quant(*pair("qcc%d" % r, "qcs%d" % r, 0, 128), v("ctl", 0, 512))
+        claims_out(r)
+
+    LO = [0]
+    for h in range(7):
+        LO.append(LO[h] + 64 * (7 - h))
+    qx = pair("qxc", "qxs", 0, 384)
+
+    def state(lo):
+        for b in range(lo, 4):
+            mx(v("pf%d" % b, 0, 384), *pair("ec", "es", 128 * b, 128 * b + 128), *qx)
+
+    def carry(h):
+        ts(v("occ", 4 * h, 4 * h + 4), v("trb", LO[h] + 1, LO[h] + 64, 16), 32.0 * h, ADD)
+
+    for r in range(ROUNDS):
+        last = r == ROUNDS - 1
+        quant(*qx, v("xt", 0, 1536))
+        mx(v("ps", 0, 384), *pair("quc", "qus", 0, 128), *qx)
+        if r > 0:
+            mx(v("pf0", 0, 384), *pair("ec", "es", 0, 128), *qx)
+            lists(r - 1)
+        else:
+            quant(*pair("enc", "ens", 0, 512), v("ent", 0, 2048))
+        for x in range(16):
+            ts(v("bt", 24 * x, 24 * x + 24), v("ps", x, 384, 16), 0.0, GT)
+        quant(*pair("bc", "bs", 0, 128), v("bt", 0, 512))
+        mx(v("pe", 0, 128), *pair("bc", "bs", 0, 128), *pair("ctc", "cts", 0, 128))
+        if r == 0:
+            slots_first()
+            tell()
+        else:
+            flags_in(r - 1)
+            state(1)
+        copy(v("of0", 0, 28), v("pe", 0, 28))
+        for h in range(7):
+            a, m = LO[h], 7 - h
+            w, o, b = v("win", 1024 * h, 1024 * h + 1024), "of%d" % h, m - SHARE[h] * (r > 0 or h > 1)
+            if b < m:
+                act(v("res", a + 64 * b, a + 64 * m), ind(w, v(o, 4 * b, 4 * m)))
+            copy(v("res", a, a + 64 * b), ind(w, v(o, 0, 4 * b)))
+            if h % 2:
+                carry(h - 1)
+            if r > 0 and h == 0:
+                pack(r - 1)
+            if r == 0 and h == 1:
+                fill(v("fp", 0, 4), 0.0)
+                quant(*pair("qtc", "qts", 0, 128), v("trt", 0, 512))
+            if r == 0 and h == 3:
+                quant(*pair("ec", "es", 0, 512), v("et", 0, 2048))
+                state(0)
+            if h in FSL:
+                t = h - FSL[0]
+                act(v("fs", 384 * t, 384 * t + 384), v("pf%d" % t, 0, 384))
+            if h == 5:
+                act(v("ores", 0, 384), ind(v("ow", 256 * r, 256 * r + 256), v("occ", 0, 24)))
+            if h == 6:
+                turn(v("otr", 0, 384), v("ores", 0, 384))
+                for k in range(4):
+                    e = v("otr", 16 * k + 1, 384, 64)
+                    run("V", lambda: g.vector.tensor_tensor_scan(T.fp[:, 4 + k:28:4], e[0], e[0], 0.0, MAX, MAX), [v("fp", 4 + k, 28, 4)], [e])
+            turn(v("trb", a, a + 64 * m), v("res", a, a + 64 * m))
+            if h < 6:
+                for k in range(4):
+                    ts(v("of%d" % (h + 1), k, 4 * (m - 1), 4), v("trb", a + 64 + 16 * k, a + 64 * m, 64), 32.0, MUL, v("trb", a + 16 * k, a + 16 * k + 1), ADD)
+            if h == 6:
+                tt(v("lf", 0, 24), v("otr", 0, 384, 16), v("fp", 0, 24), ADD)
+                carry(h)
+            if h % 2 == 0:
+                ts(v("occ", 4 * h + 4, 4 * h + 8), v("trb", a, a + 64, 16), 32.0 * h + 32.0, ADD)
+        copy(v("lu", 0, 24), v("lf", 0, 24))
+        dl = "dl%d" % r
+        for lev in range(6):
+            dma("S", dl, v("ol", 0, 24, p=one(lev, 16)), v("lu", 4 * lev, 4 * lev + 4, p=(0, 96)))
+        if r == 0:
+            for t in range(4):
+                pd = "pd%d" % (t % 2)
+                mx(v(pd, 0, 128), *pair("enc", "ens", 128 * t, 128 * t + 128), *pair("qtc", "qts", 0, 128))
+                for s in range(2):
+                    act(v("tw", 192 * t + 16 * s, 192 * t + 16 * s + 16), v(pd, s, 32, 2))
+        copy(v("ores", 384, 512), ind(v("ow", 256 * r, 256 * r + 256), v("occ", 24, 32)))
+        turn(v("otr", 384, 512), v("ores", 384, 512))
+        tt(v("fp", 28, 32), v("fp", 24, 28), v("otr", 385, 448, 16), MAX)
+        tt(v("lf", 24, 32), v("otr", 384, 512, 16), v("fp", 24, 32), ADD)
+        copy(v("lu", 24, 32), v("lf", 24, 32))
+        dma("S", dl, v("ol", 0, 24, p=one(6, 16)), v("lu", 24, 28, p=(0, 96)))
+        dma("A", dl, v("ol", 0, 24, p=one(7, 16)), v("lu", 28, 32, p=(0, 96)))
+        if r == 0:
+            first_rest()
+        else:
+            unpack(r - 1)
+            take_list(r - 1)
+            new_slots(r - 1)
+        if last:
+            quant(*pair("qvc", "qvs", 0, 128), v("vt", 0, 512))
+        ol = v("ol", 0, 24)
+
+        def pick(t):
+            a = 768 * r + 192 * t
+            act(v("gt", 384 * (t - 2), 384 * (t - 1)), ind(v("tw", a, a + 128), ol))
+
+        def diff(t):
+            a = 768 * r + 192 * t
+            if t < 2:
+                tt(v("zt", t, 1536, 4), ind(v("tw", a, a + 128), ol), v("fs", 384 * t, 384 * t + 384), ADD)
+            else:
+                tt(v("zt", t, 1536, 4), v("pf%d" % t, 0, 384), v("gt", 384 * (t - 2), 384 * (t - 1)), ADD)
+
+        def mine(s):
+            act(v("mm", 384 * s, 384 * s + 384), ind(v("mw", 128 * s, 128 * s + 128), ol))
+
+        def full_size(t, vector):
+            if vector:
+                ts(v("zp", 400 * t, 400 * t + 384), v("zt", t, 1536, 4), 64.0, MUL)
+            else:
+                act(v("zp", 400 * t, 400 * t + 384), v("zt", t, 1536, 4), 64.0)
+
+        def products():
+            quant(*pair("qzc", "qzs", 0, 384), v("zt", 0, 1536))
+            for t in range(4):
+                mx(v("pf%d" % t, 0, 384), *pair("wq", "wp", 128 * t, 128 * t + 128), *pair("qzc", "qzs", 0, 384))
+
+        def first_of(s):
+            e = v("mm", 384 * s, 384 * s + 384)
+            o = v("pr", 384 * s, 384 * s + 384)
+            run("V", lambda: g.vector.tensor_tensor_scan(o[0], e[0], e[0], 1.0, MUL, MIN), [o], [e])
+            if last:
+                run("V", lambda: g.vector.tensor_reduce(T.cnt[:, s:s + 1], o[0], AxisListType.X, ADD), [v("cnt", s, s + 1)], [o])
+            else:
+                run("A", lambda: g.scalar.activation(T.jnk[:], o[0], COPY, accum_out=T.cnt[:, s:s + 1]), [v("jnk", 0, 384), v("cnt", s, s + 1)], [o])
+
+        def layer(t):
+            tt(v("xt", t, 1536, 4), v("pf%d" % t, 0, 384), v("zp", 400 * t, 400 * t + 384), ADD)
+        if last:
+            mine(0)
+            pick(2)
+            pick(3)
+            mine(1)
+            diff(0)
+            diff(1)
+            first_of(0)
+            diff(2)
+            diff(3)
+            full_size(2, False)
+            full_size(3, False)
+            first_of(1)
+            full_size(0, True)
+            full_size(1, True)
+            lists(r)
+            products()
+            pack(r)
+            for t in range(4):
+                layer(t)
+        else:
+            pick(2)
+            pick(3)
+            for t in range(4):
+                diff(t)
+            products()
+            mine(0)
+            mine(1)
+            for t in range(4):
+                full_size(t, t < NZ)
+            first_of(0)
+            layer(0)
+            first_of(1)
+            for t in range(1, 4):
+                layer(t)
+    r = ROUNDS - 1
+    quant(*qx, v("xt", 0, 1536))
+    mx(v("ps", 0, 384), *pair("qvc", "qvs", 0, 128), *qx)
+    dma("S", "dout", inp(T.oc[:]), codes("qxc", 0, 384))
+    for k in range(4):
+        dma("S", "dout", inp(T.osc[4 * k:4 * k + 4, :]), v("qxs", 0, 384, p=(32 * k, 32 * k + 4)))
+    act(v("bpt", 0, 384), ind(v("bw", 0, 128), v("ol", 0, 24)))
+    dma("S", "dout", inp(T.bp[:, 0:384]), (T.bpt[0:128:16, :], [("bpt", (0, 128, 0, 384, 1))]))
+    act(v("yt", 0, 384), v("ps", 0, 384))
+    dma("S", "dout", inp(T.y[:]), v("yt", 0, 384))
+    take_list(r)
+    ts(v("full", 0, 2), v("lw", 16 * r + 16, 16 * r + 18), 0.0, EQ)
+    dma("S", "dout", inp(T.bp[:, 384:416]), v("full", 0, 2))
+    unpack(r)
+    for t in range(4):
+        a = 768 * r + 192 * t
+        for s in range(2):
+            out, win = v("rtt", 4 * s + t, 128, 8), ind(v("tw", a, a + 160), v("tlf", 2 * s, 2 * s + 1))
+            if t % 2:
+                ts(out, win, -64.0, MUL)
+            else:
+                act(out, win, -64.0)
+    dma("S", "dout", inp(T.rt[:]), v("rtt", 0, 128))
+    for s in sorted(total):
+        if known["P"].get(s, 0) < total[s]:
+            g.wait_ge(T.sem[s], total[s])

@@ -2,33 +2,137 @@ import math
 from concourse.bass import DstId, RemoteDMATransfer
 from concourse.mybir import dt, AluOpType, AxisListType, ActivationFunctionType
 
-ROUNDS, C = 3, 384
-SHARE, FSL, NZ = (3, 3, 2, 2, 1, 1, 0), (3, 4), 1
-KIND = {"f": "float32", "b": "bfloat16", "i": "int32", "h": "uint16", "s": "uint8", "c": "float8_e4m3fn_x4"}
-SPEC = """b xt 1536 ut 512 vt 512 trt 512 et 2048 ent 2048 ct 512 bt 512 win 7168 tab 64 tat 64 res 1792 trb 1792 ow 768
-b ores 512 otr 512 fp 32 lf 32 gt 768 zt 1536 zp 1600 mw 256 mm 768 pr 768 jnk 384 lim 64 ctl 512 zero 512 lw 64 tw 2304
-b bw 128 me 4 nx 4
-c qxc 384 quc 128 qvc 128 qtc 128 wq 512 ec 512 enc 512 ctc 128 bc 128 qzc 384 qcc0 128 qcc1 128 qcc2 128 lc0 160 lc1 160 lc2 160
-s qxs 384 qus 128 qvs 128 qts 128 wp 512 es 512 ens 512 cts 128 bs 128 qzs 384 qcs0 128 qcs1 128 qcs2 128 ls0 160 ls1 160 ls2 160
-i tia 32 tib 32 pidx 1 pint 2 flw 2
-h occ 32 lu 32 ol 24 clu 2 tl 4 tlf 4 of0 28 of1 28 of2 28 of3 28 of4 28 of5 28 of6 28
-f ones 128 idn 128 fs 768 cnt 2 tk 2 rtt 128 yt 384 bpt 384 full 2 pf 2 hrow 7 s16 2 l16 2 i128 128 w5 8 mh 8"""
-PSUM = ("ps", "pe", "pf0", "pf1", "pf2", "pf3", "pd0", "pd1")
-SCRATCH = {"tdr": ("dram", [160, 32], "bfloat16")}
-for _n in ("fo", "fd0", "fd1"):
-    SCRATCH[_n] = ("dram", [2, 128, 2], "bfloat16")
+ROUNDS, C, H = 3, 384, 192
+OPT = dict(share=(3, 3, 2, 2, 1, 1, 2), nv=2, full="VAAA", eps=0.05, bias=0.5, claim=0.0, fills="VVAAAPP", tries=600, seed=1, amp=0.6, part=0.05)
+KIND = {"f": "float32", "b": "bfloat16", "i": "int32", "h": "uint16", "s": "uint8", "c": "float8_e4m3fn_x4", "e": "float16"}
+SPEC = """b xt 1792 ut 512 vt 512 trt 512 et 2048 win 7840 tab 64 tat 64 res0 1152 res1 1152 trb0 1152 trb1 1152 bits 288 ev0 144 ev1 144 horn 144
+b stg0 32 stg1 32 stt0 32 stt1 32 gt0 768 gt1 768 fs0 768 fs1 768 zt0 768 zt1 768 zp 1600 mw 128 mm 768 lim 16 ctl 512 zero 1056 lw 6 tw 1152
+b bw 64 me 2 nx 2 own 32 clr 32 clt 32 jnk 768
+e pr 768
+c qxc 448 qfc 384 quc 128 qpc 128 qvc 128 wq 512 ec 512 qzc 384 qcc0 128 qcc1 128 qcc2 128 lc 224
+s qxs 448 qfs 384 qus 128 qps 128 qvs 128 wp 512 es 512 qzs 384 qcs0 128 qcs1 128 qcs2 128 ls 224
+i tia 32 tib 32 pidx 1 pint 3 flw 2 flr 32 odd 64
+h ol0 16 ol1 16 oe0 16 oe1 16 clu 2 tl 8 of0 128 of1 128 cl 2 ul 8
+f ones 128 idn 128 rtt 128 yt 384 bpt 384 full 2 pf 3 s16 2 l16 2 i64 64 col 16 tk 4 c32 8 got 6 key 4 chg 2 plc 32"""
+PSUM = tuple("pb%d" % k for k in range(8))
+SCRATCH = {"tdr": ("dram", [5, 33, 32], "bfloat16")}
+for _n in ("fd00", "fd01", "fd10", "fd11"):
+    SCRATCH[_n] = ("dram", [128, 2], "bfloat16")
 for _l in SPEC.split("\n"):
     _w = _l.split()
     for _k in range(1, len(_w), 2):
         SCRATCH[_w[_k]] = ("sbuf", [128, int(_w[_k + 1])], KIND[_w[0]])
 for _n in PSUM:
     SCRATCH[_n] = ("psum", [128, 512], "float32")
-DMAS = "dx du dti dtr dw dfl dfo dow0 dv dw0 dw1 dtd dw2 dw4 dl0 dl1 dl2 dlr0 dlr1 dlw0 dlw1 dout".split()
-SEMAPHORES = "cv ca ct_ cp loc rn rf0 rf1 rf2 rc0 rc1 rc2 rs0 rs1 rs2".split() + DMAS
+DMAS = "dx0 dx1 du dta dtb dtr dw dfl dfr dow0 dow1 dv dw0 dw1 dt0 dt1 dw2 dw4 dlr00 dlr01 dlr10 dlr11 dout".split()
+DMAS += ["dl%d%d%d" % (_k // 4, _k // 2 % 2, _k % 2) for _k in range(12)]
+SEMAPHORES = "cv ca ct_ cp loc rn rf00 rf01 rf10 rf11 rf20 rc0 rc1 rc2 rs0 rs1 rs2".split() + DMAS
 
 ADD, SUB, MUL, MAX, MIN = AluOpType.add, AluOpType.subtract, AluOpType.mult, AluOpType.max, AluOpType.min
-EQ, NE, GT, GE = AluOpType.is_equal, AluOpType.not_equal, AluOpType.is_gt, AluOpType.is_ge
+EQ, NE, GT, GE, LT = AluOpType.is_equal, AluOpType.not_equal, AluOpType.is_gt, AluOpType.is_ge, AluOpType.is_lt
+AND, SHR = AluOpType.bitwise_and, AluOpType.arith_shift_right
 COPY = ActivationFunctionType.Copy
+ORDER = []
+PACE = ((0.85e-3, 0.15, 1.6, 2.0, 0.02, 1.56), (0.95e-3, 0.10, 2.0, 2.4, 0.03, 1.3), (1.1e-3, 0.15, 1.5, 2.6, 0.02, 1.9))
+
+
+def hit(a, b):
+    return a[0] < b[1] and b[0] < a[1] and a[2] < b[3] and b[2] < a[3] and (a[2] - b[2]) % math.gcd(a[4], b[4]) == 0
+
+
+def covers(a, b):
+    return a[4] == 1 and a[0] <= b[0] and b[1] <= a[1] and a[2] <= b[2] and b[3] <= a[3]
+
+
+def arrange(ops):
+    n = len(ops)
+    deps = [set(o["after"]) for o in ops]
+    wr, rd, kin = {}, {}, {}
+    for k, o in enumerate(ops):
+        for name, reg in o["ins"]:
+            deps[k].update(e[1] for e in wr.get(name, []) if hit(reg, e[0]))
+            if name in PSUM:
+                deps[k].update(e[1] for e in rd.get(name, []))
+        for name, reg in o["outs"]:
+            deps[k].update(e[1] for e in wr.get(name, []) + rd.get(name, []) if name in PSUM or hit(reg, e[0]))
+        for name, reg in o["outs"]:
+            wr[name] = [e for e in wr.get(name, []) if not covers(reg, e[0])] + [(reg, k)]
+            rd[name] = [e for e in rd.get(name, []) if not covers(reg, e[0])]
+        for name, reg in o["ins"]:
+            rd.setdefault(name, []).append((reg, k))
+        for d in list(deps[k]):
+            if ops[d]["kind"] == "d" and d not in o["after"]:
+                deps[k].update(kin[ops[d]["sem"]])
+        deps[k].discard(k)
+        if o["kind"] == "d":
+            kin.setdefault(o["sem"], []).append(k)
+    users = [[] for _ in ops]
+    for k in range(n):
+        for d in deps[k]:
+            users[d].append(k)
+    qs = [o["q"] for o in ops]
+    deps = [sorted(d) for d in deps]
+
+    def costs(p):
+        hold = [o["hold"] + max(o["cyc"] + p[5] * o["got"], 64) * p[0] * (o["kind"] == "c") for o in ops]
+        late = [{"d": p[2], "a": p[3]}.get(o["kind"], 0.0) + p[1] for o in ops]
+        move = [(p[4] * o["rows"] + 5e-5 * o["size"]) / 16 for o in ops]
+        return hold, late, move
+    cost = [costs(p) for p in PACE]
+    hold, late, move = cost[0]
+    way = [0.0] * n
+    for k in range(n - 1, -1, -1):
+        way[k] = hold[k] + late[k] + move[k] + max([way[u] for u in users[k]] + [0.0])
+
+    def place(rank):
+        left = [len(d) for d in deps]
+        ready = {}
+        for k in range(n):
+            if not left[k]:
+                ready.setdefault(qs[k], []).append(k)
+        at, free, order, rings = [0.0] * n, {q: 0.0 for q in qs}, [], 0.0
+        while len(order) < n:
+            t, q = min((max(min(at[k] for k in ks), free[q]), q) for q, ks in ready.items() if ks)
+            k = max([k for k in ready[q] if at[k] <= t + OPT["eps"]], key=lambda k: (rank[k], -k))
+            done = free[q] = max(t, at[k]) + hold[k]
+            if move[k]:
+                done = rings = max(rings, done) + move[k]
+            ready[q].remove(k)
+            order.append(k)
+            for u in users[k]:
+                at[u] = max(at[u], done + late[k])
+                left[u] -= 1
+                if not left[u]:
+                    ready.setdefault(qs[u], []).append(u)
+        return order
+
+    def span(order):
+        total = 0.0
+        for hold, late, move in cost:
+            end, free, rings = [0.0] * n, {q: 0.0 for q in qs}, 0.0
+            for k in order:
+                done = free[qs[k]] = max([free[qs[k]]] + [end[d] for d in deps[k]]) + hold[k]
+                if move[k]:
+                    done = rings = max(rings, done) + move[k]
+                end[k] = done + late[k]
+            total += max(end)
+        return total / len(cost)
+    rank = [way[k] + ops[k]["pri"] for k in range(n)]
+    order = place(rank)
+    best, x = span(order), OPT["seed"]
+    for _ in range(OPT["tries"]):
+        other = list(rank)
+        for k in range(n):
+            x = (x * 1103515245 + 12345) % 2147483648
+            if x < OPT["part"] * 2147483648:
+                x = (x * 1103515245 + 12345) % 2147483648
+                other[k] += OPT["amp"] * (x / 1073741824 - 1.0)
+        o = place(other)
+        t = span(o)
+        if t <= best:
+            best, rank, order = t, other, o
+    OPT["span"] = best
+    return order
 
 
 def rank_program(g, core, T, topo):
@@ -38,57 +142,7 @@ def rank_program(g, core, T, topo):
     nxt, prv = T.cores[(rank + 1) % len(T.cores)], T.cores[(rank - 1) % len(T.cores)]
     eng = {"V": g.vector, "A": g.scalar, "T": g.tensor, "S": g.sync, "P": g}
     semof = {"V": "cv", "A": "ca", "T": "ct_", "P": "cp"}
-    total = {}
-    known = {q: {} for q in eng}
-    clock = {}
-    wr, rd = {}, {}
-
-    def hit(a, b):
-        return a[0] < b[1] and b[0] < a[1] and a[2] < b[3] and b[2] < a[3] and (a[2] - b[2]) % math.gcd(a[4], b[4]) == 0
-
-    def covers(a, b):
-        return a[4] == 1 and a[0] <= b[0] and b[1] <= a[1] and a[2] <= b[2] and b[3] <= a[3]
-
-    def learn(q, sem, val):
-        k = known[q]
-        if k.get(sem, 0) >= val:
-            return
-        if sem in DMAS:
-            val = total[sem]
-        eng[q].wait_ge(T.sem[sem], val)
-        k[sem] = val
-        for (s, x), c in clock.items():
-            if s == sem and x <= val and (sem in DMAS or x == val):
-                for s2, x2 in c.items():
-                    if k.get(s2, 0) < x2:
-                        k[s2] = x2
-
-    def need(q, outs, ins):
-        toks = {}
-
-        def add(e):
-            toks[e[2]] = max(toks.get(e[2], 0), e[3])
-        for name, reg in ins:
-            for e in wr.get(name, []):
-                if hit(reg, e[0]):
-                    add(e)
-            if name in PSUM:
-                for e in rd.get(name, []):
-                    if e[1] != q:
-                        add(e)
-        for name, reg in outs:
-            for e in wr.get(name, []) + rd.get(name, []):
-                if name in PSUM or hit(reg, e[0]):
-                    add(e)
-        for s in sorted(toks):
-            learn(q, s, toks[s])
-
-    def note(q, outs, ins, sem, val):
-        for name, reg in outs:
-            wr[name] = [e for e in wr.get(name, []) if not covers(reg, e[0])] + [(reg, q, sem, val)]
-            rd[name] = [e for e in rd.get(name, []) if not covers(reg, e[0])]
-        for name, reg in ins:
-            rd.setdefault(name, []).append((reg, q, sem, val))
+    ops, pri = [], [0.0]
 
     def regs(vs):
         out = []
@@ -96,165 +150,214 @@ def rank_program(g, core, T, topo):
             out += e[1]
         return out
 
-    def run(q, fn, outs, ins):
-        o, i = regs(outs), regs(ins)
-        need(q, o, i)
-        sem = semof[q]
-        total[sem] = total.get(sem, 0) + 1
-        clock[(sem, total[sem])] = dict(known[q])
-        fn().then_inc(T.sem[sem], 1)
-        note(q, o, i, sem, total[sem])
+    def add(q, kind, fn, outs, ins, sem, cnt=1, hold=0.0, cyc=0, got=0, rows=0, size=0, after=()):
+        ops.append(dict(q=q, kind=kind, fn=fn, outs=regs(outs), ins=regs(ins), sem=sem, cnt=cnt, hold=hold, cyc=cyc, got=got, rows=rows, size=size, after=after, pri=pri[0]))
+        return len(ops) - 1
 
-    def dma(q, sem, out, in_):
-        o, i = regs([out]), regs([in_])
-        need(q, o, i)
-        total[sem] = total.get(sem, 0) + 16
-        clock[(sem, total[sem])] = dict(known[q])
-        eng[q].dma_start(out[0], in_[0]).then_inc(T.sem[sem], 16)
-        note(q, o, i, sem, total[sem])
+    def run(q, fn, outs, ins, cyc, got=0):
+        add(q, "c", fn, outs, ins, semof[q], cyc=cyc, got=got)
+
+    def dma(q, sem, out, in_, size=1024, rows=16, after=()):
+        return add(q, "d", lambda: eng[q].dma_start(out[0], in_[0]), [out], [in_], sem, 16, 0.07, rows=rows, size=size, after=after)
 
     def v(name, a, b, s=1, p=(0, 128)):
-        t = T[name]
-        return (t[p[0]:p[1], a:b:s] if s != 1 else t[p[0]:p[1], a:b], [(name, (p[0], p[1], a, b, s))])
+        t, q = T[name], slice(*p)
+        if s < 0:
+            return (t[q, slice(b - 1, a - 1 if a else None, -1)], [(name, (p[0], p[1], a, b, 1))], b - a, name)
+        return (t[q, a:b:s] if s != 1 else t[q, a:b], [(name, (p[0], p[1], a, b, s))], len(range(a, b, s)), name)
+
+    def rows16(name, first, last, a, b):
+        return (T[name][first:last:16, a:b], [(name, (first, last, a, b, 1))])
 
     def codes(name, a, b):
         return (T[name][:, a:b].bitcast(dt.uint8), [(name, (0, 128, a, b, 1))])
-
-    def rows(name, a, b):
-        return (T[name][a:b, :], [(name, (a, b, 0, 32, 1))])
-
-    def slot(name, k=None):
-        return (T[name][:], [(name, (0, 2, 0, 256, 1))]) if k is None else (T[name][k], [(name, (k, k + 1, 0, 256, 1))])
 
     def inp(ap):
         return (ap, [])
 
     def ind(win, off):
-        return (win[0].indirect(off[0]), win[1] + off[1])
+        return (win[0].indirect(off[0]), win[1] + off[1], 16 * off[2], None)
+
+    def price(out, in_):
+        if in_[3] is None:
+            return 60, in_[2]
+        narrow = all(SCRATCH[e[3]][2] in ("bfloat16", "uint16", "float16") for e in (out, in_))
+        return (in_[2] / 2 if narrow else in_[2]), 0
 
     def copy(out, in_):
-        run("V", lambda: g.vector.tensor_copy(out[0], in_[0]), [out], [in_])
+        run("V", lambda: g.vector.tensor_copy(out[0], in_[0]), [out], [in_], *price(out, in_))
 
     def act(out, in_, scale=1.0):
-        run("A", lambda: g.scalar.activation(out[0], in_[0], COPY, scale=scale) if scale != 1.0 else g.scalar.activation(out[0], in_[0], COPY), [out], [in_])
+        run("A", lambda: g.scalar.activation(out[0], in_[0], COPY, scale=scale) if scale != 1.0 else g.scalar.activation(out[0], in_[0], COPY), [out], [in_],
+            *((in_[2], 0) if in_[3] else (78, in_[2])))
+
+    def count(out, in_, total):
+        run("A", lambda: g.scalar.activation(out[0], in_[0], COPY, accum_out=total[0]), [out, total], [in_], 100, in_[2])
+
+    def scaled(q, out, in_, scale):
+        if q == "A":
+            act(out, in_, scale)
+        else:
+            ts(out, in_, scale, MUL)
 
     def tt(out, a, b, op):
-        run("V", lambda: g.vector.tensor_tensor(out[0], a[0], b[0], op), [out], [a, b])
+        run("V", lambda: g.vector.tensor_tensor(out[0], a[0], b[0], op), [out], [a, b], *(price(out, a) if a[3] is None else (a[2] * (1 if a[3] in PSUM else 2), 0)))
 
     def ts(out, a, s1, op0, s2=None, op1=None):
         ins = [a] + [s for s in (s1, s2) if isinstance(s, tuple)]
         x1 = s1[0] if isinstance(s1, tuple) else s1
         x2 = s2[0] if isinstance(s2, tuple) else s2
         if op1 is None:
-            run("V", lambda: g.vector.tensor_scalar(out[0], a[0], x1, None, op0), [out], ins)
+            run("V", lambda: g.vector.tensor_scalar(out[0], a[0], x1, None, op0), [out], ins, *price(out, a))
         else:
-            run("V", lambda: g.vector.tensor_scalar(out[0], a[0], x1, x2, op0, op1), [out], ins)
+            run("V", lambda: g.vector.tensor_scalar(out[0], a[0], x1, x2, op0, op1), [out], ins, *price(out, a))
+
+    def scan(out, a, b, op0, op1):
+        run("V", lambda: g.vector.tensor_tensor_scan(out[0], a[0], b[0], 0.0, op0, op1), [out], [a, b], *price(out, a))
 
     def fill(out, c):
-        run("V", lambda: g.vector.memset(out[0], c), [out], [])
+        run("V", lambda: g.vector.memset(out[0], c), [out], [], *price(out, out))
 
     def quant(c, s, in_):
-        run("V", lambda: g.vector.quantize_mx(c[0], s[0], in_[0]), [c, s], [in_])
+        run("V", lambda: g.vector.quantize_mx(c[0], s[0], in_[0]), [c, s], [in_], 15 + 0.265 * in_[2])
 
     def mx(out, lc, ls, rc, rs):
-        run("T", lambda: g.tensor.matmul_mx(out[0], lc[0], ls[0], rc[0], rs[0], True, True), [out], [lc, ls, rc, rs])
+        run("T", lambda: g.tensor.matmul_mx(out[0], lc[0], ls[0], rc[0], rs[0], True, True), [out], [lc, ls, rc, rs], 1.3 * (rc[2] + 16))
 
     def pair(c, s, a, b):
         return v(c, a, b), v(s, a, b)
 
     def turn(out, in_):
-        run("V", lambda: g.vector.transpose(out[0], in_[0]), [out], [in_])
+        run("V", lambda: g.vector.transpose(out[0], in_[0]), [out], [in_], *price(out, in_))
 
-    def iota(out, pattern, base, cm):
-        run("P", lambda: g.iota(out[0], pattern, base, cm, allow_small_or_imprecise_dtypes=True), [out], [])
+    def iota(out, pattern, base, cm=0):
+        run("P", lambda: g.iota(out[0], pattern, base, cm, allow_small_or_imprecise_dtypes=True), [out], [], 160 + 2 * out[2])
+
+    def zeros(q, out):
+        if q == "A":
+            act(out, v("zero", 0, out[2]))
+        elif q == "V":
+            fill(out, 0.0)
+        else:
+            iota(out, [[0, out[2]]], 0)
 
     def one(G, k=1):
         return (16 * G, 16 * G + k)
 
-    dma("S", "dti", v("tia", 0, 32), inp(T.ti[0:4, :]))
-    dma("A", "dti", v("tib", 0, 32, p=(0, 96)), inp(T.ti[4:7, :]))
-    dma("S", "dx", v("xt", 0, 1536), inp(T.x[:]))
-    dma("A", "du", v("ut", 0, 512), inp(T.u[:]))
-    dma("S", "dtr", v("trt", 0, 128), inp(T.tr[:]))
-    dma("S", "dfl", v("flw", 0, 2), inp(T.fl[:]))
+    def col(k, p=(0, 128)):
+        return v("col", k, k + 1, p=p)
 
+    pri[0] = 9.0
+    dma("S", "dta", v("tia", 0, 32), inp(T.ti[0:4, :]), 16384, 128)
+    dma("A", "dtb", v("tib", 0, 32, p=(0, 96)), inp(T.ti[4:7, :]), 12288, 96)
+    run("V", lambda: g.vector.memset(T.flr[:], 0), [v("flr", 0, 32)], [], 1)
+    dma("A", "dfr", rows16("flr", 0, 128, 0, 32), inp(T.fl[:]))
+    pri[0] = 0.0
+    dma("S", "dx0", v("xt", 0, 768), inp(T.x[:, 0:768]), 196608, 128)
+    dma("A", "du", v("ut", 0, 512), inp(T.u[:]), 131072, 128)
+    dma("S", "dx1", v("xt", 896, 1664), inp(T.x[:, 768:1536]), 196608, 128)
+
+    fill(v("zero", 0, 1056), 0.0)
     fill(v("ones", 0, 128), 1.0)
     iota(v("pidx", 0, 1), [[0, 1]], 0, 1)
-    run("P", lambda: g.affine_select(T.idn[:], T.ones[:], [[-1, 128]], EQ, 0.0, 0, 1), [v("idn", 0, 128)], [v("ones", 0, 128)])
-    iota(v("hrow", 0, 7), [[1, 7]], 1, 0)
-    iota(v("s16", 0, 2), [[16, 2]], 0, 0)
-    iota(v("win", 0, 1024), [[1, 32], [0, 32]], 0, 0)
-    iota(v("win", 2048, 3072), [[0, 32], [1, 32]], 0, 0)
-    iota(v("win", 6144, 7168), [[0, 32], [1, 32]], 0, 0)
-    iota(v("i128", 0, 128), [[1, 128]], -32, 0)
-    iota(v("ow", 0, 768), [[0, 768]], 0, 0)
-    iota(v("tw", 0, 2304), [[0, 2304]], 0, 0)
-    iota(v("bw", 0, 64), [[0, 2], [1, 2], [2, 16]], 0, 0)
-    fill(v("ent", 0, 2048), 0.0)
-    for b in range(4):
-        ts(v("ent", 512 * b + b, 512 * b + 512, 4), v("idn", 0, 128), -(2.0 ** -6), MUL)
-    fill(v("win", 1024, 2048), 0.0)
-    fill(v("ct", 0, 512), 0.0)
-    run("V", lambda: g.vector.tensor_scalar(T.pint[:, 0:1], T.pidx[:], 15, None, AluOpType.bitwise_and), [v("pint", 0, 1)], [v("pidx", 0, 1)])
-    run("V", lambda: g.vector.tensor_scalar(T.pint[:, 1:2], T.pidx[:], 4, None, AluOpType.arith_shift_right), [v("pint", 1, 2)], [v("pidx", 0, 1)])
-    copy(v("pf", 0, 2), v("pint", 0, 2))
-    i15, grp = v("pf", 0, 1), v("pf", 1, 2)
-    for k in range(5):
-        ts(v("w5", k, k + 1), i15, float(k), EQ, 2.0 ** (4 - k), MUL)
-    ts(v("w5", 6, 7), grp, 0.0, EQ, 32.0, MUL)
-    run("V", lambda: g.vector.tensor_reduce(T.w5[:, 5:6], T.w5[:, 0:5], AxisListType.X, ADD), [v("w5", 5, 6)], [v("w5", 0, 5)])
-    wcol = v("w5", 5, 6)
-    fill(v("bt", 384, 512), 0.0)
-    fill(v("trt", 128, 512), 0.0)
-    tt(v("w5", 7, 8), v("w5", 6, 7), wcol, MUL)
-    ts(v("mh", 0, 7), v("hrow", 0, 7), grp, EQ, wcol, MUL)
+    run("P", lambda: g.affine_select(T.idn[:], T.ones[:], [[-1, 128]], EQ, 0.0, 0, 1), [v("idn", 0, 128)], [v("ones", 0, 128)], 460)
+    iota(v("s16", 0, 2), [[16, 2]], 0)
+    iota(v("i64", 0, 64), [[1, 64]], 0)
+    iota(v("bw", 0, 32), [[1, 2], [2, 16]], 0)
+    fill(v("bw", 32, 64), -1.0)
+    fill(v("clr", 0, 32), 0.0)
+    iota(v("clr", 0, 12), [[1, 2], [2, 6]], 0)
+    iota(v("clr", 16, 28), [[2, 2], [4, 3], [1, 2]], 0)
+    copy(v("clr", 16, 28, p=(96, 128)), v("clr", 0, 12, p=(96, 128)))
+    turn(v("clt", 0, 32), v("clr", 0, 32))
+    copy(v("cl", 0, 1), v("clt", 0, 1))
+    ts(v("pint", 0, 1), v("pidx", 0, 1), 15, AND)
+    ts(v("pint", 1, 2), v("pidx", 0, 1), 5, SHR)
+    ts(v("pint", 2, 3), v("pidx", 0, 1), 4, SHR)
+    copy(v("pf", 0, 3), v("pint", 0, 3))
+    i15, blk, grp = v("pf", 0, 1), v("pf", 1, 2), v("pf", 2, 3)
+    ts(col(0), blk, 32.0, MUL, 32.0, ADD)
+    ts(col(1), blk, 32.0, MUL, 160.0, ADD)
+    ts(col(2), i15, 0.0, EQ, -15.0, MUL)
+    ts(col(3), i15, 0.0, EQ, 160.0, MUL)
+    ts(col(4), grp, 6.0, EQ, 175.0, MUL)
+    ts(col(5), grp, 5.0, EQ, 166.0, MUL)
+    ts(col(7), grp, 6.0, EQ, 24.0, MUL)
+    dead, more, alive = col(8), col(9), col(10)
+    ts(dead, col(4), 17.0, ADD)
+    ts(more, col(5), col(7), ADD, 8.0, ADD)
+    ts(alive, more, col(4), ADD, 17.0, ADD)
+    ts(col(6), i15, 8.0, GE, 8.0, MUL)
     ts(v("l16", 0, 2), v("s16", 0, 2), i15, ADD)
-    for k in range(4):
-        ts(v("ct", 5 * k, 112, 16), v("mh", 0, 7), v("w5", 7, 8), ADD)
-    copy(v("tab", 0, 32), v("tia", 0, 32))
-    copy(v("tab", 32, 64, p=(0, 96)), v("tib", 0, 32, p=(0, 96)))
+    iota(v("c32", 0, 8), [[0, 2], [32, 4]], 0)
+    ts(v("ul", 0, 8), v("c32", 0, 8), i15, ADD, col(6), ADD)
+    fill(v("horn", 0, 144), 2.0)
+    fill(v("horn", 0, 144, 8), 0.0)
+    fill(v("bits", 0, 288), 0.0)
+    fill(v("bits", 68, 288, 72), 40.0)
+    for b in range(2):
+        fill(v("xt", 896 * b + 768, 896 * b + 896), 0.0)
+        fill(v("stg%d" % b, 0, 32), 0.0)
+        fill(v("stt%d" % b, 0, 32, p=(96, 128)), 0.0)
+    TAB = [0] + [480 + 1056 * h for h in range(1, 7)]
+    SIX = TAB[6] - 32
+    ts(v("win", 1024, 1280), v("zero", 0, 256), col(2), ADD, 32.0, ADD)
+    ts(v("win", 1216, 1248, p=(0, 96)), v("zero", 0, 32, p=(0, 96)), col(3, (0, 96)), ADD, 32.0, ADD)
+    iota(v("win", 1280, 1536), [[0, 8], [1, 16], [16, 2]], 0)
+    iota(v("win", SIX, SIX + 32), [[1, 16], [16, 2]], 0)
+    for h in range(7):
+        zeros(OPT["fills"][h], v("win", TAB[h], TAB[h] + (1024 if h in (0, 5, 6) else 1056)))
+    ts(v("tab", 0, 32), v("tia", 0, 32), col(0), ADD)
+    ts(v("tab", 32, 64, p=(0, 64)), v("tib", 0, 32, p=(0, 64)), col(1, (0, 64)), ADD)
+    p6 = (64, 96)
+    ts(v("odd", 0, 32, p=p6), v("tib", 0, 32, p=p6), 1, AND)
+    ts(v("odd", 32, 64, p=p6), v("tib", 0, 32, p=p6), 1, SHR)
+    ts(v("plc", 0, 32, p=p6), v("odd", 0, 32, p=p6), 16.0, MUL, 224.0, ADD)
+    tt(v("tab", 32, 64, p=p6), v("plc", 0, 32, p=p6), v("odd", 32, 64, p=p6), ADD)
     turn(v("tat", 0, 32), v("tab", 0, 32))
     turn(v("tat", 32, 64, p=(0, 96)), v("tab", 32, 64, p=(0, 96)))
-    act(v("win", 3072, 4096), v("ent", 0, 1024), 0.0)
-    for G in range(6):
-        dma("SA"[G % 2], "dw0", v("win", 0, 1024, p=one(G)), v("tab", 0, 32, p=(0, 32)))
-    dma("S", "dtd", rows("tdr", 0, 64), v("tat", 0, 32, p=(64, 128)))
-    dma("A", "dtd", rows("tdr", 64, 160), v("tat", 32, 64, p=(0, 96)))
-    for G in range(6):
-        dma("SA"[G % 2], "dw1", v("win", 1024, 2048, p=one(G)), v("tat", 0, 32, p=(32, 64)))
-    act(v("win", 5120, 6144), v("ent", 0, 1024), 0.0)
-    act(v("win", 4096, 5120), v("win", 2048, 3072))
-    act(v("et", 0, 2048), v("ent", 0, 2048), -1.0)
-    for G in range(6):
-        dma("S", "dw2", v("win", 2048, 4096, p=one(G)), rows("tdr", 0, 64))
-    for G in range(6):
-        dma("S", "dw4", v("win", 4096, 7168, p=one(G)), rows("tdr", 64, 160))
-    dma("S", "dw", codes("wq", 0, 512), inp(T.wc[:]))
-    dma("S", "dw", v("wp", 0, 512), inp(T.ws[:]))
-    dma("S", "dv", v("vt", 0, 512), inp(T.v[:]))
-    quant(*pair("ctc", "cts", 0, 128), v("ct", 0, 512))
-    quant(*pair("quc", "qus", 0, 128), v("ut", 0, 512))
 
-    def slots_first():
-        ts(v("me", 2, 4), v("flw", 0, 2), -64.0, MUL, 64.0, ADD)
-        ts(v("tk", 0, 2), v("flw", 0, 2), -32.0, MUL, 32.0, ADD)
-        tt(v("me", 0, 2), v("tk", 0, 2), v("l16", 0, 2), ADD)
-        for k in range(2):
-            dma("S", "dfo", slot("fo", k), v("me", 2 * k, 2 * k + 2))
+    def staged(a, b, k=33):
+        return (T.tdr[a:b, 0:k, :], [("tdr", (a, b, 0, k, 1))])
+    for h in range(2):
         for G in range(6):
-            dma("S", "dow0", v("ow", 0, 256, p=one(G, 2)), slot("fo"))
-        copy(v("lw", 0, 2), v("me", 2, 4))
-
-    def first_rest():
-        for s in range(2):
-            ts(v("mw", 128 * s, 128 * s + 128), v("i128", 0, 128), v("l16", s, s + 1), NE)
-        fill(v("bw", 64, 128), -1.0)
-        for t in range(4):
-            fill(v("zp", 400 * t + 384, 400 * t + 400), 0.0)
-        fill(v("ctl", 128, 512), 0.0)
-        fill(v("zero", 0, 512), 0.0)
-        for k in range(3):
-            quant(*pair("lc%d" % k, "ls%d" % k, 32, 160), v("zero", 0, 512))
+            dma("S", "dw%d" % h, v("win", TAB[h], TAB[h] + 1024, p=one(G)), v("tat", 0, 32, p=(32 * h, 32 * h + 32)), 2048, 32)
+    dma("S", "dt0", (T.tdr[:, 32, :], [("tdr", (0, 5, 32, 33, 1))]), v("zero", 0, 32, p=(0, 5)))
+    dma("S", "dt0", staged(0, 2, 32), v("tat", 0, 32, p=(64, 128)), 4096, 64)
+    dma("S", "dt1", staged(2, 5, 32), v("tat", 32, 64, p=(0, 96)), 6144, 96)
+    for G in range(6):
+        dma("S", "dw2", v("win", TAB[2], TAB[4], p=one(G)), staged(0, 2), 4224)
+    for G in range(6):
+        dma("S", "dw4", v("win", TAB[4], TAB[6], p=one(G)), staged(2, 4), 4224)
+        k = dma("S", "dw4", v("win", TAB[6], 7840, p=one(G)), staged(4, 5, 32), 2048)
+    dma("S", "dfl", v("flw", 0, 2), inp(T.fl[:]), 1024, 128)
+    dma("S", "dtr", v("trt", 0, 128), inp(T.tr[:]), 32768, 128, (k,))
+    dma("S", "dw", codes("wq", 0, 512), inp(T.wc[:]), 262144, 128, (k,))
+    dma("S", "dw", v("wp", 0, 512), inp(T.ws[:]), 65536, 128, (k,))
+    dma("S", "dv", v("vt", 0, 512), inp(T.v[:]), 131072, 128, (k,))
+    ts(v("own", 0, 32), v("flr", 0, 32), more, MUL, dead, ADD)
+    for G in range(6):
+        dma("A", "dow0", v("win", 1280, 1472, p=one(G)), rows16("own", 0, 96, 0, 32), 384, 6)
+    for G in range(6):
+        dma("S", "dow1", v("win", SIX, SIX + 32, p=one(G)), v("own", 0, 32, p=one(6)), 64, 1)
+    ts(v("me", 0, 2), v("flw", 0, 2), more, MUL, dead, ADD)
+    quant(*pair("quc", "qus", 0, 128), v("ut", 0, 512))
+    ul = v("ul", 0, 8)
+    run("V", lambda: g.vector.tensor_copy(T.qpc[:, 0:128].bitcast(dt.uint32), T.quc[:, 0:128].bitcast(dt.uint32).indirect(ul[0])), [v("qpc", 0, 128)], [v("quc", 0, 128), ul], 60, 128)
+    act(v("qps", 0, 128), ind(v("qus", 0, 128), ul))
+    for k in range(2):
+        zeros("A", v("et", 1024 * k, 1024 * k + 1024))
+    for b in range(4):
+        act(v("et", 512 * b + b, 512 * b + 512, 4), v("idn", 0, 128), 2.0 ** -6)
+    quant(*pair("ec", "es", 0, 512), v("et", 0, 2048))
+    zeros("P", v("trt", 128, 512))
+    quant(*pair("lc", "ls", 0, 128), v("trt", 0, 512))
+    zeros("P", v("ctl", 128, 512))
+    zeros("P", v("tw", 0, 1152))
+    for t in range(4):
+        zeros("P", v("zp", 400 * t + 384, 400 * t + 400))
+    for s in range(2):
+        ts(v("mw", 64 * s, 64 * s + 64), v("i64", 0, 64), v("l16", s, s + 1), NE)
 
     elist = topo.engines(core, nxt)
     n = 1
@@ -266,273 +369,247 @@ def rank_program(g, core, T, topo):
     halves = [sum(1 << e for e in elist[:half]), sum(1 << e for e in elist[half:])]
     rid, pid, _ = topo.addr(nxt)
 
-    def send(ins, cnt, fn):
-        need("P", [], regs(ins))
-        total["loc"] = total.get("loc", 0) + cnt
-        fn()
-        note("P", [], regs(ins), "loc", total["loc"])
+    def send(ins, cnt, fn, where, sem, hold=0.3):
+        k = add("P", "r", fn, [], ins, "loc", cnt, hold)
+        add("R", "a", None, [(None, where)], [], sem, cnt, after=(k,))
 
-    def arrived(where, sem, cnt=n):
-        total[sem] = cnt
-        note("R", where, [], sem, cnt)
+    ridb, pidb, _b = topo.addr(prv)
+    maskb = sum(1 << e for e in topo.engines(core, prv)[:half])
+    send([v("me", 0, 2)], half, lambda: g.remote_dma(T.nx[:], T.me[:], T.sem.rn, T.sem.loc, pidb, ridb, maskb), [("nx", (0, 128, 0, 2, 1))], "rn", 1.8)
 
-    def tell():
-        ridb, pidb, _b = topo.addr(prv)
-        maskb = sum(1 << e for e in topo.engines(core, prv)[:half])
-        send([v("me", 0, 4)], half, lambda: g.remote_dma(T.nx[:], T.me[:], T.sem.rn, T.sem.loc, pidb, ridb, maskb))
-        arrived([("nx", (0, 128, 0, 4, 1))], "rn", half)
+    def bank(b, t, a=0, z=H, s=1):
+        return v("pb%d" % (4 * b + t), a, z, s)
 
-    def flags_out(r):
-        k, sem = 16 * r, "rf%d" % r
-        if r == ROUNDS - 1:
-            send([v("lim", k + 2, k + 4)], n, lambda: g.remote_dma(T.lw[:, k + 16:k + 18], T.lim[:, k + 2:k + 4], T.sem[sem], T.sem.loc, pid, rid, full_mask))
-            arrived([("lw", (0, 128, k + 16, k + 18, 1))], sem)
-        else:
-            fd = T["fd%d" % r]
-            tr = [RemoteDMATransfer(dst_ids=[DstId(rid=rid, pnc=pid)], dma_engine_mask=halves[e], remote_sem=T.sem[sem], src=T.lim[:, k + 2 * e:k + 2 * e + 2], dst=fd[e]) for e in range(2)]
-            send([v("lim", k, k + 4)], n, lambda: g.remote_dma_fused(tr, local_sem=T.sem.loc))
-            arrived([("fd%d" % r, (0, 2, 0, 256, 1))], sem)
+    def mine(r):
+        return v("me", 0, 2) if r == 0 else v("lw", 2 * r - 2, 2 * r)
 
-    def claims_out(r):
-        lc, ls, qc, qs = T["lc%d" % r], T["ls%d" % r], T["qcc%d" % r], T["qcs%d" % r]
-        send([v("qcc%d" % r, 0, 32)], n, lambda: g.remote_dma(lc[:, 0:32].bitcast(dt.uint8), qc[:, 0:32].bitcast(dt.uint8), T.sem["rc%d" % r], T.sem.loc, pid, rid, full_mask))
-        send([v("qcs%d" % r, 0, 32)], n, lambda: g.remote_dma(ls[:, 0:32], qs[:, 0:32], T.sem["rs%d" % r], T.sem.loc, pid, rid, full_mask))
-        arrived([("lc%d" % r, (0, 128, 0, 32, 1))], "rc%d" % r)
-        arrived([("ls%d" % r, (0, 128, 0, 32, 1))], "rs%d" % r)
-
-    def flags_in(r):
-        for G in range(6):
-            dma("S", "dlr%d" % r, v("ow", 256 * r + 256, 256 * r + 512, p=one(G, 2)), slot("fd%d" % r))
-        dma("S", "dlw%d" % r, v("lw", 16 * r + 16, 16 * r + 18), slot("fd%d" % r, 1))
-
-    def take_list(r):
-        k = 16 * r
-        tt(v("tk", 0, 2), v("lw", k, k + 2), v("lw", k + 16, k + 18), SUB)
-        for s in range(2):
-            o = v("tlf", 2 * s, 2 * s + 1) if r == ROUNDS - 1 else v("tl", 2 * r + s, 2 * r + s + 1)
-            ts(o, v("tk", s, s + 1), 2.0, MUL, v("l16", s, s + 1), ADD)
+    def theirs(r, a=0, z=2):
+        return v("nx", a, z) if r == 0 else v("lim", 4 * r - 4 + a, 4 * r - 4 + z)
 
     def unpack(r):
+        lo = 0 if r < 0 else 32 + 32 * r
         for t in range(4):
-            pd = "pd%d" % (t % 2)
-            mx(v(pd, 0, 128), *pair("enc", "ens", 128 * t, 128 * t + 128), *pair("lc%d" % r, "ls%d" % r, 0, 128))
-            a = 768 * r + 192 * t + 128
-            if t % 2 and r == ROUNDS - 1:
-                copy(v("tw", a, a + 32), v(pd, 0, 32))
+            b, k = t % 2, 2 + t // 2
+            mx(bank(b, k, 0, 128), *pair("ec", "es", 128 * t, 128 * t + 128), *pair("lc", "ls", lo, lo + 128))
+            if r < 0:
+                for s in range(2):
+                    act(v("tw", 96 * t + 16 * s, 96 * t + 16 * s + 16), bank(b, k, s, 32, 2), -1.0)
             else:
-                act(v("tw", a, a + 32), v(pd, 0, 32))
+                a = 384 * r + 96 * t
+                scaled("V" if r == ROUNDS - 1 and t % 2 else "A", v("tw", a + 64, a + 96), bank(b, k, 96, 128), -1.0)
+        if r >= 0:
+            tt(v("chg", 0, 2), mine(r + 1), mine(r), NE)
+            for s in range(2):
+                a = 4 + 2 * s if r == ROUNDS - 1 else 2 * r + s
+                ts(v("tl", a, a + 1), v("chg", s, s + 1), 64.0, MUL, v("l16", s, s + 1), ADD)
+        if 0 <= r < ROUNDS - 1:
+            for t in range(4):
+                a = 384 * r + 96 * t
+                act(v("tw", a + 384, a + 416), ind(v("tw", a, a + 96), v("tl", 2 * r, 2 * r + 2)))
 
-    def new_slots(r):
-        for t in range(4):
-            a = 768 * r + 192 * t
-            act(v("tw", a + 768, a + 800), ind(v("tw", a, a + 160), v("tl", 2 * r, 2 * r + 2)))
+    def keys(r):
+        ts(v("key", 0, 2), mine(r), dead, EQ, alive, MUL)
+        for s in range(2):
+            ts(v("key", 2 + s, 3 + s), theirs(r, s, s + 1), dead, EQ, v("key", s, s + 1), MUL)
 
-    def lists(r):
-        k = 16 * r
-        copy(v("clu", 0, 2), v("cnt", 0, 2))
-        ts(v("lim", k + 6, k + 8), v("cnt", 0, 2), float(C), GE, 128.0, MUL)
-        if r < ROUNDS - 1:
-            tt(v("lim", k + 4, k + 6), v("lim", k + 6, k + 8), v("l16", 0, 2), ADD)
-            old = v("nx", 0, 4) if r == 0 else v("lim", k - 16, k - 12)
-            tt(v("lim", k, k + 4), old, v("lim", k + 4, k + 8), MIN)
+    def rows_out(r, early, name, a, step):
+        k, tk, tag = 4 * r + 2 * early, 2 * early, "%d%d" % (r, early)
+        for s in range(2):
+            ts(v("tk", tk + s, tk + s + 1), v(name, a + step * s, a + step * s + 1), float(C), LT, v("key", 2 + s, 3 + s), MUL)
+        tt(v("lim", k, k + 2), theirs(r), v("tk", tk, tk + 2), MAX)
+        sem, src, at = T.sem["rf" + tag], T.lim[:, k:k + 2], ("lw", (0, 128, 2 * r, 2 * r + 2, 1))
+        if r == ROUNDS - 1:
+            send([v("lim", k, k + 2)], n, lambda: g.remote_dma(T.lw[:, 2 * r:2 * r + 2], src, sem, T.sem.loc, pid, rid, full_mask), [at], "rf" + tag)
+            return
+        fd, where = T["fd" + tag], [("fd" + tag, (0, 128, 0, 2, 1))]
+        if early:
+            send([v("lim", k, k + 2)], n, lambda: g.remote_dma(fd[:], src, sem, T.sem.loc, pid, rid, full_mask), where, "rf" + tag)
         else:
-            tt(v("lim", k + 2, k + 4), v("lim", k - 14, k - 12), v("lim", k + 6, k + 8), MIN)
-        flags_out(r)
+            tr = [RemoteDMATransfer(dst_ids=[DstId(rid=rid, pnc=pid)], dma_engine_mask=halves[e], remote_sem=sem, src=src, dst=d) for e, d in enumerate((fd[:], T.lw[:, 2 * r:2 * r + 2]))]
+            send([v("lim", k, k + 2)], n, lambda: g.remote_dma_fused(tr, local_sem=T.sem.loc), where + [at], "rf" + tag)
+        for G in range(6):
+            if early:
+                dma("S", "dlr" + tag, v("win", 1280, 1472, p=one(G)), (fd[0:96, :], where), 384, 1)
+            else:
+                dma("S", "dlr" + tag, v("win", SIX, SIX + 32, p=one(G)), (fd[96:112, :], where), 64, 1)
+
+    def early(r, b):
+        turn(v("stt%d" % b, 0, 32, p=(0, 96)), v("stg%d" % b, 0, 32, p=(0, 96)))
+        if r < ROUNDS - 1:
+            copy(v("oe%d" % b, 0, 16), ind(v("stt%d" % b, 0, 32), v("cl", 0, 1)))
+            for s in range(2):
+                k = 2 * b + s
+                count(v("jnk", H * k, H * k + H), ind(v("mw", 64 * s, 64 * s + 64), v("oe%d" % b, 0, 12)), v("got", k, k + 1))
+            if b:
+                tt(v("got", 4, 6), v("got", 0, 2), v("got", 2, 4), ADD)
+                rows_out(r, 1, "got", 4, 1)
+
+    def claims(r):
+        for s in range(2):
+            e = v("mm", 384 * s, 384 * s + 384, -1)
+            scan(v("pr", 384 * s, 384 * s + 384), e, e, MUL, ADD)
+        copy(v("clu", 0, 2), v("pr", 383, 768, 384))
+        rows_out(r, 0, "pr", 383, 384)
         for t in range(4):
             act(v("ctl", t, 128, 4), ind(v("zp", 400 * t, 400 * t + 400), v("clu", 0, 2)))
-
-    def pack(r):
+        qc, qs, a = T["qcc%d" % r], T["qcs%d" % r], 128 + 32 * r
         quant(*pair("qcc%d" % r, "qcs%d" % r, 0, 128), v("ctl", 0, 512))
-        claims_out(r)
+        send([v("qcc%d" % r, 0, 32)], n, lambda: g.remote_dma(T.lc[:, a:a + 32].bitcast(dt.uint8), qc[:, 0:32].bitcast(dt.uint8), T.sem["rc%d" % r], T.sem.loc, pid, rid, full_mask),
+             [("lc", (0, 128, a, a + 32, 1))], "rc%d" % r)
+        send([v("qcs%d" % r, 0, 32)], n, lambda: g.remote_dma(T.ls[:, a:a + 32], qs[:, 0:32], T.sem["rs%d" % r], T.sem.loc, pid, rid, full_mask),
+             [("ls", (0, 128, a, a + 32, 1))], "rs%d" % r)
 
     LO = [0]
-    for h in range(7):
-        LO.append(LO[h] + 64 * (7 - h))
-    qx = pair("qxc", "qxs", 0, 384)
+    for h in range(8):
+        LO.append(LO[h] + 32 * (8 - h))
 
-    def state(lo):
-        for b in range(lo, 4):
-            mx(v("pf%d" % b, 0, 384), *pair("ec", "es", 128 * b, 128 * b + 128), *qx)
+    def images(r, b):
+        a = 224 * b
+        k = 224 if r == 0 else H
+        quant(*pair("qxc", "qxs", a, a + k), v("xt", 896 * b, 896 * b + 4 * k))
+        for k in range(2):
+            mx(bank(b, k, 0, 128), *pair("qxc", "qxs", a + 96 * k, a + 96 * k + 128), *pair("qpc", "qps", 0, 128))
+            ts(v("bits", 144 * b + 72 * k, 144 * b + 72 * k + 64), bank(b, k, 0, 64), 0.0, GT)
+        ev = "ev%d" % b
+        scan(v(ev, 0, 144), v("horn", 0, 144), v("bits", 144 * b, 144 * b + 144), MUL, ADD)
+        for k in range(2):
+            ts(v("of%d" % b, k, 16, 2), v(ev, 72 * k + 12, 72 * k + 72, 8), 32.0, MUL, v(ev, 72 * k + 4, 72 * k + 5), ADD)
 
-    def carry(h):
-        ts(v("occ", 4 * h, 4 * h + 4), v("trb", LO[h] + 1, LO[h] + 64, 16), 32.0 * h, ADD)
+    def level(r, b, h):
+        a, m, res, trb, o = LO[h], 8 - h, "res%d" % b, "trb%d" % b, "of%d" % b
+        w = v("win", 0, 1536) if h == 0 else v("win", 480, TAB[h] + 1024)
+        k = OPT["share"][h]
+        if k:
+            copy(v(res, a, a + 32 * k), ind(w, v(o, 16 * h, 16 * h + 2 * k)))
+        if k < m:
+            act(v(res, a + 32 * k, a + 32 * m), ind(w, v(o, 16 * h + 2 * k, 16 * h + 2 * m)))
+        z = a + 32 * m
+
+        def stage(h, row, a):
+            dma("S", "dl%d%d%d" % (r, b, h // 6), v("stg%d" % b, 16 * (h % 2), 16 * (h % 2) + 16, p=(32 * (h // 2), 32 * (h // 2) + 12)), rows16(res, row, 96, a, a + 32), 384, 12)
+        stage(h, 1, z - 32)
+        if h < 6:
+            turn(v(trb, a, z), v(res, a, z))
+            for G in range(2):
+                ts(v(o, 16 * h + 16 + G, 16 * h + 16 + 2 * (m - 1), 2), v(trb, a + 32 + 16 * G, z, 32), 32.0, MUL, v(trb, a + 16 * G, a + 16 * G + 1), ADD)
+        else:
+            tt(v(res, z, z + 32), v(res, a, a + 32), v(res, a + 32, z), SUB)
+            stage(7, 0, z)
+
+    def state(r, b):
+        for t in range(4):
+            mx(bank(b, t), *pair("ec", "es", 128 * t, 128 * t + 128), *pair("qxc", "qxs", 224 * b, 224 * b + H))
+            if t < OPT["nv"]:
+                act(v("fs%d" % b, H * t, H * t + H), bank(b, t))
+
+    def diff(r, b):
+        turn(v("stt%d" % b, 0, 32, p=(96, 128)), v("stg%d" % b, 0, 32, p=(96, 128)))
+        copy(v("ol%d" % b, 0, 16), ind(v("stt%d" % b, 0, 32), v("cl", 0, 1)))
+        ol, zt = v("ol%d" % b, 0, 12), "zt%d" % b
+        for s in range(2):
+            act(v("mm", 384 * s + H * b, 384 * s + H * b + H), ind(v("mw", 64 * s, 64 * s + 64), ol))
+        for t in range(4):
+            w = ind(v("tw", 384 * r + 96 * t, 384 * r + 96 * t + 64), ol)
+            if t < OPT["nv"]:
+                tt(v(zt, t, 768, 4), w, v("fs%d" % b, H * t, H * t + H), ADD)
+            else:
+                act(v("gt%d" % b, H * t, H * t + H), w)
+                tt(v(zt, t, 768, 4), bank(b, t), v("gt%d" % b, H * t, H * t + H), ADD)
+            scaled(OPT["full"][t], v("zp", 400 * t + H * b, 400 * t + H * b + H), v(zt, t, 768, 4), 64.0)
+        if r == ROUNDS - 1:
+            act(v("bpt", H * b, H * b + H), ind(v("bw", 0, 64), ol))
+
+    def layer(r, b):
+        qz = pair("qzc", "qzs", H * b, H * b + H)
+        quant(*qz, v("zt%d" % b, 0, 768))
+        for t in range(4):
+            mx(bank(b, t), *pair("wq", "wp", 128 * t, 128 * t + 128), *qz)
+            tt(v("xt", 896 * b + t, 896 * b + 768, 4), bank(b, t), v("zp", 400 * t + H * b, 400 * t + H * b + H), ADD)
+
+    def both(fn, *args):
+        for b in range(2):
+            pri[0] = OPT["bias"] * (1 - b)
+            fn(args[0], b, *args[1:])
+        pri[0] = 0.0
 
     for r in range(ROUNDS):
-        last = r == ROUNDS - 1
-        quant(*qx, v("xt", 0, 1536))
-        mx(v("ps", 0, 384), *pair("quc", "qus", 0, 128), *qx)
-        if r > 0:
-            mx(v("pf0", 0, 384), *pair("ec", "es", 0, 128), *qx)
-            lists(r - 1)
-        else:
-            quant(*pair("enc", "ens", 0, 512), v("ent", 0, 2048))
-        for x in range(16):
-            ts(v("bt", 24 * x, 24 * x + 24), v("ps", x, 384, 16), 0.0, GT)
-        quant(*pair("bc", "bs", 0, 128), v("bt", 0, 512))
-        mx(v("pe", 0, 128), *pair("bc", "bs", 0, 128), *pair("ctc", "cts", 0, 128))
-        if r == 0:
-            slots_first()
-            tell()
-        else:
-            flags_in(r - 1)
-            state(1)
-        copy(v("of0", 0, 28), v("pe", 0, 28))
+        both(images, r)
+        unpack(r - 1)
+        both(state, r)
+        keys(r)
         for h in range(7):
-            a, m = LO[h], 7 - h
-            w, o, b = v("win", 1024 * h, 1024 * h + 1024), "of%d" % h, m - SHARE[h] * (r > 0 or h > 1)
-            if b < m:
-                act(v("res", a + 64 * b, a + 64 * m), ind(w, v(o, 4 * b, 4 * m)))
-            copy(v("res", a, a + 64 * b), ind(w, v(o, 0, 4 * b)))
-            if h % 2:
-                carry(h - 1)
-            if r > 0 and h == 0:
-                pack(r - 1)
-            if r == 0 and h == 1:
-                fill(v("fp", 0, 4), 0.0)
-                quant(*pair("qtc", "qts", 0, 128), v("trt", 0, 512))
-            if r == 0 and h == 3:
-                quant(*pair("ec", "es", 0, 512), v("et", 0, 2048))
-                state(0)
-            if h in FSL:
-                t = h - FSL[0]
-                act(v("fs", 384 * t, 384 * t + 384), v("pf%d" % t, 0, 384))
-            if h == 5:
-                act(v("ores", 0, 384), ind(v("ow", 256 * r, 256 * r + 256), v("occ", 0, 24)))
-            if h == 6:
-                turn(v("otr", 0, 384), v("ores", 0, 384))
-                for k in range(4):
-                    e = v("otr", 16 * k + 1, 384, 64)
-                    run("V", lambda: g.vector.tensor_tensor_scan(T.fp[:, 4 + k:28:4], e[0], e[0], 0.0, MAX, MAX), [v("fp", 4 + k, 28, 4)], [e])
-            turn(v("trb", a, a + 64 * m), v("res", a, a + 64 * m))
-            if h < 6:
-                for k in range(4):
-                    ts(v("of%d" % (h + 1), k, 4 * (m - 1), 4), v("trb", a + 64 + 16 * k, a + 64 * m, 64), 32.0, MUL, v("trb", a + 16 * k, a + 16 * k + 1), ADD)
-            if h == 6:
-                tt(v("lf", 0, 24), v("otr", 0, 384, 16), v("fp", 0, 24), ADD)
-                carry(h)
-            if h % 2 == 0:
-                ts(v("occ", 4 * h + 4, 4 * h + 8), v("trb", a, a + 64, 16), 32.0 * h + 32.0, ADD)
-        copy(v("lu", 0, 24), v("lf", 0, 24))
-        dl = "dl%d" % r
-        for lev in range(6):
-            dma("S", dl, v("ol", 0, 24, p=one(lev, 16)), v("lu", 4 * lev, 4 * lev + 4, p=(0, 96)))
-        if r == 0:
-            for t in range(4):
-                pd = "pd%d" % (t % 2)
-                mx(v(pd, 0, 128), *pair("enc", "ens", 128 * t, 128 * t + 128), *pair("qtc", "qts", 0, 128))
-                for s in range(2):
-                    act(v("tw", 192 * t + 16 * s, 192 * t + 16 * s + 16), v(pd, s, 32, 2))
-        copy(v("ores", 384, 512), ind(v("ow", 256 * r, 256 * r + 256), v("occ", 24, 32)))
-        turn(v("otr", 384, 512), v("ores", 384, 512))
-        tt(v("fp", 28, 32), v("fp", 24, 28), v("otr", 385, 448, 16), MAX)
-        tt(v("lf", 24, 32), v("otr", 384, 512, 16), v("fp", 24, 32), ADD)
-        copy(v("lu", 24, 32), v("lf", 24, 32))
-        dma("S", dl, v("ol", 0, 24, p=one(6, 16)), v("lu", 24, 28, p=(0, 96)))
-        dma("A", dl, v("ol", 0, 24, p=one(7, 16)), v("lu", 28, 32, p=(0, 96)))
-        if r == 0:
-            first_rest()
-        else:
-            unpack(r - 1)
-            take_list(r - 1)
-            new_slots(r - 1)
-        if last:
-            quant(*pair("qvc", "qvs", 0, 128), v("vt", 0, 512))
-        ol = v("ol", 0, 24)
-
-        def pick(t):
-            a = 768 * r + 192 * t
-            act(v("gt", 384 * (t - 2), 384 * (t - 1)), ind(v("tw", a, a + 128), ol))
-
-        def diff(t):
-            a = 768 * r + 192 * t
-            if t < 2:
-                tt(v("zt", t, 1536, 4), ind(v("tw", a, a + 128), ol), v("fs", 384 * t, 384 * t + 384), ADD)
-            else:
-                tt(v("zt", t, 1536, 4), v("pf%d" % t, 0, 384), v("gt", 384 * (t - 2), 384 * (t - 1)), ADD)
-
-        def mine(s):
-            act(v("mm", 384 * s, 384 * s + 384), ind(v("mw", 128 * s, 128 * s + 128), ol))
-
-        def full_size(t, vector):
-            if vector:
-                ts(v("zp", 400 * t, 400 * t + 384), v("zt", t, 1536, 4), 64.0, MUL)
-            else:
-                act(v("zp", 400 * t, 400 * t + 384), v("zt", t, 1536, 4), 64.0)
-
-        def products():
-            quant(*pair("qzc", "qzs", 0, 384), v("zt", 0, 1536))
-            for t in range(4):
-                mx(v("pf%d" % t, 0, 384), *pair("wq", "wp", 128 * t, 128 * t + 128), *pair("qzc", "qzs", 0, 384))
-
-        def first_of(s):
-            e = v("mm", 384 * s, 384 * s + 384)
-            o = v("pr", 384 * s, 384 * s + 384)
-            run("V", lambda: g.vector.tensor_tensor_scan(o[0], e[0], e[0], 1.0, MUL, MIN), [o], [e])
-            if last:
-                run("V", lambda: g.vector.tensor_reduce(T.cnt[:, s:s + 1], o[0], AxisListType.X, ADD), [v("cnt", s, s + 1)], [o])
-            else:
-                run("A", lambda: g.scalar.activation(T.jnk[:], o[0], COPY, accum_out=T.cnt[:, s:s + 1]), [v("jnk", 0, 384), v("cnt", s, s + 1)], [o])
-
-        def layer(t):
-            tt(v("xt", t, 1536, 4), v("pf%d" % t, 0, 384), v("zp", 400 * t, 400 * t + 384), ADD)
-        if last:
-            mine(0)
-            pick(2)
-            pick(3)
-            mine(1)
-            diff(0)
-            diff(1)
-            first_of(0)
-            diff(2)
-            diff(3)
-            full_size(2, False)
-            full_size(3, False)
-            first_of(1)
-            full_size(0, True)
-            full_size(1, True)
-            lists(r)
-            products()
-            pack(r)
-            for t in range(4):
-                layer(t)
-        else:
-            pick(2)
-            pick(3)
-            for t in range(4):
-                diff(t)
-            products()
-            mine(0)
-            mine(1)
-            for t in range(4):
-                full_size(t, t < NZ)
-            first_of(0)
-            layer(0)
-            first_of(1)
-            for t in range(1, 4):
-                layer(t)
+            both(level, r, h)
+        both(early, r)
+        both(diff, r)
+        pri[0] = OPT["claim"]
+        claims(r)
+        both(layer, r)
     r = ROUNDS - 1
-    quant(*qx, v("xt", 0, 1536))
-    mx(v("ps", 0, 384), *pair("qvc", "qvs", 0, 128), *qx)
-    dma("S", "dout", inp(T.oc[:]), codes("qxc", 0, 384))
+    quant(*pair("qvc", "qvs", 0, 128), v("vt", 0, 512))
+    dma("S", "dout", inp(T.bp[:, 0:384]), rows16("bpt", 0, 128, 0, 384), 12288, 24)
+    for b in range(2):
+        qf = pair("qfc", "qfs", H * b, H * b + H)
+        quant(*qf, v("xt", 896 * b, 896 * b + 768))
+        mx(bank(b, 0), *pair("qvc", "qvs", 0, 128), *qf)
+        dma("S", "dout", inp(T.oc[:, 768 * b:768 * b + 768]), codes("qfc", H * b, H * b + H), 98304, 128)
+        act(v("yt", H * b, H * b + H), bank(b, 0))
+        dma("A", "dout", inp(T.y[:, H * b:H * b + H]), v("yt", H * b, H * b + H), 98304, 128)
     for k in range(4):
-        dma("S", "dout", inp(T.osc[4 * k:4 * k + 4, :]), v("qxs", 0, 384, p=(32 * k, 32 * k + 4)))
-    act(v("bpt", 0, 384), ind(v("bw", 0, 128), v("ol", 0, 24)))
-    dma("S", "dout", inp(T.bp[:, 0:384]), (T.bpt[0:128:16, :], [("bpt", (0, 128, 0, 384, 1))]))
-    act(v("yt", 0, 384), v("ps", 0, 384))
-    dma("S", "dout", inp(T.y[:]), v("yt", 0, 384))
-    take_list(r)
-    ts(v("full", 0, 2), v("lw", 16 * r + 16, 16 * r + 18), 0.0, EQ)
-    dma("S", "dout", inp(T.bp[:, 384:416]), v("full", 0, 2))
+        dma("S", "dout", inp(T.osc[4 * k:4 * k + 4, :]), v("qfs", 0, 384, p=(32 * k, 32 * k + 4)))
+    ts(v("full", 0, 2), mine(ROUNDS), dead, NE)
+    dma("S", "dout", inp(T.bp[:, 384:416]), v("full", 0, 2), 1024, 128)
     unpack(r)
     for t in range(4):
-        a = 768 * r + 192 * t
+        a = 384 * r + 96 * t
         for s in range(2):
-            out, win = v("rtt", 4 * s + t, 128, 8), ind(v("tw", a, a + 160), v("tlf", 2 * s, 2 * s + 1))
-            if t % 2:
-                ts(out, win, -64.0, MUL)
-            else:
-                act(out, win, -64.0)
-    dma("S", "dout", inp(T.rt[:]), v("rtt", 0, 128))
+            scaled("V" if t % 2 else "A", v("rtt", 4 * s + t, 128, 8), ind(v("tw", a, a + 96), v("tl", 4 + 2 * s, 5 + 2 * s)), -64.0)
+    dma("S", "dout", inp(T.rt[:]), v("rtt", 0, 128), 65536, 128)
+
+    if not ORDER:
+        ORDER.extend(arrange(ops))
+    total = {}
+    known = {q: {} for q in eng}
+    clock = {}
+    wr, rd = {}, {}
+
+    def learn(q, sem, val):
+        k = known[q]
+        if k.get(sem, 0) >= val:
+            return
+        if sem in DMAS or sem == "loc":
+            val = total[sem]
+        eng[q].wait_ge(T.sem[sem], val)
+        k[sem] = val
+        for x, c in clock.get(sem, {}).items():
+            if x == val or (sem in DMAS and x < val):
+                for s2, x2 in c.items():
+                    if k.get(s2, 0) < x2:
+                        k[s2] = x2
+
+    for k in ORDER:
+        o = ops[k]
+        q, sem, toks = o["q"], o["sem"], {}
+        if o["kind"] != "a":
+            for name, reg in o["ins"]:
+                for e in [e for e in wr.get(name, []) if hit(reg, e[0])] + [e for e in rd.get(name, []) if name in PSUM and e[1] != q]:
+                    toks[e[2]] = max(toks.get(e[2], 0), e[3])
+            for name, reg in o["outs"]:
+                for e in wr.get(name, []) + rd.get(name, []):
+                    if name in PSUM or hit(reg, e[0]):
+                        toks[e[2]] = max(toks.get(e[2], 0), e[3])
+            for s in sorted(toks):
+                learn(q, s, toks[s])
+        total[sem] = total.get(sem, 0) + o["cnt"]
+        if o["kind"] in "cd":
+            clock.setdefault(sem, {})[total[sem]] = dict(known[q])
+            o["fn"]().then_inc(T.sem[sem], o["cnt"])
+        elif o["kind"] == "r":
+            o["fn"]()
+        for name, reg in o["outs"]:
+            wr[name] = [e for e in wr.get(name, []) if not covers(reg, e[0])] + [(reg, q, sem, total[sem])]
+            rd[name] = [e for e in rd.get(name, []) if not covers(reg, e[0])]
+        for name, reg in o["ins"]:
+            rd.setdefault(name, []).append((reg, q, sem, total[sem]))
     for s in sorted(total):
         if known["P"].get(s, 0) < total[s]:
             g.wait_ge(T.sem[s], total[s])

@@ -3,17 +3,18 @@ from concourse.bass import DstId, RemoteDMATransfer
 from concourse.mybir import dt, AluOpType, AxisListType, ActivationFunctionType
 
 ROUNDS, C, H = 3, 384, 192
-OPT = dict(share=(3, 3, 2, 2, 1, 1, 2), nv=2, full="VAAA", eps=0.05, bias=0.5, claim=0.0, fills="VVAAAPP", tries=600, seed=1, amp=0.6, part=0.05)
+OPT = dict(share=(3, 3, 2, 2, 1, 1, 0), nv=2, full="VVAA", eps=0.05, bias=1.0, claim=0.0, fills="VVAAAPP", own="SA", soon=0.0, last=0.0,
+           turns=5, tries=300, amp=0.3, part=0.05, swaps=6000, heat=0.06, seed=1)
 KIND = {"f": "float32", "b": "bfloat16", "i": "int32", "h": "uint16", "s": "uint8", "c": "float8_e4m3fn_x4", "e": "float16"}
-SPEC = """b xt 1792 ut 512 vt 512 trt 512 et 2048 win 7840 tab 64 tat 64 res0 1152 res1 1152 trb0 1152 trb1 1152 bits 288 ev0 144 ev1 144 horn 144
-b stg0 32 stg1 32 stt0 32 stt1 32 gt0 768 gt1 768 fs0 768 fs1 768 zt0 768 zt1 768 zp 1600 mw 128 mm 768 lim 16 ctl 512 zero 1056 lw 6 tw 1152
-b bw 64 me 2 nx 2 own 32 clr 32 clt 32 jnk 768
+SPEC = """b xt 1792 ut 512 vt 512 trt 512 et 2048 win 7952 tab 64 tat 64 res0 1152 res1 1152 trb0 1152 trb1 1152 bits 288 ev0 144 ev1 144 horn 144
+b stg0 32 stg1 32 stt0 32 stt1 32 gt0 768 gt1 768 fs0 768 fs1 768 zt0 768 zt1 768 zp 1600 mw 128 mm 768 lim 16 ctl 512 zero 1056 lw 6 tw 1024
+b bw 64 me 2 nx 2 clr 32 clt 32 jnk 768
 e pr 768
 c qxc 448 qfc 384 quc 128 qpc 128 qvc 128 wq 512 ec 512 qzc 384 qcc0 128 qcc1 128 qcc2 128 lc 224
 s qxs 448 qfs 384 qus 128 qps 128 qvs 128 wp 512 es 512 qzs 384 qcs0 128 qcs1 128 qcs2 128 ls 224
-i tia 32 tib 32 pidx 1 pint 3 flw 2 flr 32 odd 64
-h ol0 16 ol1 16 oe0 16 oe1 16 clu 2 tl 8 of0 128 of1 128 cl 2 ul 8
-f ones 128 idn 128 rtt 128 yt 384 bpt 384 full 2 pf 3 s16 2 l16 2 i64 64 col 16 tk 4 c32 8 got 6 key 4 chg 2 plc 32"""
+i tia 32 tib 32 pidx 1 pint 3 flw 2 odd 64
+h ol0 16 ol1 16 oe0 16 oe1 16 clu 2 of0 128 of1 128 cl 2 ul 8
+f ones 128 idn 128 rtt 128 yt 384 bpt 384 full 2 pf 3 s16 2 l16 2 i64 64 col 16 tk 4 c32 8 got 12 key 4 chg 2 plc 32"""
 PSUM = tuple("pb%d" % k for k in range(8))
 SCRATCH = {"tdr": ("dram", [5, 33, 32], "bfloat16")}
 for _n in ("fd00", "fd01", "fd10", "fd11"):
@@ -24,14 +25,14 @@ for _l in SPEC.split("\n"):
         SCRATCH[_w[_k]] = ("sbuf", [128, int(_w[_k + 1])], KIND[_w[0]])
 for _n in PSUM:
     SCRATCH[_n] = ("psum", [128, 512], "float32")
-DMAS = "dx0 dx1 du dta dtb dtr dw dfl dfr dow0 dow1 dv dw0 dw1 dt0 dt1 dw2 dw4 dlr00 dlr01 dlr10 dlr11 dout".split()
+DMAS = "dx0 dx1 du dta dtb dtr dw dfl dow0 dow1 dv dw0 dw1 dt0 dt1 dw2 dw4 dlr00 dlr01 dlr10 dlr11 dout".split()
 DMAS += ["dl%d%d%d" % (_k // 4, _k // 2 % 2, _k % 2) for _k in range(12)]
 SEMAPHORES = "cv ca ct_ cp loc rn rf00 rf01 rf10 rf11 rf20 rc0 rc1 rc2 rs0 rs1 rs2".split() + DMAS
 
 ADD, SUB, MUL, MAX, MIN = AluOpType.add, AluOpType.subtract, AluOpType.mult, AluOpType.max, AluOpType.min
 EQ, NE, GT, GE, LT = AluOpType.is_equal, AluOpType.not_equal, AluOpType.is_gt, AluOpType.is_ge, AluOpType.is_lt
 AND, SHR = AluOpType.bitwise_and, AluOpType.arith_shift_right
-COPY = ActivationFunctionType.Copy
+COPY, SAME, SIGN = ActivationFunctionType.Copy, ActivationFunctionType.Identity, ActivationFunctionType.Sign
 ORDER = []
 PACE = ((0.85e-3, 0.15, 1.6, 2.0, 0.02, 1.56), (0.95e-3, 0.10, 2.0, 2.4, 0.03, 1.3), (1.1e-3, 0.15, 1.5, 2.6, 0.02, 1.9))
 
@@ -117,9 +118,61 @@ def arrange(ops):
                 end[k] = done + late[k]
             total += max(end)
         return total / len(cost)
+
+    def back(order):
+        left = [len(u) for u in users]
+        pos = [0] * n
+        for i, k in enumerate(order):
+            pos[k] = i
+        ready = {}
+        at, free, out = [0.0] * n, {q: 0.0 for q in qs}, [0.0] * n
+        for k in range(n):
+            if not left[k]:
+                at[k] = late[k] + move[k]
+                ready.setdefault(qs[k], []).append(k)
+        for _ in range(n):
+            t, q = min((max(min(at[k] for k in ks), free[q]), q) for q, ks in ready.items() if ks)
+            k = max([k for k in ready[q] if at[k] <= t + OPT["eps"]], key=lambda k: pos[k])
+            out[k] = free[q] = max(t, at[k]) + hold[k]
+            ready[q].remove(k)
+            for d in deps[k]:
+                at[d] = max(at[d], out[k] + late[d] + move[d])
+                left[d] -= 1
+                if not left[d]:
+                    ready.setdefault(qs[d], []).append(d)
+        return out
+
+    def chain(order, c):
+        hold, late, move = c
+        end, free, rings, last, why, ring = [0.0] * n, {q: 0.0 for q in qs}, 0.0, {}, [None] * n, None
+        for k in order:
+            t, w = free[qs[k]], (last.get(qs[k]), True)
+            for d in deps[k]:
+                if end[d] >= t:
+                    t, w = end[d], (d, False)
+            done = free[qs[k]] = t + hold[k]
+            if move[k]:
+                if rings > done:
+                    w = (ring, True)
+                done = rings = max(rings, done) + move[k]
+                ring = k
+            last[qs[k]], why[k], end[k] = k, w, done + late[k]
+        k, out = max(range(n), key=lambda k: end[k]), []
+        while why[k][0] is not None:
+            if why[k][1]:
+                out.append((why[k][0], k))
+            k = why[k][0]
+        return out
     rank = [way[k] + ops[k]["pri"] for k in range(n)]
     order = place(rank)
     best, x = span(order), OPT["seed"]
+    o = order
+    for _ in range(OPT["turns"]):
+        other = back(o)
+        o = place(other)
+        t = span(o)
+        if t <= best:
+            best, rank, order = t, other, o
     for _ in range(OPT["tries"]):
         other = list(rank)
         for k in range(n):
@@ -131,6 +184,37 @@ def arrange(ops):
         t = span(o)
         if t <= best:
             best, rank, order = t, other, o
+    now, t0, pairs = order, best, []
+    for step in range(OPT["swaps"]):
+        if not pairs:
+            pairs = chain(now, cost[step % len(cost)])
+        x = (x * 1103515245 + 12345) % 2147483648
+        a, b = pairs.pop((x >> 8) % len(pairs))
+        i, j = now.index(a), now.index(b)
+        mid = now[i:j + 1]
+        if (x >> 7) % 2:
+            take = {b}
+            for k in reversed(mid):
+                if k in take:
+                    take.update(deps[k])
+            if a in take:
+                continue
+            new = [k for k in mid if k in take] + [k for k in mid if k not in take]
+        else:
+            take = {a}
+            for k in mid:
+                if k in take:
+                    take.update(users[k])
+            if b in take:
+                continue
+            new = [k for k in mid if k not in take] + [k for k in mid if k in take]
+        o = now[:i] + new + now[j + 1:]
+        t = span(o)
+        x = (x * 1103515245 + 12345) % 2147483648
+        if t <= t0 + OPT["heat"] * (1 - step / OPT["swaps"]) * x / 2147483648:
+            now, t0, pairs = o, t, []
+            if t < best:
+                best, order = t, o
     OPT["span"] = best
     return order
 
@@ -194,6 +278,10 @@ def rank_program(g, core, T, topo):
     def count(out, in_, total):
         run("A", lambda: g.scalar.activation(out[0], in_[0], COPY, accum_out=total[0]), [out, total], [in_], 100, in_[2])
 
+    def line(out, in_, func, scale, bias):
+        ins = [in_] + [e for e in (scale, bias) if isinstance(e, tuple)]
+        run("A", lambda: g.scalar.activation(out[0], in_[0], func, bias=bias[0], scale=scale[0] if isinstance(scale, tuple) else scale), [out], ins, in_[2])
+
     def scaled(q, out, in_, scale):
         if q == "A":
             act(out, in_, scale)
@@ -201,7 +289,8 @@ def rank_program(g, core, T, topo):
             ts(out, in_, scale, MUL)
 
     def tt(out, a, b, op):
-        run("V", lambda: g.vector.tensor_tensor(out[0], a[0], b[0], op), [out], [a, b], *(price(out, a) if a[3] is None else (a[2] * (1 if a[3] in PSUM else 2), 0)))
+        run("V", lambda: g.vector.tensor_tensor(out[0], a[0], b[0], op), [out], [a, b],
+            *(price(out, a) if a[3] is None else (a[2] * (1 if a[3] in PSUM or b[3] in PSUM else 2), 0)))
 
     def ts(out, a, s1, op0, s2=None, op1=None):
         ins = [a] + [s for s in (s1, s2) if isinstance(s, tuple)]
@@ -241,17 +330,13 @@ def rank_program(g, core, T, topo):
         else:
             iota(out, [[0, out[2]]], 0)
 
-    def one(G, k=1):
-        return (16 * G, 16 * G + k)
-
     def col(k, p=(0, 128)):
         return v("col", k, k + 1, p=p)
 
     pri[0] = 9.0
     dma("S", "dta", v("tia", 0, 32), inp(T.ti[0:4, :]), 16384, 128)
     dma("A", "dtb", v("tib", 0, 32, p=(0, 96)), inp(T.ti[4:7, :]), 12288, 96)
-    run("V", lambda: g.vector.memset(T.flr[:], 0), [v("flr", 0, 32)], [], 1)
-    dma("A", "dfr", rows16("flr", 0, 128, 0, 32), inp(T.fl[:]))
+    dma("S", "dfl", v("flw", 0, 2), inp(T.fl[:]), 1024, 128)
     pri[0] = 0.0
     dma("S", "dx0", v("xt", 0, 768), inp(T.x[:, 0:768]), 196608, 128)
     dma("A", "du", v("ut", 0, 512), inp(T.u[:]), 131072, 128)
@@ -276,17 +361,18 @@ def rank_program(g, core, T, topo):
     ts(v("pint", 2, 3), v("pidx", 0, 1), 4, SHR)
     copy(v("pf", 0, 3), v("pint", 0, 3))
     i15, blk, grp = v("pf", 0, 1), v("pf", 1, 2), v("pf", 2, 3)
+    ts(col(11), blk, 3.0, EQ, 2.0, MUL)
     ts(col(0), blk, 32.0, MUL, 32.0, ADD)
-    ts(col(1), blk, 32.0, MUL, 160.0, ADD)
+    ts(col(1), blk, 32.0, MUL, 162.0, ADD)
     ts(col(2), i15, 0.0, EQ, -15.0, MUL)
     ts(col(3), i15, 0.0, EQ, 160.0, MUL)
     ts(col(4), grp, 6.0, EQ, 175.0, MUL)
-    ts(col(5), grp, 5.0, EQ, 166.0, MUL)
-    ts(col(7), grp, 6.0, EQ, 24.0, MUL)
-    dead, more, alive = col(8), col(9), col(10)
+    ts(col(5), grp, 3.0, GE, 102.0, MUL)
+    ts(col(7), grp, 6.0, EQ, -78.0, MUL)
+    dead, more = col(8), col(9)
     ts(dead, col(4), 17.0, ADD)
     ts(more, col(5), col(7), ADD, 8.0, ADD)
-    ts(alive, more, col(4), ADD, 17.0, ADD)
+    fill(col(12), float(C))
     ts(col(6), i15, 8.0, GE, 8.0, MUL)
     ts(v("l16", 0, 2), v("s16", 0, 2), i15, ADD)
     iota(v("c32", 0, 8), [[0, 2], [32, 4]], 0)
@@ -298,16 +384,19 @@ def rank_program(g, core, T, topo):
     for b in range(2):
         fill(v("xt", 896 * b + 768, 896 * b + 896), 0.0)
         fill(v("stg%d" % b, 0, 32), 0.0)
-        fill(v("stt%d" % b, 0, 32, p=(96, 128)), 0.0)
-    TAB = [0] + [480 + 1056 * h for h in range(1, 7)]
-    SIX = TAB[6] - 32
+        fill(v("stt%d" % b, 0, 32, p=(64, 128)), 0.0)
+    TAB = [0] + [480 + 1056 * h + 66 * (h > 3) for h in range(1, 8)]
+    LATE = TAB[4] - 96
+
+    def row(G, a, z):
+        return (T.win[16 * G:16 * G + 1, a:z], [("win", (16 * G, 16 * G + 1, a // 8 * 8, -(-z // 8) * 8, 1))])
     ts(v("win", 1024, 1280), v("zero", 0, 256), col(2), ADD, 32.0, ADD)
-    ts(v("win", 1216, 1248, p=(0, 96)), v("zero", 0, 32, p=(0, 96)), col(3, (0, 96)), ADD, 32.0, ADD)
+    ts(v("win", 1218, 1250, p=(0, 96)), v("zero", 0, 32, p=(0, 96)), col(3, (0, 96)), ADD, 32.0, ADD)
     iota(v("win", 1280, 1536), [[0, 8], [1, 16], [16, 2]], 0)
-    iota(v("win", SIX, SIX + 32), [[1, 16], [16, 2]], 0)
+    iota(v("win", LATE, TAB[4]), [[0, 3], [1, 16], [16, 2]], 0)
     for h in range(7):
-        zeros(OPT["fills"][h], v("win", TAB[h], TAB[h] + (1024 if h in (0, 5, 6) else 1056)))
-    ts(v("tab", 0, 32), v("tia", 0, 32), col(0), ADD)
+        zeros(OPT["fills"][h], v("win", TAB[h], 1024 if h == 0 else LATE if h == 3 else TAB[h + 1]))
+    ts(v("tab", 0, 32), v("tia", 0, 32), col(0), ADD, col(11), ADD)
     ts(v("tab", 32, 64, p=(0, 64)), v("tib", 0, 32, p=(0, 64)), col(1, (0, 64)), ADD)
     p6 = (64, 96)
     ts(v("odd", 0, 32, p=p6), v("tib", 0, 32, p=p6), 1, AND)
@@ -321,26 +410,23 @@ def rank_program(g, core, T, topo):
         return (T.tdr[a:b, 0:k, :], [("tdr", (a, b, 0, k, 1))])
     for h in range(2):
         for G in range(6):
-            dma("S", "dw%d" % h, v("win", TAB[h], TAB[h] + 1024, p=one(G)), v("tat", 0, 32, p=(32 * h, 32 * h + 32)), 2048, 32)
+            dma("S", "dw%d" % h, row(G, TAB[h], TAB[h] + 1024), v("tat", 0, 32, p=(32 * h, 32 * h + 32)), 2048, 32)
     dma("S", "dt0", (T.tdr[:, 32, :], [("tdr", (0, 5, 32, 33, 1))]), v("zero", 0, 32, p=(0, 5)))
     dma("S", "dt0", staged(0, 2, 32), v("tat", 0, 32, p=(64, 128)), 4096, 64)
     dma("S", "dt1", staged(2, 5, 32), v("tat", 32, 64, p=(0, 96)), 6144, 96)
     for G in range(6):
-        dma("S", "dw2", v("win", TAB[2], TAB[4], p=one(G)), staged(0, 2), 4224)
+        dma("S", "dw2", row(G, TAB[2], TAB[2] + 2112), staged(0, 2), 4224)
     for G in range(6):
-        dma("S", "dw4", v("win", TAB[4], TAB[6], p=one(G)), staged(2, 4), 4224)
-        k = dma("S", "dw4", v("win", TAB[6], 7840, p=one(G)), staged(4, 5, 32), 2048)
-    dma("S", "dfl", v("flw", 0, 2), inp(T.fl[:]), 1024, 128)
+        k = dma("S", "dw4", row(G, TAB[4], TAB[7]), staged(2, 5), 6336)
     dma("S", "dtr", v("trt", 0, 128), inp(T.tr[:]), 32768, 128, (k,))
     dma("S", "dw", codes("wq", 0, 512), inp(T.wc[:]), 262144, 128, (k,))
     dma("S", "dw", v("wp", 0, 512), inp(T.ws[:]), 65536, 128, (k,))
     dma("S", "dv", v("vt", 0, 512), inp(T.v[:]), 131072, 128, (k,))
-    ts(v("own", 0, 32), v("flr", 0, 32), more, MUL, dead, ADD)
-    for G in range(6):
-        dma("A", "dow0", v("win", 1280, 1472, p=one(G)), rows16("own", 0, 96, 0, 32), 384, 6)
-    for G in range(6):
-        dma("S", "dow1", v("win", SIX, SIX + 32, p=one(G)), v("own", 0, 32, p=one(6)), 64, 1)
     ts(v("me", 0, 2), v("flw", 0, 2), more, MUL, dead, ADD)
+    for G in range(6):
+        dma(OPT["own"][G % 2], "dow0", row(G, 1280, 1408), v("me", 0, 2, p=(0, 64)), 256, 64)
+    for G in range(6):
+        dma("S", "dow1", row(G, LATE, TAB[4]), v("me", 0, 2, p=(64, 112)), 192, 48)
     quant(*pair("quc", "qus", 0, 128), v("ut", 0, 512))
     ul = v("ul", 0, 8)
     run("V", lambda: g.vector.tensor_copy(T.qpc[:, 0:128].bitcast(dt.uint32), T.quc[:, 0:128].bitcast(dt.uint32).indirect(ul[0])), [v("qpc", 0, 128)], [v("quc", 0, 128), ul], 60, 128)
@@ -353,7 +439,7 @@ def rank_program(g, core, T, topo):
     zeros("P", v("trt", 128, 512))
     quant(*pair("lc", "ls", 0, 128), v("trt", 0, 512))
     zeros("P", v("ctl", 128, 512))
-    zeros("P", v("tw", 0, 1152))
+    zeros("P", v("tw", 0, 768))
     for t in range(4):
         zeros("P", v("zp", 400 * t + 384, 400 * t + 400))
     for s in range(2):
@@ -393,30 +479,24 @@ def rank_program(g, core, T, topo):
             mx(bank(b, k, 0, 128), *pair("ec", "es", 128 * t, 128 * t + 128), *pair("lc", "ls", lo, lo + 128))
             if r < 0:
                 for s in range(2):
-                    act(v("tw", 96 * t + 16 * s, 96 * t + 16 * s + 16), bank(b, k, s, 32, 2), -1.0)
+                    act(v("tw", 64 * t + 16 * s, 64 * t + 16 * s + 16), bank(b, k, s, 32, 2), -1.0)
             else:
-                a = 384 * r + 96 * t
-                scaled("V" if r == ROUNDS - 1 and t % 2 else "A", v("tw", a + 64, a + 96), bank(b, k, 96, 128), -1.0)
-        if r >= 0:
-            tt(v("chg", 0, 2), mine(r + 1), mine(r), NE)
-            for s in range(2):
-                a = 4 + 2 * s if r == ROUNDS - 1 else 2 * r + s
-                ts(v("tl", a, a + 1), v("chg", s, s + 1), 64.0, MUL, v("l16", s, s + 1), ADD)
-        if 0 <= r < ROUNDS - 1:
-            for t in range(4):
-                a = 384 * r + 96 * t
-                act(v("tw", a + 384, a + 416), ind(v("tw", a, a + 96), v("tl", 2 * r, 2 * r + 2)))
+                a = 256 * r + 64 * t
+                tt(v("tw", a + 256, a + 288), v("tw", a, a + 32), bank(b, k, 96, 128), SUB)
 
     def keys(r):
-        ts(v("key", 0, 2), mine(r), dead, EQ, alive, MUL)
+        ts(v("key", 0, 2), mine(r), dead, EQ, more, MUL)
         for s in range(2):
             ts(v("key", 2 + s, 3 + s), theirs(r, s, s + 1), dead, EQ, v("key", s, s + 1), MUL)
+        ts(v("chg", 0, 2), v("key", 2, 4), 0.0, EQ, float(C), MUL)
 
-    def rows_out(r, early, name, a, step):
+    def rows_out(r, early, a):
         k, tk, tag = 4 * r + 2 * early, 2 * early, "%d%d" % (r, early)
+        line(v("got", a + 4, a + 6), v("got", a, a + 2), SAME, -1.0, col(12))
         for s in range(2):
-            ts(v("tk", tk + s, tk + s + 1), v(name, a + step * s, a + step * s + 1), float(C), LT, v("key", 2 + s, 3 + s), MUL)
-        tt(v("lim", k, k + 2), theirs(r), v("tk", tk, tk + 2), MAX)
+            line(v("tk", tk + s, tk + s + 1), v("got", a + 2 + s, a + 3 + s), SIGN, -1.0, v("got", a + 4 + s, a + 5 + s))
+        for s in range(2):
+            line(v("lim", k + s, k + s + 1), v("tk", tk + s, tk + s + 1), SAME, v("key", 2 + s, 3 + s), theirs(r, s, s + 1))
         sem, src, at = T.sem["rf" + tag], T.lim[:, k:k + 2], ("lw", (0, 128, 2 * r, 2 * r + 2, 1))
         if r == ROUNDS - 1:
             send([v("lim", k, k + 2)], n, lambda: g.remote_dma(T.lw[:, 2 * r:2 * r + 2], src, sem, T.sem.loc, pid, rid, full_mask), [at], "rf" + tag)
@@ -429,27 +509,26 @@ def rank_program(g, core, T, topo):
             send([v("lim", k, k + 2)], n, lambda: g.remote_dma_fused(tr, local_sem=T.sem.loc), where + [at], "rf" + tag)
         for G in range(6):
             if early:
-                dma("S", "dlr" + tag, v("win", 1280, 1472, p=one(G)), (fd[0:96, :], where), 384, 1)
+                dma("S", "dlr" + tag, row(G, 1280, 1408), (fd[0:64, :], where), 256, 1)
             else:
-                dma("S", "dlr" + tag, v("win", SIX, SIX + 32, p=one(G)), (fd[96:112, :], where), 64, 1)
+                dma("S", "dlr" + tag, row(G, LATE, TAB[4]), (fd[64:112, :], where), 192, 1)
 
     def early(r, b):
-        turn(v("stt%d" % b, 0, 32, p=(0, 96)), v("stg%d" % b, 0, 32, p=(0, 96)))
+        turn(v("stt%d" % b, 0, 32, p=(0, 64)), v("stg%d" % b, 0, 32, p=(0, 64)))
         if r < ROUNDS - 1:
             copy(v("oe%d" % b, 0, 16), ind(v("stt%d" % b, 0, 32), v("cl", 0, 1)))
             for s in range(2):
                 k = 2 * b + s
                 count(v("jnk", H * k, H * k + H), ind(v("mw", 64 * s, 64 * s + 64), v("oe%d" % b, 0, 12)), v("got", k, k + 1))
             if b:
-                tt(v("got", 4, 6), v("got", 0, 2), v("got", 2, 4), ADD)
-                rows_out(r, 1, "got", 4, 1)
+                rows_out(r, 1, 0)
 
     def claims(r):
         for s in range(2):
             e = v("mm", 384 * s, 384 * s + 384, -1)
             scan(v("pr", 384 * s, 384 * s + 384), e, e, MUL, ADD)
-        copy(v("clu", 0, 2), v("pr", 383, 768, 384))
-        rows_out(r, 0, "pr", 383, 384)
+            ts(v("clu", s, s + 1), v("pr", 384 * s + 383, 384 * s + 384), v("chg", s, s + 1), MAX)
+        rows_out(r, 0, 6)
         for t in range(4):
             act(v("ctl", t, 128, 4), ind(v("zp", 400 * t, 400 * t + 400), v("clu", 0, 2)))
         qc, qs, a = T["qcc%d" % r], T["qcs%d" % r], 128 + 32 * r
@@ -486,7 +565,7 @@ def rank_program(g, core, T, topo):
         z = a + 32 * m
 
         def stage(h, row, a):
-            dma("S", "dl%d%d%d" % (r, b, h // 6), v("stg%d" % b, 16 * (h % 2), 16 * (h % 2) + 16, p=(32 * (h // 2), 32 * (h // 2) + 12)), rows16(res, row, 96, a, a + 32), 384, 12)
+            dma("S", "dl%d%d%d" % (r, b, h // 4), v("stg%d" % b, 16 * (h % 2), 16 * (h % 2) + 16, p=(32 * (h // 2), 32 * (h // 2) + 12)), rows16(res, row, 96, a, a + 32), 384, 12)
         stage(h, 1, z - 32)
         if h < 6:
             turn(v(trb, a, z), v(res, a, z))
@@ -503,13 +582,13 @@ def rank_program(g, core, T, topo):
                 act(v("fs%d" % b, H * t, H * t + H), bank(b, t))
 
     def diff(r, b):
-        turn(v("stt%d" % b, 0, 32, p=(96, 128)), v("stg%d" % b, 0, 32, p=(96, 128)))
+        turn(v("stt%d" % b, 0, 32, p=(64, 128)), v("stg%d" % b, 0, 32, p=(64, 128)))
         copy(v("ol%d" % b, 0, 16), ind(v("stt%d" % b, 0, 32), v("cl", 0, 1)))
         ol, zt = v("ol%d" % b, 0, 12), "zt%d" % b
         for s in range(2):
-            act(v("mm", 384 * s + H * b, 384 * s + H * b + H), ind(v("mw", 64 * s, 64 * s + 64), ol))
+            count(v("mm", 384 * s + H * b, 384 * s + H * b + H), ind(v("mw", 64 * s, 64 * s + 64), ol), v("got", 6 + 2 * b + s, 7 + 2 * b + s))
         for t in range(4):
-            w = ind(v("tw", 384 * r + 96 * t, 384 * r + 96 * t + 64), ol)
+            w = ind(v("tw", 256 * r + 64 * t, 256 * r + 64 * t + 64), ol)
             if t < OPT["nv"]:
                 tt(v(zt, t, 768, 4), w, v("fs%d" % b, H * t, H * t + H), ADD)
             else:
@@ -539,9 +618,12 @@ def rank_program(g, core, T, topo):
         keys(r)
         for h in range(7):
             both(level, r, h)
+        mark = len(ops)
         both(early, r)
+        for o in ops[mark:]:
+            o["pri"] += OPT["soon"]
         both(diff, r)
-        pri[0] = OPT["claim"]
+        pri[0] = OPT["claim"] + OPT["last"] * (r == ROUNDS - 1)
         claims(r)
         both(layer, r)
     r = ROUNDS - 1
@@ -560,9 +642,9 @@ def rank_program(g, core, T, topo):
     dma("S", "dout", inp(T.bp[:, 384:416]), v("full", 0, 2), 1024, 128)
     unpack(r)
     for t in range(4):
-        a = 384 * r + 96 * t
+        a = 768 + 64 * t
         for s in range(2):
-            scaled("V" if t % 2 else "A", v("rtt", 4 * s + t, 128, 8), ind(v("tw", a, a + 96), v("tl", 4 + 2 * s, 5 + 2 * s)), -64.0)
+            scaled("VA"[s] if t < 3 else "V", v("rtt", 4 * s + t, 128, 8), v("tw", a + 16 * s, a + 16 * s + 16), -64.0)
     dma("S", "dout", inp(T.rt[:]), v("rtt", 0, 128), 65536, 128)
 
     if not ORDER:

@@ -3,38 +3,39 @@ from concourse.bass import DstId, RemoteDMATransfer
 from concourse.mybir import dt, AluOpType, AxisListType, ActivationFunctionType
 
 ROUNDS, C, H = 3, 384, 192
-OPT = dict(share=(3, 3, 2, 2, 1, 1, 0), nv=2, full="VVAA", eps=0.05, bias=1.0, claim=0.0, fills="VVAAAPP", own="SA", soon=0.0, last=0.0,
+OPT = dict(share=(3, 3, 2, 2, 1, 1, 0), nv=2, full="AAAA", eps=0.05, bias=1.0, claim=1.0, fills="AAP", more="AAAAA", tell=3.0, ahead="tx", rows="SS", soon=1.0, last=0.0,
            turns=5, tries=300, amp=0.3, part=0.05, swaps=6000, heat=0.06, seed=1)
 KIND = {"f": "float32", "b": "bfloat16", "i": "int32", "h": "uint16", "s": "uint8", "c": "float8_e4m3fn_x4", "e": "float16"}
-SPEC = """b xt 1792 ut 512 vt 512 trt 512 et 2048 win 7952 tab 64 tat 64 res0 1152 res1 1152 trb0 1152 trb1 1152 bits 288 ev0 144 ev1 144 horn 144
-b stg0 32 stg1 32 stt0 32 stt1 32 gt0 768 gt1 768 fs0 768 fs1 768 zt0 768 zt1 768 zp 1600 mw 128 mm 768 lim 16 ctl 512 zero 1056 lw 6 tw 1024
-b bw 64 me 2 nx 2 clr 32 clt 32 jnk 768
+SPEC = """b xt 1792 ut 512 vt 512 trt 512 et 516 win 3200 tab 64 tat 64 res0 1152 res1 1152 trb0 1152 trb1 1152 bits 288 ev0 144 ev1 144 horn 144
+b stg0 32 stg1 32 stt0 32 stt1 32 gt0 768 gt1 768 fs0 768 fs1 768 zt0 768 zt1 768 zp 1600 mw 64 mwe 128 mm 384 lim 6 ctl 512 zero 1024 lw 6 tw 1024
+b bw 64 me 4 nx 4 clr 32 clt 32 jnk 384 ste 32 stf 32 le0 2 le1 2 lwe 2 up 384 down 384 mwa 128
 e pr 768
 c qxc 448 qfc 384 quc 128 qpc 128 qvc 128 wq 512 ec 512 qzc 384 qcc0 128 qcc1 128 qcc2 128 lc 224
 s qxs 448 qfs 384 qus 128 qps 128 qvs 128 wp 512 es 512 qzs 384 qcs0 128 qcs1 128 qcs2 128 ls 224
-i tia 32 tib 32 pidx 1 pint 3 flw 2 odd 64
-h ol0 16 ol1 16 oe0 16 oe1 16 clu 2 of0 128 of1 128 cl 2 ul 8
-f ones 128 idn 128 rtt 128 yt 384 bpt 384 full 2 pf 3 s16 2 l16 2 i64 64 col 16 tk 4 c32 8 got 12 key 4 chg 2 plc 32"""
+i tia 32 tib 32 pidx 1 pint 4 flw 2 fle 1 flr 32 odd 64
+h ol0 16 ol1 16 oe 24 clu 2 of0 128 of1 128 cl 2 ul 8
+f rtt 128 yt 384 bpt 384 full 2 pf 4 s16 2 l16 2 col 24 tk 4 c32 8 got 2 key 4 chg 2 plc 32"""
 PSUM = tuple("pb%d" % k for k in range(8))
-SCRATCH = {"tdr": ("dram", [5, 33, 32], "bfloat16")}
-for _n in ("fd00", "fd01", "fd10", "fd11"):
-    SCRATCH[_n] = ("dram", [128, 2], "bfloat16")
+SCRATCH = {"tdr": ("dram", [5, 32, 32], "bfloat16")}
+for _n in range(2):
+    SCRATCH["fd%d" % _n] = ("dram", [128, 2], "bfloat16")
+    SCRATCH["fe%d" % _n] = ("dram", [128, 1], "bfloat16")
 for _l in SPEC.split("\n"):
     _w = _l.split()
     for _k in range(1, len(_w), 2):
         SCRATCH[_w[_k]] = ("sbuf", [128, int(_w[_k + 1])], KIND[_w[0]])
 for _n in PSUM:
     SCRATCH[_n] = ("psum", [128, 512], "float32")
-DMAS = "dx0 dx1 du dta dtb dtr dw dfl dow0 dow1 dv dw0 dw1 dt0 dt1 dw2 dw4 dlr00 dlr01 dlr10 dlr11 dout".split()
-DMAS += ["dl%d%d%d" % (_k // 4, _k // 2 % 2, _k % 2) for _k in range(12)]
-SEMAPHORES = "cv ca ct_ cp loc rn rf00 rf01 rf10 rf11 rf20 rc0 rc1 rc2 rs0 rs1 rs2".split() + DMAS
+DMAS = "dx0 dx1 du dta dtb dtr dw dfl dfr dv dw0 dt0 dt1 dw2 dw4 dlr0 dlr1 der0 der1 dme de0 de1 dout".split()
+DMAS += ["dl%d%d" % (_k // 2, _k % 2) for _k in range(6)]
+SEMAPHORES = "cv ca ct_ cp loc rn rf0 rf1 rf2 re0 re1 rc0 rc1 rc2 rs0 rs1 rs2".split() + DMAS
 
 ADD, SUB, MUL, MAX, MIN = AluOpType.add, AluOpType.subtract, AluOpType.mult, AluOpType.max, AluOpType.min
 EQ, NE, GT, GE, LT = AluOpType.is_equal, AluOpType.not_equal, AluOpType.is_gt, AluOpType.is_ge, AluOpType.is_lt
 AND, SHR = AluOpType.bitwise_and, AluOpType.arith_shift_right
 COPY, SAME, SIGN = ActivationFunctionType.Copy, ActivationFunctionType.Identity, ActivationFunctionType.Sign
 ORDER = []
-PACE = ((0.85e-3, 0.15, 1.6, 2.0, 0.02, 1.56), (0.95e-3, 0.10, 2.0, 2.4, 0.03, 1.3), (1.1e-3, 0.15, 1.5, 2.6, 0.02, 1.9))
+PACE = ((0.88e-3, 0.2, 0.8, 1.7, 0.03, 1.56), (0.85e-3, 0.2, 1.2, 2.8, 0.04, 1.3), (1.15e-3, 0.2, 1.0, 2.0, 0.03, 1.9))
 
 
 def hit(a, b):
@@ -278,9 +279,11 @@ def rank_program(g, core, T, topo):
     def count(out, in_, total):
         run("A", lambda: g.scalar.activation(out[0], in_[0], COPY, accum_out=total[0]), [out, total], [in_], 100, in_[2])
 
-    def line(out, in_, func, scale, bias):
-        ins = [in_] + [e for e in (scale, bias) if isinstance(e, tuple)]
-        run("A", lambda: g.scalar.activation(out[0], in_[0], func, bias=bias[0], scale=scale[0] if isinstance(scale, tuple) else scale), [out], ins, in_[2])
+    def sign(out, in_):
+        run("A", lambda: g.scalar.activation(out[0], in_[0], SIGN), [out], [in_], in_[2])
+
+    def line(out, in_, scale, bias):
+        run("A", lambda: g.scalar.activation(out[0], in_[0], SAME, bias=bias[0], scale=scale[0]), [out], [in_, scale, bias], in_[2])
 
     def scaled(q, out, in_, scale):
         if q == "A":
@@ -301,8 +304,8 @@ def rank_program(g, core, T, topo):
         else:
             run("V", lambda: g.vector.tensor_scalar(out[0], a[0], x1, x2, op0, op1), [out], ins, *price(out, a))
 
-    def scan(out, a, b, op0, op1):
-        run("V", lambda: g.vector.tensor_tensor_scan(out[0], a[0], b[0], 0.0, op0, op1), [out], [a, b], *price(out, a))
+    def scan(out, a, b, first, op0, op1):
+        run("V", lambda: g.vector.tensor_tensor_scan(out[0], a[0], b[0], first, op0, op1), [out], [a, b], *price(out, a))
 
     def fill(out, c):
         run("V", lambda: g.vector.memset(out[0], c), [out], [], *price(out, out))
@@ -320,34 +323,49 @@ def rank_program(g, core, T, topo):
         run("V", lambda: g.vector.transpose(out[0], in_[0]), [out], [in_], *price(out, in_))
 
     def iota(out, pattern, base, cm=0):
-        run("P", lambda: g.iota(out[0], pattern, base, cm, allow_small_or_imprecise_dtypes=True), [out], [], 160 + 2 * out[2])
-
-    def zeros(q, out):
-        if q == "A":
-            act(out, v("zero", 0, out[2]))
-        elif q == "V":
-            fill(out, 0.0)
+        if SCRATCH[out[3]][2] == "int32":
+            run("P", lambda: g.iota(out[0], pattern, base, cm), [out], [], 160 + 2 * out[2])
         else:
-            iota(out, [[0, out[2]]], 0)
+            run("P", lambda: g.iota(out[0], pattern, base, cm, allow_small_or_imprecise_dtypes=True), [out], [], 160 + 2 * out[2])
 
-    def col(k, p=(0, 128)):
-        return v("col", k, k + 1, p=p)
+    def const(q, out, c=0):
+        if q == "A":
+            z = v("zero", 0, out[2])
+            run("A", lambda: g.scalar.activation(out[0], z[0], COPY, bias=float(c)) if c else g.scalar.activation(out[0], z[0], COPY), [out], [z], out[2])
+        elif q == "V":
+            fill(out, float(c))
+        else:
+            iota(out, [[0, out[2]]], c)
 
+    def col(k, n=1):
+        return v("col", k, k + n)
+
+    iota(v("flr", 0, 32), [[-1, 16], [-16, 2]], 32)
     pri[0] = 9.0
     dma("S", "dta", v("tia", 0, 32), inp(T.ti[0:4, :]), 16384, 128)
-    dma("A", "dtb", v("tib", 0, 32, p=(0, 96)), inp(T.ti[4:7, :]), 12288, 96)
-    dma("S", "dfl", v("flw", 0, 2), inp(T.fl[:]), 1024, 128)
     pri[0] = 0.0
+    dma("S", "du", v("ut", 0, 512), inp(T.u[:]), 131072, 128)
     dma("S", "dx0", v("xt", 0, 768), inp(T.x[:, 0:768]), 196608, 128)
-    dma("A", "du", v("ut", 0, 512), inp(T.u[:]), 131072, 128)
-    dma("S", "dx1", v("xt", 896, 1664), inp(T.x[:, 768:1536]), 196608, 128)
+    for G in range(6):
+        dma("S", "dfr", v("flr", 0, 32, p=(16 * G, 16 * G + 7)), inp(T.fl[0:7, :]), 896, 7)
 
-    fill(v("zero", 0, 1056), 0.0)
-    fill(v("ones", 0, 128), 1.0)
+    def loads(names, after):
+        for c in names:
+            if c == "t":
+                dma("S", "dtb", v("tib", 0, 32, p=(0, 96)), inp(T.ti[4:7, :]), 12288, 96, after)
+            elif c == "x":
+                dma("S", "dx1", v("xt", 896, 1664), inp(T.x[:, 768:1536]), 196608, 128, after)
+            else:
+                dma("S", "dfl", v("flw", 0, 2), inp(T.fl[:]), 1024, 128, after)
+                dma("S", "dfl", v("fle", 0, 1), inp(T.fl[0:4, :]), 512, 128, after)
+    loads(OPT["ahead"], ())
+
+    if "A" in OPT["fills"]:
+        fill(v("zero", 0, 1024), 0.0)
+    else:
+        fill(v("zero", 0, 64), 0.0)
     iota(v("pidx", 0, 1), [[0, 1]], 0, 1)
-    run("P", lambda: g.affine_select(T.idn[:], T.ones[:], [[-1, 128]], EQ, 0.0, 0, 1), [v("idn", 0, 128)], [v("ones", 0, 128)], 460)
-    iota(v("s16", 0, 2), [[16, 2]], 0)
-    iota(v("i64", 0, 64), [[1, 64]], 0)
+    iota(v("s16", 0, 2), [[1, 2]], 0)
     iota(v("bw", 0, 32), [[1, 2], [2, 16]], 0)
     fill(v("bw", 32, 64), -1.0)
     fill(v("clr", 0, 32), 0.0)
@@ -356,94 +374,88 @@ def rank_program(g, core, T, topo):
     copy(v("clr", 16, 28, p=(96, 128)), v("clr", 0, 12, p=(96, 128)))
     turn(v("clt", 0, 32), v("clr", 0, 32))
     copy(v("cl", 0, 1), v("clt", 0, 1))
-    ts(v("pint", 0, 1), v("pidx", 0, 1), 15, AND)
-    ts(v("pint", 1, 2), v("pidx", 0, 1), 5, SHR)
-    ts(v("pint", 2, 3), v("pidx", 0, 1), 4, SHR)
-    copy(v("pf", 0, 3), v("pint", 0, 3))
-    i15, blk, grp = v("pf", 0, 1), v("pf", 1, 2), v("pf", 2, 3)
-    ts(col(11), blk, 3.0, EQ, 2.0, MUL)
-    ts(col(0), blk, 32.0, MUL, 32.0, ADD)
-    ts(col(1), blk, 32.0, MUL, 162.0, ADD)
-    ts(col(2), i15, 0.0, EQ, -15.0, MUL)
-    ts(col(3), i15, 0.0, EQ, 160.0, MUL)
-    ts(col(4), grp, 6.0, EQ, 175.0, MUL)
-    ts(col(5), grp, 3.0, GE, 102.0, MUL)
-    ts(col(7), grp, 6.0, EQ, -78.0, MUL)
-    dead, more = col(8), col(9)
-    ts(dead, col(4), 17.0, ADD)
-    ts(more, col(5), col(7), ADD, 8.0, ADD)
-    fill(col(12), float(C))
-    ts(col(6), i15, 8.0, GE, 8.0, MUL)
-    ts(v("l16", 0, 2), v("s16", 0, 2), i15, ADD)
+    for k, (c, op) in enumerate(((15, AND), (4, SHR), (5, SHR), (31, AND))):
+        ts(v("pint", k, k + 1), v("pidx", 0, 1), c, op)
+    copy(v("pf", 0, 4), v("pint", 0, 4))
+    i15, i31, lev = v("pf", 0, 1), v("pf", 3, 4), v("pf", 0, 3)
+    ts(col(8, 3), lev, 1.0, GE, 32.0, MUL)
+    ts(col(12, 3), lev, 3.0, GE, -32.0, MUL)
+    ts(col(16, 3), lev, 6.0, LT, 32.0, ADD)
+    tt(col(20, 3), col(8, 3), col(12, 3), ADD)
+    tt(col(0, 3), col(20, 3), col(16, 3), ADD)
+    ts(col(8, 3), lev, 6.0, NE, 31.0, MUL)
+    ts(col(4, 3), col(8, 3), -32.0, ADD)
+    dead, more = col(1), col(5)
+    ts(col(3), i15, 8.0, GE, 8.0, MUL)
     iota(v("c32", 0, 8), [[0, 2], [32, 4]], 0)
-    ts(v("ul", 0, 8), v("c32", 0, 8), i15, ADD, col(6), ADD)
+    ts(v("ul", 0, 8), v("c32", 0, 8), i15, ADD, col(3), ADD)
     fill(v("horn", 0, 144), 2.0)
     fill(v("horn", 0, 144, 8), 0.0)
     fill(v("bits", 0, 288), 0.0)
-    fill(v("bits", 68, 288, 72), 40.0)
+    fill(v("bits", 68, 288, 72), 32.0)
     for b in range(2):
-        fill(v("xt", 896 * b + 768, 896 * b + 896), 0.0)
+        const("P", v("xt", 896 * b + 768, 896 * b + 896))
         fill(v("stg%d" % b, 0, 32), 0.0)
-        fill(v("stt%d" % b, 0, 32, p=(64, 128)), 0.0)
-    TAB = [0] + [480 + 1056 * h + 66 * (h > 3) for h in range(1, 8)]
-    LATE = TAB[4] - 96
+    fill(v("ste", 0, 32), 0.0)
+    TAB = (1024, 1024, 0, 0, 2112, 2112, 2112)
+    SOON, LATE = 2048, 3136
 
-    def row(G, a, z):
-        return (T.win[16 * G:16 * G + 1, a:z], [("win", (16 * G, 16 * G + 1, a // 8 * 8, -(-z // 8) * 8, 1))])
-    ts(v("win", 1024, 1280), v("zero", 0, 256), col(2), ADD, 32.0, ADD)
-    ts(v("win", 1218, 1250, p=(0, 96)), v("zero", 0, 32, p=(0, 96)), col(3, (0, 96)), ADD, 32.0, ADD)
-    iota(v("win", 1280, 1536), [[0, 8], [1, 16], [16, 2]], 0)
-    iota(v("win", LATE, TAB[4]), [[0, 3], [1, 16], [16, 2]], 0)
-    for h in range(7):
-        zeros(OPT["fills"][h], v("win", TAB[h], 1024 if h == 0 else LATE if h == 3 else TAB[h + 1]))
-    ts(v("tab", 0, 32), v("tia", 0, 32), col(0), ADD, col(11), ADD)
-    ts(v("tab", 32, 64, p=(0, 64)), v("tib", 0, 32, p=(0, 64)), col(1, (0, 64)), ADD)
+    def rows(G, h, k, a, z):
+        return v("win", a, z, p=(16 * G + h, 16 * G + k))
+    for q, a in zip(OPT["fills"], (1024, 0, 2112)):
+        const(q, v("win", a, a + 1024))
+    for a in (SOON, LATE):
+        ts(v("win", a, a + 32), v("flr", 0, 32), col(4), MUL, col(0), ADD)
+        ts(v("win", a + 32, a + 64), v("zero", 0, 32), col(0), ADD)
+    copy(v("tab", 0, 32), v("tia", 0, 32))
+    turn(v("tat", 0, 32), v("tab", 0, 32))
+
+    def staged(a, b):
+        return (T.tdr[a:b, :, :], [("tdr", (a, b, 0, 1, 1))])
+    for G in range(6):
+        k = dma(OPT["rows"][G % 2], "dw0", rows(G, 0, 2, 1024, 2048), v("tat", 0, 32, p=(0, 64)), 4096, 64)
+    dma("S", "dt0", staged(0, 2), v("tat", 0, 32, p=(64, 128)), 4096, 64)
+    loads([c for c in "txf" if c not in OPT["ahead"]], (k,))
+    copy(v("tab", 32, 64, p=(0, 64)), v("tib", 0, 32, p=(0, 64)))
     p6 = (64, 96)
     ts(v("odd", 0, 32, p=p6), v("tib", 0, 32, p=p6), 1, AND)
     ts(v("odd", 32, 64, p=p6), v("tib", 0, 32, p=p6), 1, SHR)
-    ts(v("plc", 0, 32, p=p6), v("odd", 0, 32, p=p6), 16.0, MUL, 224.0, ADD)
+    ts(v("plc", 0, 32, p=p6), v("odd", 0, 32, p=p6), 16.0, MUL)
     tt(v("tab", 32, 64, p=p6), v("plc", 0, 32, p=p6), v("odd", 32, 64, p=p6), ADD)
-    turn(v("tat", 0, 32), v("tab", 0, 32))
     turn(v("tat", 32, 64, p=(0, 96)), v("tab", 32, 64, p=(0, 96)))
-
-    def staged(a, b, k=33):
-        return (T.tdr[a:b, 0:k, :], [("tdr", (a, b, 0, k, 1))])
-    for h in range(2):
-        for G in range(6):
-            dma("S", "dw%d" % h, row(G, TAB[h], TAB[h] + 1024), v("tat", 0, 32, p=(32 * h, 32 * h + 32)), 2048, 32)
-    dma("S", "dt0", (T.tdr[:, 32, :], [("tdr", (0, 5, 32, 33, 1))]), v("zero", 0, 32, p=(0, 5)))
-    dma("S", "dt0", staged(0, 2, 32), v("tat", 0, 32, p=(64, 128)), 4096, 64)
-    dma("S", "dt1", staged(2, 5, 32), v("tat", 32, 64, p=(0, 96)), 6144, 96)
+    dma("S", "dt1", staged(2, 5), v("tat", 32, 64, p=(0, 96)), 6144, 96)
     for G in range(6):
-        dma("S", "dw2", row(G, TAB[2], TAB[2] + 2112), staged(0, 2), 4224)
+        dma("S", "dw2", rows(G, 2, 4, 0, 1024), staged(0, 2), 4096)
     for G in range(6):
-        k = dma("S", "dw4", row(G, TAB[4], TAB[7]), staged(2, 5), 6336)
+        k = dma("S", "dw4", rows(G, 4, 7, 2112, 3136), staged(2, 5), 6144)
     dma("S", "dtr", v("trt", 0, 128), inp(T.tr[:]), 32768, 128, (k,))
-    dma("S", "dw", codes("wq", 0, 512), inp(T.wc[:]), 262144, 128, (k,))
+    for a in (0, 256):
+        dma("S", "dw", codes("wq", a, a + 256), inp(T.wc[:, 4 * a:4 * a + 1024]), 131072, 128, (k,))
     dma("S", "dw", v("wp", 0, 512), inp(T.ws[:]), 65536, 128, (k,))
-    dma("S", "dv", v("vt", 0, 512), inp(T.v[:]), 131072, 128, (k,))
     ts(v("me", 0, 2), v("flw", 0, 2), more, MUL, dead, ADD)
-    for G in range(6):
-        dma(OPT["own"][G % 2], "dow0", row(G, 1280, 1408), v("me", 0, 2, p=(0, 64)), 256, 64)
-    for G in range(6):
-        dma("S", "dow1", row(G, LATE, TAB[4]), v("me", 0, 2, p=(64, 112)), 192, 48)
+    ts(v("me", 2, 3), v("fle", 0, 1), -1.0, MUL, col(2), ADD)
+    copy(v("me", 3, 4), col(2))
     quant(*pair("quc", "qus", 0, 128), v("ut", 0, 512))
     ul = v("ul", 0, 8)
     run("V", lambda: g.vector.tensor_copy(T.qpc[:, 0:128].bitcast(dt.uint32), T.quc[:, 0:128].bitcast(dt.uint32).indirect(ul[0])), [v("qpc", 0, 128)], [v("quc", 0, 128), ul], 60, 128)
     act(v("qps", 0, 128), ind(v("qus", 0, 128), ul))
-    for k in range(2):
-        zeros("A", v("et", 1024 * k, 1024 * k + 1024))
+    fill(v("et", 0, 516), 2.0 ** -6)
+    run("P", lambda: g.affine_select(T.et[:], T.et[:], [[1, 516]], EQ, 0.0, -3, -4), [v("et", 0, 516)], [v("et", 0, 516)], 200 + 2 * 516)
     for b in range(4):
-        act(v("et", 512 * b + b, 512 * b + 512, 4), v("idn", 0, 128), 2.0 ** -6)
-    quant(*pair("ec", "es", 0, 512), v("et", 0, 2048))
-    zeros("P", v("trt", 128, 512))
+        quant(*pair("ec", "es", 128 * b, 128 * b + 128), v("et", 3 - b, 515 - b))
+    const(OPT["more"][0], v("trt", 128, 512))
     quant(*pair("lc", "ls", 0, 128), v("trt", 0, 512))
-    zeros("P", v("ctl", 128, 512))
-    zeros("P", v("tw", 0, 768))
+    const(OPT["more"][1], v("ctl", 128, 512))
+    const(OPT["more"][2], v("tw", 0, 768))
+    const(OPT["more"][3], v("up", 0, 384), 1)
+    const(OPT["more"][4], v("down", 0, 384), -1)
     for t in range(4):
-        zeros("P", v("zp", 400 * t + 384, 400 * t + 400))
-    for s in range(2):
-        ts(v("mw", 64 * s, 64 * s + 64), v("i64", 0, 64), v("l16", s, s + 1), NE)
+        const("P", v("zp", 400 * t + 384, 400 * t + 400))
+    ts(v("l16", 0, 2), v("s16", 0, 2), i15, ADD, i15, ADD)
+    ts(v("mwa", 0, 64), v("bw", 0, 64), v("l16", 0, 1), EQ, -1024.0, MUL)
+    ts(v("mwa", 64, 128), v("bw", 0, 64), v("l16", 1, 2), NE, -1024.0, MUL)
+    tt(v("mw", 0, 64), v("mwa", 0, 64), v("mwa", 64, 128), ADD)
+    ts(v("mwe", 0, 64), v("bw", 0, 64), i31, EQ, -1.0, MUL)
 
     elist = topo.engines(core, nxt)
     n = 1
@@ -461,7 +473,8 @@ def rank_program(g, core, T, topo):
 
     ridb, pidb, _b = topo.addr(prv)
     maskb = sum(1 << e for e in topo.engines(core, prv)[:half])
-    send([v("me", 0, 2)], half, lambda: g.remote_dma(T.nx[:], T.me[:], T.sem.rn, T.sem.loc, pidb, ridb, maskb), [("nx", (0, 128, 0, 2, 1))], "rn", 1.8)
+    pri[0] = OPT["tell"]
+    send([v("me", 0, 4)], half, lambda: g.remote_dma(T.nx[:], T.me[:], T.sem.rn, T.sem.loc, pidb, ridb, maskb), [("nx", (0, 128, 0, 4, 1))], "rn", 1.8)
 
     def bank(b, t, a=0, z=H, s=1):
         return v("pb%d" % (4 * b + t), a, z, s)
@@ -469,8 +482,8 @@ def rank_program(g, core, T, topo):
     def mine(r):
         return v("me", 0, 2) if r == 0 else v("lw", 2 * r - 2, 2 * r)
 
-    def theirs(r, a=0, z=2):
-        return v("nx", a, z) if r == 0 else v("lim", 4 * r - 4 + a, 4 * r - 4 + z)
+    def theirs(r):
+        return v("nx", 0, 2) if r == 0 else v("lim", 2 * r - 2, 2 * r)
 
     def unpack(r):
         lo = 0 if r < 0 else 32 + 32 * r
@@ -485,50 +498,43 @@ def rank_program(g, core, T, topo):
                 tt(v("tw", a + 256, a + 288), v("tw", a, a + 32), bank(b, k, 96, 128), SUB)
 
     def keys(r):
-        ts(v("key", 0, 2), mine(r), dead, EQ, more, MUL)
-        for s in range(2):
-            ts(v("key", 2 + s, 3 + s), theirs(r, s, s + 1), dead, EQ, v("key", s, s + 1), MUL)
-        ts(v("chg", 0, 2), v("key", 2, 4), 0.0, EQ, float(C), MUL)
+        tt(v("key", 0, 2), mine(r), theirs(r), MIN)
+        ts(v("chg", 0, 2), v("key", 0, 2), dead, NE, float(C), MUL)
 
-    def rows_out(r, early, a):
-        k, tk, tag = 4 * r + 2 * early, 2 * early, "%d%d" % (r, early)
-        line(v("got", a + 4, a + 6), v("got", a, a + 2), SAME, -1.0, col(12))
-        for s in range(2):
-            line(v("tk", tk + s, tk + s + 1), v("got", a + 2 + s, a + 3 + s), SIGN, -1.0, v("got", a + 4 + s, a + 5 + s))
-        for s in range(2):
-            line(v("lim", k + s, k + s + 1), v("tk", tk + s, tk + s + 1), SAME, v("key", 2 + s, 3 + s), theirs(r, s, s + 1))
-        sem, src, at = T.sem["rf" + tag], T.lim[:, k:k + 2], ("lw", (0, 128, 2 * r, 2 * r + 2, 1))
-        if r == ROUNDS - 1:
-            send([v("lim", k, k + 2)], n, lambda: g.remote_dma(T.lw[:, 2 * r:2 * r + 2], src, sem, T.sem.loc, pid, rid, full_mask), [at], "rf" + tag)
-            return
-        fd, where = T["fd" + tag], [("fd" + tag, (0, 128, 0, 2, 1))]
-        if early:
-            send([v("lim", k, k + 2)], n, lambda: g.remote_dma(fd[:], src, sem, T.sem.loc, pid, rid, full_mask), where, "rf" + tag)
-        else:
-            tr = [RemoteDMATransfer(dst_ids=[DstId(rid=rid, pnc=pid)], dma_engine_mask=halves[e], remote_sem=sem, src=src, dst=d) for e, d in enumerate((fd[:], T.lw[:, 2 * r:2 * r + 2]))]
-            send([v("lim", k, k + 2)], n, lambda: g.remote_dma_fused(tr, local_sem=T.sem.loc), where + [at], "rf" + tag)
+    def early(r):
+        own, far = (v("me", 2, 3), v("nx", 2, 3)) if r == 0 else (v("lwe", 0, 1), v("le0", 0, 1))
+        ts(v("key", 2, 3), own, far, MIN, v("me", 3, 4), EQ)
+        ts(v("mwe", 64, 128), v("mwe", 0, 64), v("key", 2, 3), MUL)
+        turn(v("stf", 0, 32), v("ste", 0, 32))
+        copy(v("oe", 0, 24), v("stf", 0, 24))
+        count(v("jnk", 0, C), ind(v("mwe", 64, 128), v("oe", 0, 24)), v("got", 0, 1))
+        le, fe, where = v("le%d" % r, 0, 1), T["fe%d" % r], [("fe%d" % r, (0, 128, 0, 1, 1))]
+        ts(le, v("got", 0, 1), -1.0, MAX, far, ADD)
+        send([le], n, lambda: g.remote_dma(fe[:], le[0], T.sem["re%d" % r], T.sem.loc, pid, rid, full_mask), where, "re%d" % r)
         for G in range(6):
-            if early:
-                dma("S", "dlr" + tag, row(G, 1280, 1408), (fd[0:64, :], where), 256, 1)
-            else:
-                dma("S", "dlr" + tag, row(G, LATE, TAB[4]), (fd[64:112, :], where), 192, 1)
-
-    def early(r, b):
-        turn(v("stt%d" % b, 0, 32, p=(0, 64)), v("stg%d" % b, 0, 32, p=(0, 64)))
-        if r < ROUNDS - 1:
-            copy(v("oe%d" % b, 0, 16), ind(v("stt%d" % b, 0, 32), v("cl", 0, 1)))
-            for s in range(2):
-                k = 2 * b + s
-                count(v("jnk", H * k, H * k + H), ind(v("mw", 64 * s, 64 * s + 64), v("oe%d" % b, 0, 12)), v("got", k, k + 1))
-            if b:
-                rows_out(r, 1, 0)
+            dma(OPT["rows"][G % 2], "der%d" % r, rows(G, 0, 4, SOON, SOON + 32), (fe[:], where), 256, 4)
+        if r == 0:
+            k = dma("S", "dme", v("lwe", 0, 1), (fe[:], where), 256, 128)
+            dma("S", "dv", v("vt", 0, 512), inp(T.v[:]), 131072, 128, (k,))
 
     def claims(r):
-        for s in range(2):
-            e = v("mm", 384 * s, 384 * s + 384, -1)
-            scan(v("pr", 384 * s, 384 * s + 384), e, e, MUL, ADD)
-            ts(v("clu", s, s + 1), v("pr", 384 * s + 383, 384 * s + 384), v("chg", s, s + 1), MAX)
-        rows_out(r, 0, 6)
+        e = v("mm", 0, C, -1)
+        scan(v("pr", 0, C), v("up", 0, C), e, -2048.0, ADD, MIN)
+        ts(v("clu", 0, 1), v("pr", C - 1, C), 2048.0, ADD, v("chg", 0, 1), MAX)
+        scan(v("pr", C, 2 * C), v("down", 0, C), e, 0.0, ADD, MAX)
+        ts(v("clu", 1, 2), v("pr", 2 * C - 1, 2 * C), -1.0, MUL, v("chg", 1, 2), MAX)
+        ts(v("tk", 2, 4), v("clu", 0, 2), float(C), LT, more, MUL)
+        lim = v("lim", 2 * r, 2 * r + 2)
+        tt(lim, v("tk", 2, 4), theirs(r), ADD)
+        sem, at = T.sem["rf%d" % r], ("lw", (0, 128, 2 * r, 2 * r + 2, 1))
+        if r == ROUNDS - 1:
+            send([lim], n, lambda: g.remote_dma(T.lw[:, 2 * r:2 * r + 2], lim[0], sem, T.sem.loc, pid, rid, full_mask), [at], "rf%d" % r)
+        else:
+            fd, where = T["fd%d" % r], [("fd%d" % r, (0, 128, 0, 2, 1))]
+            tr = [RemoteDMATransfer(dst_ids=[DstId(rid=rid, pnc=pid)], dma_engine_mask=halves[e], remote_sem=sem, src=lim[0], dst=d) for e, d in enumerate((fd[:], T.lw[:, 2 * r:2 * r + 2]))]
+            send([lim], n, lambda: g.remote_dma_fused(tr, local_sem=T.sem.loc), where + [at], "rf%d" % r)
+            for G in range(6):
+                dma("S", "dlr%d" % r, rows(G, 4, 7, LATE, LATE + 32), (fd[64:112, :], where), 192, 3)
         for t in range(4):
             act(v("ctl", t, 128, 4), ind(v("zp", 400 * t, 400 * t + 400), v("clu", 0, 2)))
         qc, qs, a = T["qcc%d" % r], T["qcs%d" % r], 128 + 32 * r
@@ -550,13 +556,13 @@ def rank_program(g, core, T, topo):
             mx(bank(b, k, 0, 128), *pair("qxc", "qxs", a + 96 * k, a + 96 * k + 128), *pair("qpc", "qps", 0, 128))
             ts(v("bits", 144 * b + 72 * k, 144 * b + 72 * k + 64), bank(b, k, 0, 64), 0.0, GT)
         ev = "ev%d" % b
-        scan(v(ev, 0, 144), v("horn", 0, 144), v("bits", 144 * b, 144 * b + 144), MUL, ADD)
+        scan(v(ev, 0, 144), v("horn", 0, 144), v("bits", 144 * b, 144 * b + 144), 0.0, MUL, ADD)
         for k in range(2):
             ts(v("of%d" % b, k, 16, 2), v(ev, 72 * k + 12, 72 * k + 72, 8), 32.0, MUL, v(ev, 72 * k + 4, 72 * k + 5), ADD)
 
     def level(r, b, h):
         a, m, res, trb, o = LO[h], 8 - h, "res%d" % b, "trb%d" % b, "of%d" % b
-        w = v("win", 0, 1536) if h == 0 else v("win", 480, TAB[h] + 1024)
+        w = v("win", TAB[h], (SOON if h < 4 else LATE) + 64)
         k = OPT["share"][h]
         if k:
             copy(v(res, a, a + 32 * k), ind(w, v(o, 16 * h, 16 * h + 2 * k)))
@@ -565,15 +571,19 @@ def rank_program(g, core, T, topo):
         z = a + 32 * m
 
         def stage(h, row, a):
-            dma("S", "dl%d%d%d" % (r, b, h // 4), v("stg%d" % b, 16 * (h % 2), 16 * (h % 2) + 16, p=(32 * (h // 2), 32 * (h // 2) + 12)), rows16(res, row, 96, a, a + 32), 384, 12)
-        stage(h, 1, z - 32)
+            dma("S", "dl%d%d" % (r, b), v("stg%d" % b, 16 * (h % 2), 16 * (h % 2) + 16, p=(32 * (h // 2), 32 * (h // 2) + 12)), rows16(res, row, 96, a, a + 32), 384, 12)
+        if h < 4 and r < ROUNDS - 1:
+            for G in range(2):
+                dma("S", "de%d" % r, v("ste", 16 * G, 16 * G + 16, p=(32 * h + 12 * b, 32 * h + 12 * b + 12)), rows16(res, 7, 96, z - 32, z), 384, 12)
+        stage(h, 7, z - 32)
         if h < 6:
             turn(v(trb, a, z), v(res, a, z))
             for G in range(2):
-                ts(v(o, 16 * h + 16 + G, 16 * h + 16 + 2 * (m - 1), 2), v(trb, a + 32 + 16 * G, z, 32), 32.0, MUL, v(trb, a + 16 * G, a + 16 * G + 1), ADD)
+                c = a + 16 * G + h
+                ts(v(o, 16 * h + 16 + G, 16 * h + 16 + 2 * (m - 1), 2), v(trb, c + 32, z, 32), 32.0, MUL, v(trb, c, c + 1), ADD)
         else:
-            tt(v(res, z, z + 32), v(res, a, a + 32), v(res, a + 32, z), SUB)
-            stage(7, 0, z)
+            tt(v(res, z, z + 32), v(res, a, a + 32), v(res, a + 32, z), ADD)
+            stage(7, 6, z)
 
     def state(r, b):
         for t in range(4):
@@ -582,11 +592,10 @@ def rank_program(g, core, T, topo):
                 act(v("fs%d" % b, H * t, H * t + H), bank(b, t))
 
     def diff(r, b):
-        turn(v("stt%d" % b, 0, 32, p=(64, 128)), v("stg%d" % b, 0, 32, p=(64, 128)))
+        turn(v("stt%d" % b, 0, 32), v("stg%d" % b, 0, 32))
         copy(v("ol%d" % b, 0, 16), ind(v("stt%d" % b, 0, 32), v("cl", 0, 1)))
         ol, zt = v("ol%d" % b, 0, 12), "zt%d" % b
-        for s in range(2):
-            count(v("mm", 384 * s + H * b, 384 * s + H * b + H), ind(v("mw", 64 * s, 64 * s + 64), ol), v("got", 6 + 2 * b + s, 7 + 2 * b + s))
+        act(v("mm", H * b, H * b + H), ind(v("mw", 0, 64), ol))
         for t in range(4):
             w = ind(v("tw", 256 * r + 64 * t, 256 * r + 64 * t + 64), ol)
             if t < OPT["nv"]:
@@ -618,10 +627,9 @@ def rank_program(g, core, T, topo):
         keys(r)
         for h in range(7):
             both(level, r, h)
-        mark = len(ops)
-        both(early, r)
-        for o in ops[mark:]:
-            o["pri"] += OPT["soon"]
+            if h == 3 and r < ROUNDS - 1:
+                pri[0] = OPT["soon"]
+                early(r)
         both(diff, r)
         pri[0] = OPT["claim"] + OPT["last"] * (r == ROUNDS - 1)
         claims(r)

@@ -2,40 +2,42 @@ import math
 from concourse.bass import DstId, RemoteDMATransfer
 from concourse.mybir import dt, AluOpType, AxisListType, ActivationFunctionType
 
-ROUNDS, C, H = 3, 384, 192
-OPT = dict(share=(3, 3, 2, 2, 1, 1, 0), nv=2, full="AAAA", eps=0.05, bias=1.0, claim=1.0, fills="AAP", more="AAAAA", tell=3.0, ahead="tx", rows="SS", soon=1.0, last=0.0,
-           turns=5, tries=300, amp=0.3, part=0.05, swaps=6000, heat=0.06, seed=1)
+ROUNDS, C, H, BIG = 3, 384, 192, 512.0
+AT = (0, H)
+OPT = dict(share=((4, 3, 3, 2, 2, 1, 2), (4, 3, 3, 2, 2, 1, 2)), ahead="s", calm=15, few="AAAAV", lead=0.0, ctl="AAAV", gap=0.5, look=0.05, nv=(2, 2, 2, 2, 2, 2), full="AAAAAAAV", fin="AAAAAAAV", eps=0.05, bias=(0.0, 0.25, 0.5, 0.75, 1.0, 1.5), claim=0.0, fills="AVA", more="PPPPP", tell=10.0, soon=1.0, last=0.5, diag=12.0,
+           turns=3, tries=40, amp=0.3, part=0.05, swaps=6000, starts=4, heat=0.08, seed=6)
 KIND = {"f": "float32", "b": "bfloat16", "i": "int32", "h": "uint16", "s": "uint8", "c": "float8_e4m3fn_x4", "e": "float16"}
-SPEC = """b xt 1792 ut 512 vt 512 trt 512 et 516 win 3200 tab 64 tat 64 res0 1152 res1 1152 trb0 1152 trb1 1152 bits 288 ev0 144 ev1 144 horn 144
-b stg0 32 stg1 32 stt0 32 stt1 32 gt0 768 gt1 768 fs0 768 fs1 768 zt0 768 zt1 768 zp 1600 mw 64 mwe 128 mm 384 lim 6 ctl 512 zero 1024 lw 6 tw 1024
-b bw 64 me 4 nx 4 clr 32 clt 32 jnk 384 ste 32 stf 32 le0 2 le1 2 lwe 2 up 384 down 384 mwa 128
+SPEC = """b xt 1792 ut 512 vt 512 trp 512 et 516 et1 516 win 3280 tab 64 tat 64 res0 1152 res1 1152 trb0 1152 trb1 1152 bits 320 ev0 160 ev1 160 horn 160
+b stg0 32 stg1 32 stt0 32 stt1 32 gt0 768 gt1 768 fs 1600 zt0 768 zt1 768 zp 1600 mw 192 mm 768 lim 8 ctl 512 zero 1128 lw 4 tw 768
+b bw 64 me 2 nx 2 clr 32 clt 32 jnk 768 up 384 down 384 mwb 128
 e pr 768
-c qxc 448 qfc 384 quc 128 qpc 128 qvc 128 wq 512 ec 512 qzc 384 qcc0 128 qcc1 128 qcc2 128 lc 224
-s qxs 448 qfs 384 qus 128 qps 128 qvs 128 wp 512 es 512 qzs 384 qcs0 128 qcs1 128 qcs2 128 ls 224
-i tia 32 tib 32 pidx 1 pint 4 flw 2 fle 1 flr 32 odd 64
-h ol0 16 ol1 16 oe 24 clu 2 of0 128 of1 128 cl 2 ul 8
-f rtt 128 yt 384 bpt 384 full 2 pf 4 s16 2 l16 2 col 24 tk 4 c32 8 got 2 key 4 chg 2 plc 32"""
+c qxc 448 qfc 384 quc 128 qpc 128 qvc 128 wq 512 ec 1024 qzc 384 qcc0 128 qcc1 128 qcc2 128 lc 224
+s qxs 448 qfs 384 qus 128 qps 128 qvs 128 wp 512 es 1024 qzs 384 qcs0 128 qcs1 128 qcs2 128 ls 224
+i tia 32 tib 32 pidx 1 pint 2 flw 2 flr 32
+h ol 28 oe 24 clu 4 of0 128 of1 128 cl 2 ul 8
+f rtt 128 rto 128 yt 384 bpt 384 full 4 pf 2 s16 2 l16 2 col 11 c32 8 got 4 key 2 far 4"""
 PSUM = tuple("pb%d" % k for k in range(8))
-SCRATCH = {"tdr": ("dram", [5, 32, 32], "bfloat16")}
-for _n in range(2):
-    SCRATCH["fd%d" % _n] = ("dram", [128, 2], "bfloat16")
-    SCRATCH["fe%d" % _n] = ("dram", [128, 1], "bfloat16")
+SCRATCH = {"tdr": ("dram", [5, 32, 32], "bfloat16"), "fin": ("dram", [128, 2], "float32")}
+TAGS = ("00", "01", "10", "11")
+for _n in TAGS:
+    SCRATCH["fe" + _n] = ("dram", [128, 2], "bfloat16")
 for _l in SPEC.split("\n"):
     _w = _l.split()
     for _k in range(1, len(_w), 2):
         SCRATCH[_w[_k]] = ("sbuf", [128, int(_w[_k + 1])], KIND[_w[0]])
 for _n in PSUM:
     SCRATCH[_n] = ("psum", [128, 512], "float32")
-DMAS = "dx0 dx1 du dta dtb dtr dw dfl dfr dv dw0 dt0 dt1 dw2 dw4 dlr0 dlr1 der0 der1 dme de0 de1 dout".split()
-DMAS += ["dl%d%d" % (_k // 2, _k % 2) for _k in range(6)]
-SEMAPHORES = "cv ca ct_ cp loc rn rf0 rf1 rf2 re0 re1 rc0 rc1 rc2 rs0 rs1 rs2".split() + DMAS
+DMAS = "dx0 dx1 du dta dtb dtc dtr dw dfl dfr dv dw0 dt0 dt1 dw2 dw4 dout".split()
+DMAS += ["dl%d%d%d" % (_k // 4, _k // 2 % 2, _k % 2) for _k in range(12)] + ["der" + _n for _n in TAGS]
+SEMAPHORES = "cv ca ct_ cp loc rn rf rc0 rc1 rc2 rs0 rs1 rs2".split() + ["re" + _n for _n in TAGS] + DMAS
 
 ADD, SUB, MUL, MAX, MIN = AluOpType.add, AluOpType.subtract, AluOpType.mult, AluOpType.max, AluOpType.min
 EQ, NE, GT, GE, LT = AluOpType.is_equal, AluOpType.not_equal, AluOpType.is_gt, AluOpType.is_ge, AluOpType.is_lt
 AND, SHR = AluOpType.bitwise_and, AluOpType.arith_shift_right
-COPY, SAME, SIGN = ActivationFunctionType.Copy, ActivationFunctionType.Identity, ActivationFunctionType.Sign
+COPY, SAME, RELU = ActivationFunctionType.Copy, ActivationFunctionType.Identity, ActivationFunctionType.Relu
 ORDER = []
-PACE = ((0.88e-3, 0.2, 0.8, 1.7, 0.03, 1.56), (0.85e-3, 0.2, 1.2, 2.8, 0.04, 1.3), (1.15e-3, 0.2, 1.0, 2.0, 0.03, 1.9))
+PACE = ((0.85e-3, 0.2, 0.7, 1.55, 0.03, 1.56, 0.06, 1.3), (0.9e-3, 0.19, 0.9, 2.1, 0.035, 1.3, 0.12, 1.1), (1.1e-3, 0.22, 1.0, 2.8, 0.025, 1.9, 0.07, 1.3),
+        (0.83e-3, 0.22, 0.65, 1.4, 0.02, 1.2, 0.05, 1.7))
 
 
 def hit(a, b):
@@ -74,9 +76,11 @@ def arrange(ops):
             users[d].append(k)
     qs = [o["q"] for o in ops]
     deps = [sorted(d) for d in deps]
+    soft = [set(o["after"]) if o["kind"] == "d" and o["size"] < 20000 else set() for o in ops]
+    hard = [[d for d in deps[k] if d not in soft[k]] for k in range(n)]
 
     def costs(p):
-        hold = [o["hold"] + max(o["cyc"] + p[5] * o["got"], 64) * p[0] * (o["kind"] == "c") for o in ops]
+        hold = [p[6] if o["kind"] == "d" else o["hold"] + max(o["cyc"] * (p[7] if o["q"] == "T" else 1.0) + p[5] * o["got"], 64) * p[0] * (o["kind"] == "c") for o in ops]
         late = [{"d": p[2], "a": p[3]}.get(o["kind"], 0.0) + p[1] for o in ops]
         move = [(p[4] * o["rows"] + 5e-5 * o["size"]) / 16 for o in ops]
         return hold, late, move
@@ -84,7 +88,7 @@ def arrange(ops):
     hold, late, move = cost[0]
     way = [0.0] * n
     for k in range(n - 1, -1, -1):
-        way[k] = hold[k] + late[k] + move[k] + max([way[u] for u in users[k]] + [0.0])
+        way[k] = hold[k] + move[k] + max([way[u] + late[k] * (k not in soft[u]) for u in users[k]] + [late[k] + ops[k].get("tail", 0.0)])
 
     def place(rank):
         left = [len(d) for d in deps]
@@ -96,29 +100,45 @@ def arrange(ops):
         while len(order) < n:
             t, q = min((max(min(at[k] for k in ks), free[q]), q) for q, ks in ready.items() if ks)
             k = max([k for k in ready[q] if at[k] <= t + OPT["eps"]], key=lambda k: (rank[k], -k))
+            urgent = [j for j in ready[q] if rank[j] > rank[k] + OPT["gap"] and at[j] + OPT["look"] < t + hold[k]]
+            if urgent:
+                j = min(urgent, key=lambda j: at[j])
+                fit = [i for i in ready[q] if max(t, at[i]) + hold[i] <= at[j] + OPT["look"]]
+                k = max(fit, key=lambda i: (rank[i], -i)) if fit else j
             done = free[q] = max(t, at[k]) + hold[k]
             if move[k]:
                 done = rings = max(rings, done) + move[k]
             ready[q].remove(k)
             order.append(k)
             for u in users[k]:
-                at[u] = max(at[u], done + late[k])
+                at[u] = max(at[u], free[q] if k in soft[u] else done + late[k])
                 left[u] -= 1
                 if not left[u]:
                     ready.setdefault(qs[u], []).append(u)
         return order
 
-    def span(order):
-        total = 0.0
-        for hold, late, move in cost:
-            end, free, rings = [0.0] * n, {q: 0.0 for q in qs}, 0.0
-            for k in order:
-                done = free[qs[k]] = max([free[qs[k]]] + [end[d] for d in deps[k]]) + hold[k]
-                if move[k]:
-                    done = rings = max(rings, done) + move[k]
-                end[k] = done + late[k]
-            total += max(end)
-        return total / len(cost)
+    def span(order, first=0, held=None, limit=1e9):
+        total, seen, first = 0.0, [], first // 32
+        for m, (hold, late, move) in enumerate(cost):
+            end, marks = (list(held[m][0]), held[m][1][:first + 1]) if held else ([0.0] * n, [dict.fromkeys(qs + ["rings"], 0.0)])
+            free = dict(marks[-1])
+            for a in range(32 * first, n, 32):
+                rings = free["rings"]
+                for k in order[a:a + 32]:
+                    q = qs[k]
+                    t = free[q]
+                    for d in hard[k]:
+                        if end[d] > t:
+                            t = end[d]
+                    t = free[q] = t + hold[k]
+                    if move[k]:
+                        t = rings = (rings if rings > t else t) + move[k]
+                    end[k] = t + late[k]
+                free["rings"] = rings
+                marks.append(dict(free))
+            total += max(end) / len(cost)
+            seen.append((end, marks))
+        return total, seen if total <= limit else None
 
     def back(order):
         left = [len(u) for u in users]
@@ -137,7 +157,7 @@ def arrange(ops):
             out[k] = free[q] = max(t, at[k]) + hold[k]
             ready[q].remove(k)
             for d in deps[k]:
-                at[d] = max(at[d], out[k] + late[d] + move[d])
+                at[d] = max(at[d], out[k] + late[d] * (d not in soft[k]) + move[d])
                 left[d] -= 1
                 if not left[d]:
                     ready.setdefault(qs[d], []).append(d)
@@ -148,7 +168,7 @@ def arrange(ops):
         end, free, rings, last, why, ring = [0.0] * n, {q: 0.0 for q in qs}, 0.0, {}, [None] * n, None
         for k in order:
             t, w = free[qs[k]], (last.get(qs[k]), True)
-            for d in deps[k]:
+            for d in hard[k]:
                 if end[d] >= t:
                     t, w = end[d], (d, False)
             done = free[qs[k]] = t + hold[k]
@@ -164,16 +184,15 @@ def arrange(ops):
                 out.append((why[k][0], k))
             k = why[k][0]
         return out
-    rank = [way[k] + ops[k]["pri"] for k in range(n)]
-    order = place(rank)
-    best, x = span(order), OPT["seed"]
-    o = order
-    for _ in range(OPT["turns"]):
-        other = back(o)
-        o = place(other)
-        t = span(o)
-        if t <= best:
-            best, rank, order = t, other, o
+    best, x = 1e9, OPT["seed"]
+    for bias in OPT["bias"]:
+        other = [way[k] + ops[k]["pri"] + bias * ops[k].get("first", 0) for k in range(n)]
+        for _ in range(OPT["turns"] + 1):
+            o = place(other)
+            t = span(o)[0]
+            if t <= best:
+                best, rank, order = t, other, o
+            other = back(o)
     for _ in range(OPT["tries"]):
         other = list(rank)
         for k in range(n):
@@ -182,11 +201,16 @@ def arrange(ops):
                 x = (x * 1103515245 + 12345) % 2147483648
                 other[k] += OPT["amp"] * (x / 1073741824 - 1.0)
         o = place(other)
-        t = span(o)
+        t = span(o)[0]
         if t <= best:
             best, rank, order = t, other, o
-    now, t0, pairs = order, best, []
-    for step in range(OPT["swaps"]):
+    now, t0, pairs, held = order, best, [], span(order)[1]
+    first, steps = (order, best), OPT["swaps"]
+    for step in range(steps * (OPT["starts"] + 2)):
+        if step % steps == 0 and step <= steps * OPT["starts"]:
+            now, t0 = first if step < steps * OPT["starts"] else (order, best)
+            pairs, held = [], span(now)[1]
+        cool = 1 - step % steps / steps if step < steps * OPT["starts"] else (1 - (step / steps - OPT["starts"]) / 2) / 2
         if not pairs:
             pairs = chain(now, cost[step % len(cost)])
         x = (x * 1103515245 + 12345) % 2147483648
@@ -210,10 +234,10 @@ def arrange(ops):
                 continue
             new = [k for k in mid if k not in take] + [k for k in mid if k in take]
         o = now[:i] + new + now[j + 1:]
-        t = span(o)
         x = (x * 1103515245 + 12345) % 2147483648
-        if t <= t0 + OPT["heat"] * (1 - step / OPT["swaps"]) * x / 2147483648:
-            now, t0, pairs = o, t, []
+        t, seen = span(o, i, held, t0 + OPT["heat"] * cool * x / 2147483648)
+        if seen:
+            now, t0, pairs, held = o, t, [], seen
             if t < best:
                 best, order = t, o
     OPT["span"] = best
@@ -248,7 +272,7 @@ def rank_program(g, core, T, topo):
     def v(name, a, b, s=1, p=(0, 128)):
         t, q = T[name], slice(*p)
         if s < 0:
-            return (t[q, slice(b - 1, a - 1 if a else None, -1)], [(name, (p[0], p[1], a, b, 1))], b - a, name)
+            return (t[q, slice(b - 1, a - 1 if a else None, s)], [(name, (p[0], p[1], a, b, 1))], len(range(a, b, -s)), name)
         return (t[q, a:b:s] if s != 1 else t[q, a:b], [(name, (p[0], p[1], a, b, s))], len(range(a, b, s)), name)
 
     def rows16(name, first, last, a, b):
@@ -273,17 +297,18 @@ def rank_program(g, core, T, topo):
         run("V", lambda: g.vector.tensor_copy(out[0], in_[0]), [out], [in_], *price(out, in_))
 
     def act(out, in_, scale=1.0):
-        run("A", lambda: g.scalar.activation(out[0], in_[0], COPY, scale=scale) if scale != 1.0 else g.scalar.activation(out[0], in_[0], COPY), [out], [in_],
-            *((in_[2], 0) if in_[3] else (78, in_[2])))
+        if isinstance(scale, tuple):
+            run("A", lambda: g.scalar.activation(out[0], in_[0], SAME, scale=scale[0]), [out], [in_, scale], in_[2])
+        else:
+            run("A", lambda: g.scalar.activation(out[0], in_[0], COPY, scale=scale) if scale != 1.0 else g.scalar.activation(out[0], in_[0], COPY), [out], [in_],
+                *((in_[2], 0) if in_[3] else (78, in_[2])))
 
     def count(out, in_, total):
         run("A", lambda: g.scalar.activation(out[0], in_[0], COPY, accum_out=total[0]), [out, total], [in_], 100, in_[2])
 
-    def sign(out, in_):
-        run("A", lambda: g.scalar.activation(out[0], in_[0], SIGN), [out], [in_], in_[2])
-
-    def line(out, in_, scale, bias):
-        run("A", lambda: g.scalar.activation(out[0], in_[0], SAME, bias=bias[0], scale=scale[0]), [out], [in_, scale, bias], in_[2])
+    def line(out, in_, scale, bias, func=SAME):
+        x, y = [e[0] if isinstance(e, tuple) else e for e in (scale, bias)]
+        run("A", lambda: g.scalar.activation(out[0], in_[0], func, bias=y, scale=x), [out], [in_] + [e for e in (scale, bias) if isinstance(e, tuple)], in_[2])
 
     def scaled(q, out, in_, scale):
         if q == "A":
@@ -305,7 +330,8 @@ def rank_program(g, core, T, topo):
             run("V", lambda: g.vector.tensor_scalar(out[0], a[0], x1, x2, op0, op1), [out], ins, *price(out, a))
 
     def scan(out, a, b, first, op0, op1):
-        run("V", lambda: g.vector.tensor_tensor_scan(out[0], a[0], b[0], first, op0, op1), [out], [a, b], *price(out, a))
+        more = [first] if isinstance(first, tuple) else []
+        run("V", lambda: g.vector.tensor_tensor_scan(out[0], a[0], b[0], first[0] if more else first, op0, op1), [out], [a, b] + more, *price(out, a))
 
     def fill(out, c):
         run("V", lambda: g.vector.memset(out[0], c), [out], [], *price(out, out))
@@ -313,8 +339,8 @@ def rank_program(g, core, T, topo):
     def quant(c, s, in_):
         run("V", lambda: g.vector.quantize_mx(c[0], s[0], in_[0]), [c, s], [in_], 15 + 0.265 * in_[2])
 
-    def mx(out, lc, ls, rc, rs):
-        run("T", lambda: g.tensor.matmul_mx(out[0], lc[0], ls[0], rc[0], rs[0], True, True), [out], [lc, ls, rc, rs], 1.3 * (rc[2] + 16))
+    def mx(out, lc, ls, rc, rs, start=True, stop=True):
+        run("T", lambda: g.tensor.matmul_mx(out[0], lc[0], ls[0], rc[0], rs[0], start, stop), [out], [lc, ls, rc, rs], rc[2] + 16)
 
     def pair(c, s, a, b):
         return v(c, a, b), v(s, a, b)
@@ -340,122 +366,127 @@ def rank_program(g, core, T, topo):
     def col(k, n=1):
         return v("col", k, k + n)
 
-    iota(v("flr", 0, 32), [[-1, 16], [-16, 2]], 32)
+    iota(v("flr", 0, 32), [[1, 32]], 0)
     pri[0] = 9.0
-    dma("S", "dta", v("tia", 0, 32), inp(T.ti[0:4, :]), 16384, 128)
+    dma("S", "dta", v("tia", 0, 32, p=(0, 64)), inp(T.ti[0:2, :]), 8192, 64)
     pri[0] = 0.0
     dma("S", "du", v("ut", 0, 512), inp(T.u[:]), 131072, 128)
-    dma("S", "dx0", v("xt", 0, 768), inp(T.x[:, 0:768]), 196608, 128)
+    for b in range(2):
+        dma("S", "dx%d" % b, v("xt", 896 * b, 896 * b + 768), inp(T.x[:, 4 * AT[b]:4 * AT[b] + 768]), 196608, 128)
     for G in range(6):
         dma("S", "dfr", v("flr", 0, 32, p=(16 * G, 16 * G + 7)), inp(T.fl[0:7, :]), 896, 7)
 
-    def loads(names, after):
+    def later(names, after):
         for c in names:
-            if c == "t":
+            if c == "s":
+                dma("S", "dtc", v("tia", 0, 32, p=(64, 128)), inp(T.ti[2:4, :]), 8192, 64, after)
+            elif c == "t":
                 dma("S", "dtb", v("tib", 0, 32, p=(0, 96)), inp(T.ti[4:7, :]), 12288, 96, after)
-            elif c == "x":
-                dma("S", "dx1", v("xt", 896, 1664), inp(T.x[:, 768:1536]), 196608, 128, after)
             else:
                 dma("S", "dfl", v("flw", 0, 2), inp(T.fl[:]), 1024, 128, after)
-                dma("S", "dfl", v("fle", 0, 1), inp(T.fl[0:4, :]), 512, 128, after)
-    loads(OPT["ahead"], ())
+    later(OPT["ahead"], ())
 
-    if "A" in OPT["fills"]:
-        fill(v("zero", 0, 1024), 0.0)
-    else:
-        fill(v("zero", 0, 64), 0.0)
+    fill(v("zero", 0, 1128), 0.0)
     iota(v("pidx", 0, 1), [[0, 1]], 0, 1)
     iota(v("s16", 0, 2), [[1, 2]], 0)
-    iota(v("bw", 0, 32), [[1, 2], [2, 16]], 0)
-    fill(v("bw", 32, 64), -1.0)
-    fill(v("clr", 0, 32), 0.0)
+    iota(v("bw", 0, 32), [[1, 32]], 0)
+    const(OPT["few"][2], v("bw", 32, 64), -1)
+    const(OPT["few"][2], v("clr", 0, 32))
     iota(v("clr", 0, 12), [[1, 2], [2, 6]], 0)
     iota(v("clr", 16, 28), [[2, 2], [4, 3], [1, 2]], 0)
     copy(v("clr", 16, 28, p=(96, 128)), v("clr", 0, 12, p=(96, 128)))
     turn(v("clt", 0, 32), v("clr", 0, 32))
     copy(v("cl", 0, 1), v("clt", 0, 1))
-    for k, (c, op) in enumerate(((15, AND), (4, SHR), (5, SHR), (31, AND))):
-        ts(v("pint", k, k + 1), v("pidx", 0, 1), c, op)
-    copy(v("pf", 0, 4), v("pint", 0, 4))
-    i15, i31, lev = v("pf", 0, 1), v("pf", 3, 4), v("pf", 0, 3)
-    ts(col(8, 3), lev, 1.0, GE, 32.0, MUL)
-    ts(col(12, 3), lev, 3.0, GE, -32.0, MUL)
-    ts(col(16, 3), lev, 6.0, LT, 32.0, ADD)
-    tt(col(20, 3), col(8, 3), col(12, 3), ADD)
-    tt(col(0, 3), col(20, 3), col(16, 3), ADD)
-    ts(col(8, 3), lev, 6.0, NE, 31.0, MUL)
-    ts(col(4, 3), col(8, 3), -32.0, ADD)
-    dead, more = col(1), col(5)
-    ts(col(3), i15, 8.0, GE, 8.0, MUL)
-    iota(v("c32", 0, 8), [[0, 2], [32, 4]], 0)
-    ts(v("ul", 0, 8), v("c32", 0, 8), i15, ADD, col(3), ADD)
-    fill(v("horn", 0, 144), 2.0)
-    fill(v("horn", 0, 144, 8), 0.0)
-    fill(v("bits", 0, 288), 0.0)
-    fill(v("bits", 68, 288, 72), 32.0)
+    ts(v("pint", 0, 1), v("pidx", 0, 1), 15, AND)
+    ts(v("pint", 1, 2), v("pidx", 0, 1), 4, SHR)
+    copy(v("pf", 0, 2), v("pint", 0, 2))
+    i15 = v("pf", 0, 1)
+    ts(col(2, 2), v("pf", 0, 2), 6.0, GE, 31.0, MUL)
+    line(col(0, 2), col(2, 2), 1.0, 1.0)
+    dead = col(1)
+    ts(col(4), i15, 7.0, LT)
+    act(col(5), col(0), col(4))
+    line(col(6), col(4), -1.0, 1.0)
+    line(col(7), col(5), -1.0, col(6))
+    line(col(8), dead, -2.0 * BIG, BIG)
+    ts(col(9), i15, 8.0, GE, -24.0, MUL)
+    ts(col(10), i15, 8.0, GE, -27.0, MUL)
+    iota(v("c32", 0, 8), [[0, 2], [-32, 4]], 112)
+    ts(v("ul", 0, 8), v("c32", 0, 8), i15, ADD, col(9), ADD)
+    ts(v("ul", 3, 8, 4), v("c32", 3, 8, 4), i15, ADD, col(10), ADD)
+    q = OPT["few"]
+    const(q[0], v("horn", 0, 160), 2)
+    const(q[0], v("horn", 0, 160, 8))
+    const(q[0], v("horn", 4, 160, 80))
+    const(q[0], v("horn", 67, 160, 80))
+    const(q[0], v("horn", 72, 160, 80), 1)
+    const(q[1], v("bits", 0, 320), 66)
+    const(q[1], v("bits", 4, 320, 80), -2)
     for b in range(2):
         const("P", v("xt", 896 * b + 768, 896 * b + 896))
-        fill(v("stg%d" % b, 0, 32), 0.0)
-    fill(v("ste", 0, 32), 0.0)
-    TAB = (1024, 1024, 0, 0, 2112, 2112, 2112)
-    SOON, LATE = 2048, 3136
+        const(q[2], v("stg%d" % b, 0, 32))
+        const(q[2], v("stt%d" % b, 0, 32))
+    WIN = [(32, 1122)] * 2 + [(0, 2146)] * 2 + [(2176, 3266)] * 3
+    SOON, LATE = 34, 2178
 
-    def rows(G, h, k, a, z):
-        return v("win", a, z, p=(16 * G + h, 16 * G + k))
-    for q, a in zip(OPT["fills"], (1024, 0, 2112)):
-        const(q, v("win", a, a + 1024))
+    def rows(G, h, k, a, n):
+        return v("win", a, a + n, p=(16 * G + h, 16 * G + k))
+    for q, (a, z) in zip(OPT["fills"], ((0, 1128), (1128, 2176), (2176, 3280))):
+        const(q, v("win", a, z))
     for a in (SOON, LATE):
-        ts(v("win", a, a + 32), v("flr", 0, 32), col(4), MUL, col(0), ADD)
-        ts(v("win", a + 32, a + 64), v("zero", 0, 32), col(0), ADD)
-    copy(v("tab", 0, 32), v("tia", 0, 32))
-    turn(v("tat", 0, 32), v("tab", 0, 32))
+        line(v("win", a + 32, a + 64), v("zero", 0, 32), 1.0, col(0))
+        ops[-1]["outs"] = v("win", a + 30, a + 70)[1]
+        ts(v("win", a, a + 32), v("flr", 0, 32), col(7), MUL, col(5), ADD)
+
+    def tables(name, a, p, k):
+        for q, c in zip(p, k):
+            ts(v("tab", a, a + 32, p=q), v(name, 0, 32, p=q), c, ADD)
+        q = (p[0][0], p[-1][1])
+        turn(v("tat", a, a + 32, p=q), v("tab", a, a + 32, p=q))
 
     def staged(a, b):
         return (T.tdr[a:b, :, :], [("tdr", (a, b, 0, 1, 1))])
+    tables("tia", 0, ((0, 32), (32, 64)), (2.0, 34.0))
     for G in range(6):
-        k = dma(OPT["rows"][G % 2], "dw0", rows(G, 0, 2, 1024, 2048), v("tat", 0, 32, p=(0, 64)), 4096, 64)
+        k = dma("S", "dw0", rows(G, 0, 2, 98, 1024), v("tat", 0, 32, p=(0, 64)), 4096, 64)
+    later([c for c in "stf" if c not in OPT["ahead"]], (k,))
+    tables("tia", 0, ((64, 96), (96, 128)), (34.0, 2.0))
     dma("S", "dt0", staged(0, 2), v("tat", 0, 32, p=(64, 128)), 4096, 64)
-    loads([c for c in "txf" if c not in OPT["ahead"]], (k,))
-    copy(v("tab", 32, 64, p=(0, 64)), v("tib", 0, 32, p=(0, 64)))
-    p6 = (64, 96)
-    ts(v("odd", 0, 32, p=p6), v("tib", 0, 32, p=p6), 1, AND)
-    ts(v("odd", 32, 64, p=p6), v("tib", 0, 32, p=p6), 1, SHR)
-    ts(v("plc", 0, 32, p=p6), v("odd", 0, 32, p=p6), 16.0, MUL)
-    tt(v("tab", 32, 64, p=p6), v("plc", 0, 32, p=p6), v("odd", 32, 64, p=p6), ADD)
-    turn(v("tat", 32, 64, p=(0, 96)), v("tab", 32, 64, p=(0, 96)))
+    tables("tib", 32, ((0, 64), (64, 96)), (2.0, 0.0))
     dma("S", "dt1", staged(2, 5), v("tat", 32, 64, p=(0, 96)), 6144, 96)
     for G in range(6):
-        dma("S", "dw2", rows(G, 2, 4, 0, 1024), staged(0, 2), 4096)
+        dma("S", "dw2", rows(G, 2, 4, 1122, 1024), staged(0, 2), 4096)
     for G in range(6):
-        k = dma("S", "dw4", rows(G, 4, 7, 2112, 3136), staged(2, 5), 6144)
-    dma("S", "dtr", v("trt", 0, 128), inp(T.tr[:]), 32768, 128, (k,))
+        k = dma("S", "dw4", rows(G, 4, 7, LATE + 64, 1024), staged(2, 5), 6144)
+    dma("S", "dtr", v("trp", 384, 512), inp(T.tr[:]), 32768, 128, (k,))
     for a in (0, 256):
         dma("S", "dw", codes("wq", a, a + 256), inp(T.wc[:, 4 * a:4 * a + 1024]), 131072, 128, (k,))
     dma("S", "dw", v("wp", 0, 512), inp(T.ws[:]), 65536, 128, (k,))
-    ts(v("me", 0, 2), v("flw", 0, 2), more, MUL, dead, ADD)
-    ts(v("me", 2, 3), v("fle", 0, 1), -1.0, MUL, col(2), ADD)
-    copy(v("me", 3, 4), col(2))
+    pri[0] = OPT["tell"]
+    ts(v("me", 0, 2), v("flw", 0, 2), 0.0, EQ, dead, MUL)
+    pri[0] = 0.0
     quant(*pair("quc", "qus", 0, 128), v("ut", 0, 512))
     ul = v("ul", 0, 8)
     run("V", lambda: g.vector.tensor_copy(T.qpc[:, 0:128].bitcast(dt.uint32), T.quc[:, 0:128].bitcast(dt.uint32).indirect(ul[0])), [v("qpc", 0, 128)], [v("quc", 0, 128), ul], 60, 128)
     act(v("qps", 0, 128), ind(v("qus", 0, 128), ul))
-    fill(v("et", 0, 516), 2.0 ** -6)
+    pri[0] = OPT["diag"]
+    const(OPT["few"][4], v("et", 0, 516), 2.0 ** -6)
     run("P", lambda: g.affine_select(T.et[:], T.et[:], [[1, 516]], EQ, 0.0, -3, -4), [v("et", 0, 516)], [v("et", 0, 516)], 200 + 2 * 516)
     for b in range(4):
         quant(*pair("ec", "es", 128 * b, 128 * b + 128), v("et", 3 - b, 515 - b))
-    const(OPT["more"][0], v("trt", 128, 512))
-    quant(*pair("lc", "ls", 0, 128), v("trt", 0, 512))
+    pri[0] = 0.0
+    const(OPT["more"][0], v("trp", 0, 384))
+    quant(*pair("lc", "ls", 0, 128), v("trp", 0, 512))
     const(OPT["more"][1], v("ctl", 128, 512))
     const(OPT["more"][2], v("tw", 0, 768))
     const(OPT["more"][3], v("up", 0, 384), 1)
     const(OPT["more"][4], v("down", 0, 384), -1)
     for t in range(4):
         const("P", v("zp", 400 * t + 384, 400 * t + 400))
+        const("P", v("fs", 400 * t + 384, 400 * t + 400))
     ts(v("l16", 0, 2), v("s16", 0, 2), i15, ADD, i15, ADD)
-    ts(v("mwa", 0, 64), v("bw", 0, 64), v("l16", 0, 1), EQ, -1024.0, MUL)
-    ts(v("mwa", 64, 128), v("bw", 0, 64), v("l16", 1, 2), NE, -1024.0, MUL)
-    tt(v("mw", 0, 64), v("mwa", 0, 64), v("mwa", 64, 128), ADD)
-    ts(v("mwe", 0, 64), v("bw", 0, 64), i31, EQ, -1.0, MUL)
+    for s in range(2):
+        ts(v("mwb", 64 * s, 64 * s + 64), v("bw", 0, 64), v("l16", s, s + 1), EQ, -1.0, MUL)
 
     elist = topo.engines(core, nxt)
     n = 1
@@ -474,69 +505,77 @@ def rank_program(g, core, T, topo):
     ridb, pidb, _b = topo.addr(prv)
     maskb = sum(1 << e for e in topo.engines(core, prv)[:half])
     pri[0] = OPT["tell"]
-    send([v("me", 0, 4)], half, lambda: g.remote_dma(T.nx[:], T.me[:], T.sem.rn, T.sem.loc, pidb, ridb, maskb), [("nx", (0, 128, 0, 4, 1))], "rn", 1.8)
+    send([v("me", 0, 2)], half, lambda: g.remote_dma(T.nx[:], T.me[:], T.sem.rn, T.sem.loc, pidb, ridb, maskb), [("nx", (0, 128, 0, 2, 1))], "rn", 1.8)
 
     def bank(b, t, a=0, z=H, s=1):
         return v("pb%d" % (4 * b + t), a, z, s)
 
-    def mine(r):
-        return v("me", 0, 2) if r == 0 else v("lw", 2 * r - 2, 2 * r)
-
     def theirs(r):
-        return v("nx", 0, 2) if r == 0 else v("lim", 2 * r - 2, 2 * r)
+        return v("nx", 0, 2) if r == 0 else v("lim", 4 * r - 2, 4 * r)
 
     def unpack(r):
-        lo = 0 if r < 0 else 32 + 32 * r
         for t in range(4):
-            b, k = t % 2, 2 + t // 2
-            mx(bank(b, k, 0, 128), *pair("ec", "es", 128 * t, 128 * t + 128), *pair("lc", "ls", lo, lo + 128))
-            if r < 0:
-                for s in range(2):
-                    act(v("tw", 64 * t + 16 * s, 64 * t + 16 * s + 16), bank(b, k, s, 32, 2), -1.0)
-            else:
-                a = 256 * r + 64 * t
-                tt(v("tw", a + 256, a + 288), v("tw", a, a + 32), bank(b, k, 96, 128), SUB)
+            b, k = t % 2, t // 2
+            for j in range(r + 2):
+                mx(bank(b, k, 0, 128), *pair("ec", "es", 128 * t, 128 * t + 128), *pair("lc", "ls", 32 * j, 32 * j + 128), j == 0, j == r + 1)
+            a = 256 * r + 256 + 64 * t
+            act(v("tw", a, a + 32), bank(b, k, 96, 128), -1.0)
 
     def keys(r):
-        tt(v("key", 0, 2), mine(r), theirs(r), MIN)
-        ts(v("chg", 0, 2), v("key", 0, 2), dead, NE, float(C), MUL)
+        line(v("far", 0, 2), theirs(r), BIG, col(8))
+        for s in range(2):
+            a = 2 * r - 2 + s
+            line(v("key", s, s + 1), v("me", s, s + 1) if r == 0 else v("lw", a, a + 1), BIG, v("far", s, s + 1), RELU)
+            line(v("mw", 64 * s, 64 * s + 64), v("mwb", 64 * s, 64 * s + 64), v("key", s, s + 1), BIG)
+        if r < ROUNDS - 1:
+            line(v("far", 2, 4), theirs(r), 1.0, -C * BIG)
+        else:
+            line(v("full", 2, 4), theirs(r), -1.0, 1.0, RELU)
+            tt(v("mw", 128, 192), v("mw", 0, 64), v("mw", 64, 128), SUB)
 
-    def early(r):
-        own, far = (v("me", 2, 3), v("nx", 2, 3)) if r == 0 else (v("lwe", 0, 1), v("le0", 0, 1))
-        ts(v("key", 2, 3), own, far, MIN, v("me", 3, 4), EQ)
-        ts(v("mwe", 64, 128), v("mwe", 0, 64), v("key", 2, 3), MUL)
-        turn(v("stf", 0, 32), v("ste", 0, 32))
-        copy(v("oe", 0, 24), v("stf", 0, 24))
-        count(v("jnk", 0, C), ind(v("mwe", 64, 128), v("oe", 0, 24)), v("got", 0, 1))
-        le, fe, where = v("le%d" % r, 0, 1), T["fe%d" % r], [("fe%d" % r, (0, 128, 0, 1, 1))]
-        ts(le, v("got", 0, 1), -1.0, MAX, far, ADD)
-        send([le], n, lambda: g.remote_dma(fe[:], le[0], T.sem["re%d" % r], T.sem.loc, pid, rid, full_mask), where, "re%d" % r)
+    def tell(r, e):
+        tag, k = "%d%d" % (r, e), 4 * r + 2 * e
+        for s in range(2):
+            got = v("got", 2 * e + s, 2 * e + s + 1)
+            count(v(("jnk", "mm")[e], C * s, C * s + C), ind(v("mw", 64 * s, 64 * s + 64), v(("oe", "ol")[e], 0, 24)), got)
+            ts(v("lim", k + s, k + s + 1), got, v("far", 2 + s, 3 + s), ADD, 0.0, MAX)
+        lim, fe, where, sem = v("lim", k, k + 2), T["fe" + tag], [("fe" + tag, (0, 128, 0, 2, 1))], T.sem["re" + tag]
+        if e:
+            tr = [RemoteDMATransfer(dst_ids=[DstId(rid=rid, pnc=pid)], dma_engine_mask=halves[j], remote_sem=sem, src=lim[0], dst=d) for j, d in enumerate((fe[:], T.lw[:, 2 * r:2 * r + 2]))]
+            send([lim], n, lambda: g.remote_dma_fused(tr, local_sem=T.sem.loc), where + [("lw", (0, 128, 2 * r, 2 * r + 2, 1))], "re" + tag)
+        else:
+            send([lim], n, lambda: g.remote_dma(fe[:], lim[0], sem, T.sem.loc, pid, rid, full_mask), where, "re" + tag)
         for G in range(6):
-            dma(OPT["rows"][G % 2], "der%d" % r, rows(G, 0, 4, SOON, SOON + 32), (fe[:], where), 256, 4)
-        if r == 0:
-            k = dma("S", "dme", v("lwe", 0, 1), (fe[:], where), 256, 128)
+            k = dma("S", "der" + tag, rows(G, 4 * e, 4 + 3 * e, (SOON, LATE)[e], 32), (fe[64 * e:64 + 48 * e, :], where), 256, 4)
+        if r == 0 and e == 0:
             dma("S", "dv", v("vt", 0, 512), inp(T.v[:]), 131072, 128, (k,))
 
+    def early(r, b):
+        turn(v("stt%d" % b, 0, 32, p=(0, 64)), v("stg%d" % b, 0, 32, p=(0, 64)))
+        copy(v("oe", 12 * b, 12 * b + 12), v("stt%d" % b, 0, 12))
+
     def claims(r):
-        e = v("mm", 0, C, -1)
-        scan(v("pr", 0, C), v("up", 0, C), e, -2048.0, ADD, MIN)
-        ts(v("clu", 0, 1), v("pr", C - 1, C), 2048.0, ADD, v("chg", 0, 1), MAX)
-        scan(v("pr", C, 2 * C), v("down", 0, C), e, 0.0, ADD, MAX)
-        ts(v("clu", 1, 2), v("pr", 2 * C - 1, 2 * C), -1.0, MUL, v("chg", 1, 2), MAX)
-        ts(v("tk", 2, 4), v("clu", 0, 2), float(C), LT, more, MUL)
-        lim = v("lim", 2 * r, 2 * r + 2)
-        tt(lim, v("tk", 2, 4), theirs(r), ADD)
-        sem, at = T.sem["rf%d" % r], ("lw", (0, 128, 2 * r, 2 * r + 2, 1))
-        if r == ROUNDS - 1:
-            send([lim], n, lambda: g.remote_dma(T.lw[:, 2 * r:2 * r + 2], lim[0], sem, T.sem.loc, pid, rid, full_mask), [at], "rf%d" % r)
+        if r < ROUNDS - 1:
+            for s in range(2):
+                scan(v("pr", C * s, C * s + C), v("up", 0, C), v("mm", C * s, C * s + C, -1), 0.0, ADD, MIN)
+            copy(v("clu", 0, 4, 2), v("pr", C - 1, 2 * C, C))
         else:
-            fd, where = T["fd%d" % r], [("fd%d" % r, (0, 128, 0, 2, 1))]
-            tr = [RemoteDMATransfer(dst_ids=[DstId(rid=rid, pnc=pid)], dma_engine_mask=halves[e], remote_sem=sem, src=lim[0], dst=d) for e, d in enumerate((fd[:], T.lw[:, 2 * r:2 * r + 2]))]
-            send([lim], n, lambda: g.remote_dma_fused(tr, local_sem=T.sem.loc), where + [at], "rf%d" % r)
-            for G in range(6):
-                dma("S", "dlr%d" % r, rows(G, 4, 7, LATE, LATE + 32), (fd[64:112, :], where), 192, 3)
+            scan(v("pr", 0, C), v("up", 0, C), v("mm", 0, C, -1), -BIG, ADD, MIN)
+            scan(v("pr", C, 2 * C), v("down", 0, C), v("mm", 0, C, -1), BIG, ADD, MAX)
+            ts(v("clu", 0, 1), v("pr", C - 1, C), BIG, ADD)
+            ts(v("clu", 2, 3), v("pr", 2 * C - 1, 2 * C), -1.0, MUL, BIG, ADD)
+            for s in range(2):
+                ts(v("full", s, s + 1), v("clu", 2 * s, 2 * s + 1), float(C), LT, v("full", 2 + s, 3 + s), MAX)
+            where = [("fin", (0, 128, 0, 2, 1))]
+            send([v("full", 0, 2)], n, lambda: g.remote_dma(T.fin[:], T.full[:, 0:2], T.sem.rf, T.sem.loc, pid, rid, full_mask), where, "rf")
+            dma("S", "dout", inp(T.bp[:, 384:416]), (T.fin[:], where), 1024, 8)
         for t in range(4):
-            act(v("ctl", t, 128, 4), ind(v("zp", 400 * t, 400 * t + 400), v("clu", 0, 2)))
+            for s in range(2):
+                out, at = v("ctl", 4 * s + t, 128, 8), v("clu", 2 * s, 2 * s + 1)
+                if r < ROUNDS - 1:
+                    act(out, ind(v("zp", 400 * t, 400 * t + 400), at))
+                else:
+                    scaled(OPT["ctl"][t], out, ind(v("fs", 400 * t, 400 * t + 400), at), 64.0)
         qc, qs, a = T["qcc%d" % r], T["qcs%d" % r], 128 + 32 * r
         quant(*pair("qcc%d" % r, "qcs%d" % r, 0, 128), v("ctl", 0, 512))
         send([v("qcc%d" % r, 0, 32)], n, lambda: g.remote_dma(T.lc[:, a:a + 32].bitcast(dt.uint8), qc[:, 0:32].bitcast(dt.uint8), T.sem["rc%d" % r], T.sem.loc, pid, rid, full_mask),
@@ -554,16 +593,16 @@ def rank_program(g, core, T, topo):
         quant(*pair("qxc", "qxs", a, a + k), v("xt", 896 * b, 896 * b + 4 * k))
         for k in range(2):
             mx(bank(b, k, 0, 128), *pair("qxc", "qxs", a + 96 * k, a + 96 * k + 128), *pair("qpc", "qps", 0, 128))
-            ts(v("bits", 144 * b + 72 * k, 144 * b + 72 * k + 64), bank(b, k, 0, 64), 0.0, GT)
+            ts(v("bits", 160 * b + 80 * k + 8, 160 * b + 80 * k + 72), bank(b, k, 0, 64), 0.0, GT)
         ev = "ev%d" % b
-        scan(v(ev, 0, 144), v("horn", 0, 144), v("bits", 144 * b, 144 * b + 144), 0.0, MUL, ADD)
+        scan(v(ev, 0, 160), v("horn", 0, 160), v("bits", 160 * b, 160 * b + 160), 0.0, MUL, ADD)
         for k in range(2):
-            ts(v("of%d" % b, k, 16, 2), v(ev, 72 * k + 12, 72 * k + 72, 8), 32.0, MUL, v(ev, 72 * k + 4, 72 * k + 5), ADD)
+            ts(v("of%d" % b, k, 16, 2), v(ev, 80 * k + 4, 80 * k + 61, -8), 32.0, MUL, v(ev, 80 * k + 72, 80 * k + 73), ADD)
 
     def level(r, b, h):
         a, m, res, trb, o = LO[h], 8 - h, "res%d" % b, "trb%d" % b, "of%d" % b
-        w = v("win", TAB[h], (SOON if h < 4 else LATE) + 64)
-        k = OPT["share"][h]
+        w = v("win", *WIN[h])
+        k = OPT["share"][b][h]
         if k:
             copy(v(res, a, a + 32 * k), ind(w, v(o, 16 * h, 16 * h + 2 * k)))
         if k < m:
@@ -571,10 +610,7 @@ def rank_program(g, core, T, topo):
         z = a + 32 * m
 
         def stage(h, row, a):
-            dma("S", "dl%d%d" % (r, b), v("stg%d" % b, 16 * (h % 2), 16 * (h % 2) + 16, p=(32 * (h // 2), 32 * (h // 2) + 12)), rows16(res, row, 96, a, a + 32), 384, 12)
-        if h < 4 and r < ROUNDS - 1:
-            for G in range(2):
-                dma("S", "de%d" % r, v("ste", 16 * G, 16 * G + 16, p=(32 * h + 12 * b, 32 * h + 12 * b + 12)), rows16(res, 7, 96, z - 32, z), 384, 12)
+            dma("S", "dl%d%d%d" % (r, b, h // 4), v("stg%d" % b, 16 * (h % 2), 16 * (h % 2) + 16, p=(32 * (h // 2), 32 * (h // 2) + 12)), rows16(res, row, 96, a, a + 32), 384, 12)
         stage(h, 7, z - 32)
         if h < 6:
             turn(v(trb, a, z), v(res, a, z))
@@ -588,49 +624,57 @@ def rank_program(g, core, T, topo):
     def state(r, b):
         for t in range(4):
             mx(bank(b, t), *pair("ec", "es", 128 * t, 128 * t + 128), *pair("qxc", "qxs", 224 * b, 224 * b + H))
-            if t < OPT["nv"]:
-                act(v("fs%d" % b, H * t, H * t + H), bank(b, t))
+            if t < OPT["nv"][2 * r + b] or r == ROUNDS - 1:
+                act(v("fs", 400 * t + AT[b], 400 * t + AT[b] + H), bank(b, t))
 
     def diff(r, b):
-        turn(v("stt%d" % b, 0, 32), v("stg%d" % b, 0, 32))
-        copy(v("ol%d" % b, 0, 16), ind(v("stt%d" % b, 0, 32), v("cl", 0, 1)))
-        ol, zt = v("ol%d" % b, 0, 12), "zt%d" % b
-        act(v("mm", H * b, H * b + H), ind(v("mw", 0, 64), ol))
+        p = (64 * (r < ROUNDS - 1), 128)
+        turn(v("stt%d" % b, 0, 32, p=p), v("stg%d" % b, 0, 32, p=p))
+        copy(v("ol", 12 * b, 12 * b + 16), ind(v("stt%d" % b, 0, 32), v("cl", 0, 1)))
+        ol, zt = v("ol", 12 * b, 12 * b + 12), "zt%d" % b
+        if r == ROUNDS - 1:
+            act(v("mm", AT[b], AT[b] + H), ind(v("mw", 128, 192), ol))
         for t in range(4):
             w = ind(v("tw", 256 * r + 64 * t, 256 * r + 64 * t + 64), ol)
-            if t < OPT["nv"]:
-                tt(v(zt, t, 768, 4), w, v("fs%d" % b, H * t, H * t + H), ADD)
+            if t < OPT["nv"][2 * r + b]:
+                tt(v(zt, t, 768, 4), w, v("fs", 400 * t + AT[b], 400 * t + AT[b] + H), ADD)
             else:
                 act(v("gt%d" % b, H * t, H * t + H), w)
                 tt(v(zt, t, 768, 4), bank(b, t), v("gt%d" % b, H * t, H * t + H), ADD)
-            scaled(OPT["full"][t], v("zp", 400 * t + H * b, 400 * t + H * b + H), v(zt, t, 768, 4), 64.0)
+            scaled(OPT["full" if r < ROUNDS - 1 else "fin"][4 * b + t], v("zp", 400 * t + AT[b], 400 * t + AT[b] + H), v(zt, t, 768, 4), 64.0)
         if r == ROUNDS - 1:
-            act(v("bpt", H * b, H * b + H), ind(v("bw", 0, 64), ol))
+            act(v("bpt", AT[b], AT[b] + H), ind(v("bw", 0, 64), ol))
 
     def layer(r, b):
         qz = pair("qzc", "qzs", H * b, H * b + H)
         quant(*qz, v("zt%d" % b, 0, 768))
         for t in range(4):
             mx(bank(b, t), *pair("wq", "wp", 128 * t, 128 * t + 128), *qz)
-            tt(v("xt", 896 * b + t, 896 * b + 768, 4), bank(b, t), v("zp", 400 * t + H * b, 400 * t + H * b + H), ADD)
+            tt(v("xt", 896 * b + t, 896 * b + 768, 4), bank(b, t), v("zp", 400 * t + AT[b], 400 * t + AT[b] + H), ADD)
 
     def both(fn, *args):
         for b in range(2):
-            pri[0] = OPT["bias"] * (1 - b)
+            pri[0], mark = 0.0, len(ops)
             fn(args[0], b, *args[1:])
-        pri[0] = 0.0
+            for o in ops[mark:]:
+                o["first"] = 1 - b
 
+    calm = []
     for r in range(ROUNDS):
         both(images, r)
-        unpack(r - 1)
         both(state, r)
+        unpack(r - 1)
         keys(r)
         for h in range(7):
             both(level, r, h)
+            calm.append(len(ops) - 1)
             if h == 3 and r < ROUNDS - 1:
+                both(early, r)
                 pri[0] = OPT["soon"]
-                early(r)
+                tell(r, 0)
         both(diff, r)
+        if r < ROUNDS - 1:
+            tell(r, 1)
         pri[0] = OPT["claim"] + OPT["last"] * (r == ROUNDS - 1)
         claims(r)
         both(layer, r)
@@ -638,21 +682,25 @@ def rank_program(g, core, T, topo):
     quant(*pair("qvc", "qvs", 0, 128), v("vt", 0, 512))
     dma("S", "dout", inp(T.bp[:, 0:384]), rows16("bpt", 0, 128, 0, 384), 12288, 24)
     for b in range(2):
-        qf = pair("qfc", "qfs", H * b, H * b + H)
+        a = AT[b]
+        qf = pair("qfc", "qfs", a, a + H)
         quant(*qf, v("xt", 896 * b, 896 * b + 768))
         mx(bank(b, 0), *pair("qvc", "qvs", 0, 128), *qf)
-        dma("S", "dout", inp(T.oc[:, 768 * b:768 * b + 768]), codes("qfc", H * b, H * b + H), 98304, 128)
-        act(v("yt", H * b, H * b + H), bank(b, 0))
-        dma("A", "dout", inp(T.y[:, H * b:H * b + H]), v("yt", H * b, H * b + H), 98304, 128)
+        dma("S", "dout", inp(T.oc[:, 4 * a:4 * a + 768]), codes("qfc", a, a + H), 98304, 128)
+        act(v("yt", a, a + H), bank(b, 0))
+        k = dma("S", "dout", inp(T.y[:, a:a + H]), v("yt", a, a + H), 98304, 128)
+        ops[k]["tail"] = OPT["lead"] * (1 - b)
     for k in range(4):
         dma("S", "dout", inp(T.osc[4 * k:4 * k + 4, :]), v("qfs", 0, 384, p=(32 * k, 32 * k + 4)))
-    ts(v("full", 0, 2), mine(ROUNDS), dead, NE)
-    dma("S", "dout", inp(T.bp[:, 384:416]), v("full", 0, 2), 1024, 128)
-    unpack(r)
+    act(v("et1", 0, 516), v("et", 0, 516), 64.0)
+    ops[-1]["after"] = (calm[OPT["calm"]],)
     for t in range(4):
-        a = 768 + 64 * t
-        for s in range(2):
-            scaled("VA"[s] if t < 3 else "V", v("rtt", 4 * s + t, 128, 8), v("tw", a + 16 * s, a + 16 * s + 16), -64.0)
+        quant(*pair("ec", "es", 512 + 128 * t, 640 + 128 * t), v("et1", 3 - t, 515 - t))
+        act(v("rto", t, 128, 4), v("tw", 256 * r + 64 * t, 256 * r + 64 * t + 32), -64.0)
+    for t in range(4):
+        b, k = 0, (t + 1) % 4
+        mx(bank(b, k, 0, 128), *pair("ec", "es", 512 + 128 * t, 640 + 128 * t), *pair("lc", "ls", 32 + 32 * r, 160 + 32 * r))
+        tt(v("rtt", t, 128, 4), v("rto", t, 128, 4), bank(b, k, 96, 128), ADD)
     dma("S", "dout", inp(T.rt[:]), v("rtt", 0, 128), 65536, 128)
 
     if not ORDER:

import math
from concourse.bass import DstId, RemoteDMATransfer
from concourse.mybir import dt, AluOpType, AxisListType, ActivationFunctionType

ROUNDS, C, H, BIG = 3, 384, 192, 512.0
AT = (0, H)
OPT = dict(share=((4, 3, 3, 2, 2, 1, 2), (4, 3, 3, 2, 2, 1, 2)), ahead="s", calm=15, few="AAAAV", lead=0.0, ctl="AAAV", gap=0.5, look=0.05, nv=(2, 2, 2, 2, 2, 2), full="AAAAAAAV", fin="AAAAAAAV", eps=0.05, bias=(0.0, 0.25, 0.5, 0.75, 1.0, 1.5), claim=0.0, fills="AVA", more="PPPPP", tell=10.0, soon=1.0, last=0.5, diag=12.0,
           turns=3, tries=40, amp=0.3, part=0.05, swaps=6000, starts=4, heat=0.08, seed=6)
KIND = {"f": "float32", "b": "bfloat16", "i": "int32", "h": "uint16", "s": "uint8", "c": "float8_e4m3fn_x4", "e": "float16"}
SPEC = """b xt 1792 ut 512 vt 512 trp 512 et 516 et1 516 win 3280 tab 64 tat 64 res0 1152 res1 1152 trb0 1152 trb1 1152 bits 320 ev0 160 ev1 160 horn 160
b stg0 32 stg1 32 stt0 32 stt1 32 gt0 768 gt1 768 fs 1600 zt0 768 zt1 768 zp 1600 mw 192 mm 768 lim 8 ctl 512 zero 1128 lw 4 tw 768
b bw 64 me 2 nx 2 clr 32 clt 32 jnk 768 up 384 down 384 mwb 128
e pr 768
c qxc 448 qfc 384 quc 128 qpc 128 qvc 128 wq 512 ec 1024 qzc 384 qcc0 128 qcc1 128 qcc2 128 lc 224
s qxs 448 qfs 384 qus 128 qps 128 qvs 128 wp 512 es 1024 qzs 384 qcs0 128 qcs1 128 qcs2 128 ls 224
i tia 32 tib 32 pidx 1 pint 2 flw 2 flr 32
h ol 28 oe 24 clu 4 of0 128 of1 128 cl 2 ul 8
f rtt 128 rto 128 yt 384 bpt 384 full 4 pf 2 s16 2 l16 2 col 11 c32 8 got 4 key 2 far 4"""
PSUM = tuple("pb%d" % k for k in range(8))
SCRATCH = {"tdr": ("dram", [5, 32, 32], "bfloat16"), "fin": ("dram", [128, 2], "float32")}
TAGS = ("00", "01", "10", "11")
for _n in TAGS:
    SCRATCH["fe" + _n] = ("dram", [128, 2], "bfloat16")
for _l in SPEC.split("\n"):
    _w = _l.split()
    for _k in range(1, len(_w), 2):
        SCRATCH[_w[_k]] = ("sbuf", [128, int(_w[_k + 1])], KIND[_w[0]])
for _n in PSUM:
    SCRATCH[_n] = ("psum", [128, 512], "float32")
DMAS = "dx0 dx1 du dta dtb dtc dtr dw dfl dfr dv dw0 dt0 dt1 dw2 dw4 dout".split()
DMAS += ["dl%d%d%d" % (_k // 4, _k // 2 % 2, _k % 2) for _k in range(12)] + ["der" + _n for _n in TAGS]
SEMAPHORES = "cv ca ct_ cp loc rn rf rc0 rc1 rc2 rs0 rs1 rs2".split() + ["re" + _n for _n in TAGS] + DMAS

ADD, SUB, MUL, MAX, MIN = AluOpType.add, AluOpType.subtract, AluOpType.mult, AluOpType.max, AluOpType.min
EQ, NE, GT, GE, LT = AluOpType.is_equal, AluOpType.not_equal, AluOpType.is_gt, AluOpType.is_ge, AluOpType.is_lt
AND, SHR = AluOpType.bitwise_and, AluOpType.arith_shift_right
COPY, SAME, RELU = ActivationFunctionType.Copy, ActivationFunctionType.Identity, ActivationFunctionType.Relu
ORDER = []
PACE = ((0.85e-3, 0.2, 0.7, 1.55, 0.03, 1.56, 0.06, 1.3), (0.9e-3, 0.19, 0.9, 2.1, 0.035, 1.3, 0.12, 1.1), (1.1e-3, 0.22, 1.0, 2.8, 0.025, 1.9, 0.07, 1.3),
        (0.83e-3, 0.22, 0.65, 1.4, 0.02, 1.2, 0.05, 1.7))


def hit(a, b):
    return a[0] < b[1] and b[0] < a[1] and a[2] < b[3] and b[2] < a[3] and (a[2] - b[2]) % math.gcd(a[4], b[4]) == 0


def covers(a, b):
    return a[4] == 1 and a[0] <= b[0] and b[1] <= a[1] and a[2] <= b[2] and b[3] <= a[3]


def arrange(ops):
    n = len(ops)
    deps = [set(o["after"]) for o in ops]
    wr, rd, kin = {}, {}, {}
    for k, o in enumerate(ops):
        for name, reg in o["ins"]:
            deps[k].update(e[1] for e in wr.get(name, []) if hit(reg, e[0]))
            if name in PSUM:
                deps[k].update(e[1] for e in rd.get(name, []))
        for name, reg in o["outs"]:
            deps[k].update(e[1] for e in wr.get(name, []) + rd.get(name, []) if name in PSUM or hit(reg, e[0]))
        for name, reg in o["outs"]:
            wr[name] = [e for e in wr.get(name, []) if not covers(reg, e[0])] + [(reg, k)]
            rd[name] = [e for e in rd.get(name, []) if not covers(reg, e[0])]
        for name, reg in o["ins"]:
            rd.setdefault(name, []).append((reg, k))
        for d in list(deps[k]):
            if ops[d]["kind"] == "d" and d not in o["after"]:
                deps[k].update(kin[ops[d]["sem"]])
        deps[k].discard(k)
        if o["kind"] == "d":
            kin.setdefault(o["sem"], []).append(k)
    users = [[] for _ in ops]
    for k in range(n):
        for d in deps[k]:
            users[d].append(k)
    qs = [o["q"] for o in ops]
    deps = [sorted(d) for d in deps]
    soft = [set(o["after"]) if o["kind"] == "d" and o["size"] < 20000 else set() for o in ops]
    hard = [[d for d in deps[k] if d not in soft[k]] for k in range(n)]

    def costs(p):
        hold = [p[6] if o["kind"] == "d" else o["hold"] + max(o["cyc"] * (p[7] if o["q"] == "T" else 1.0) + p[5] * o["got"], 64) * p[0] * (o["kind"] == "c") for o in ops]
        late = [{"d": p[2], "a": p[3]}.get(o["kind"], 0.0) + p[1] for o in ops]
        move = [(p[4] * o["rows"] + 5e-5 * o["size"]) / 16 for o in ops]
        return hold, late, move
    cost = [costs(p) for p in PACE]
    hold, late, move = cost[0]
    way = [0.0] * n
    for k in range(n - 1, -1, -1):
        way[k] = hold[k] + move[k] + max([way[u] + late[k] * (k not in soft[u]) for u in users[k]] + [late[k] + ops[k].get("tail", 0.0)])

    def place(rank):
        left = [len(d) for d in deps]
        ready = {}
        for k in range(n):
            if not left[k]:
                ready.setdefault(qs[k], []).append(k)
        at, free, order, rings = [0.0] * n, {q: 0.0 for q in qs}, [], 0.0
        while len(order) < n:
            t, q = min((max(min(at[k] for k in ks), free[q]), q) for q, ks in ready.items() if ks)
            k = max([k for k in ready[q] if at[k] <= t + OPT["eps"]], key=lambda k: (rank[k], -k))
            urgent = [j for j in ready[q] if rank[j] > rank[k] + OPT["gap"] and at[j] + OPT["look"] < t + hold[k]]
            if urgent:
                j = min(urgent, key=lambda j: at[j])
                fit = [i for i in ready[q] if max(t, at[i]) + hold[i] <= at[j] + OPT["look"]]
                k = max(fit, key=lambda i: (rank[i], -i)) if fit else j
            done = free[q] = max(t, at[k]) + hold[k]
            if move[k]:
                done = rings = max(rings, done) + move[k]
            ready[q].remove(k)
            order.append(k)
            for u in users[k]:
                at[u] = max(at[u], free[q] if k in soft[u] else done + late[k])
                left[u] -= 1
                if not left[u]:
                    ready.setdefault(qs[u], []).append(u)
        return order

    def span(order, first=0, held=None, limit=1e9):
        total, seen, first = 0.0, [], first // 32
        for m, (hold, late, move) in enumerate(cost):
            end, marks = (list(held[m][0]), held[m][1][:first + 1]) if held else ([0.0] * n, [dict.fromkeys(qs + ["rings"], 0.0)])
            free = dict(marks[-1])
            for a in range(32 * first, n, 32):
                rings = free["rings"]
                for k in order[a:a + 32]:
                    q = qs[k]
                    t = free[q]
                    for d in hard[k]:
                        if end[d] > t:
                            t = end[d]
                    t = free[q] = t + hold[k]
                    if move[k]:
                        t = rings = (rings if rings > t else t) + move[k]
                    end[k] = t + late[k]
                free["rings"] = rings
                marks.append(dict(free))
            total += max(end) / len(cost)
            seen.append((end, marks))
        return total, seen if total <= limit else None

    def back(order):
        left = [len(u) for u in users]
        pos = [0] * n
        for i, k in enumerate(order):
            pos[k] = i
        ready = {}
        at, free, out = [0.0] * n, {q: 0.0 for q in qs}, [0.0] * n
        for k in range(n):
            if not left[k]:
                at[k] = late[k] + move[k]
                ready.setdefault(qs[k], []).append(k)
        for _ in range(n):
            t, q = min((max(min(at[k] for k in ks), free[q]), q) for q, ks in ready.items() if ks)
            k = max([k for k in ready[q] if at[k] <= t + OPT["eps"]], key=lambda k: pos[k])
            out[k] = free[q] = max(t, at[k]) + hold[k]
            ready[q].remove(k)
            for d in deps[k]:
                at[d] = max(at[d], out[k] + late[d] * (d not in soft[k]) + move[d])
                left[d] -= 1
                if not left[d]:
                    ready.setdefault(qs[d], []).append(d)
        return out

    def chain(order, c):
        hold, late, move = c
        end, free, rings, last, why, ring = [0.0] * n, {q: 0.0 for q in qs}, 0.0, {}, [None] * n, None
        for k in order:
            t, w = free[qs[k]], (last.get(qs[k]), True)
            for d in hard[k]:
                if end[d] >= t:
                    t, w = end[d], (d, False)
            done = free[qs[k]] = t + hold[k]
            if move[k]:
                if rings > done:
                    w = (ring, True)
                done = rings = max(rings, done) + move[k]
                ring = k
            last[qs[k]], why[k], end[k] = k, w, done + late[k]
        k, out = max(range(n), key=lambda k: end[k]), []
        while why[k][0] is not None:
            if why[k][1]:
                out.append((why[k][0], k))
            k = why[k][0]
        return out
    best, x = 1e9, OPT["seed"]
    for bias in OPT["bias"]:
        other = [way[k] + ops[k]["pri"] + bias * ops[k].get("first", 0) for k in range(n)]
        for _ in range(OPT["turns"] + 1):
            o = place(other)
            t = span(o)[0]
            if t <= best:
                best, rank, order = t, other, o
            other = back(o)
    for _ in range(OPT["tries"]):
        other = list(rank)
        for k in range(n):
            x = (x * 1103515245 + 12345) % 2147483648
            if x < OPT["part"] * 2147483648:
                x = (x * 1103515245 + 12345) % 2147483648
                other[k] += OPT["amp"] * (x / 1073741824 - 1.0)
        o = place(other)
        t = span(o)[0]
        if t <= best:
            best, rank, order = t, other, o
    now, t0, pairs, held = order, best, [], span(order)[1]
    first, steps = (order, best), OPT["swaps"]
    for step in range(steps * (OPT["starts"] + 2)):
        if step % steps == 0 and step <= steps * OPT["starts"]:
            now, t0 = first if step < steps * OPT["starts"] else (order, best)
            pairs, held = [], span(now)[1]
        cool = 1 - step % steps / steps if step < steps * OPT["starts"] else (1 - (step / steps - OPT["starts"]) / 2) / 2
        if not pairs:
            pairs = chain(now, cost[step % len(cost)])
        x = (x * 1103515245 + 12345) % 2147483648
        a, b = pairs.pop((x >> 8) % len(pairs))
        i, j = now.index(a), now.index(b)
        mid = now[i:j + 1]
        if (x >> 7) % 2:
            take = {b}
            for k in reversed(mid):
                if k in take:
                    take.update(deps[k])
            if a in take:
                continue
            new = [k for k in mid if k in take] + [k for k in mid if k not in take]
        else:
            take = {a}
            for k in mid:
                if k in take:
                    take.update(users[k])
            if b in take:
                continue
            new = [k for k in mid if k not in take] + [k for k in mid if k in take]
        o = now[:i] + new + now[j + 1:]
        x = (x * 1103515245 + 12345) % 2147483648
        t, seen = span(o, i, held, t0 + OPT["heat"] * cool * x / 2147483648)
        if seen:
            now, t0, pairs, held = o, t, [], seen
            if t < best:
                best, order = t, o
    OPT["span"] = best
    return order


def rank_program(g, core, T, topo):
    rank = T.rank_of(core)
    if rank is None:
        return
    nxt, prv = T.cores[(rank + 1) % len(T.cores)], T.cores[(rank - 1) % len(T.cores)]
    eng = {"V": g.vector, "A": g.scalar, "T": g.tensor, "S": g.sync, "P": g}
    semof = {"V": "cv", "A": "ca", "T": "ct_", "P": "cp"}
    ops, pri = [], [0.0]

    def regs(vs):
        out = []
        for e in vs:
            out += e[1]
        return out

    def add(q, kind, fn, outs, ins, sem, cnt=1, hold=0.0, cyc=0, got=0, rows=0, size=0, after=()):
        ops.append(dict(q=q, kind=kind, fn=fn, outs=regs(outs), ins=regs(ins), sem=sem, cnt=cnt, hold=hold, cyc=cyc, got=got, rows=rows, size=size, after=after, pri=pri[0]))
        return len(ops) - 1

    def run(q, fn, outs, ins, cyc, got=0):
        add(q, "c", fn, outs, ins, semof[q], cyc=cyc, got=got)

    def dma(q, sem, out, in_, size=1024, rows=16, after=()):
        return add(q, "d", lambda: eng[q].dma_start(out[0], in_[0]), [out], [in_], sem, 16, 0.07, rows=rows, size=size, after=after)

    def v(name, a, b, s=1, p=(0, 128)):
        t, q = T[name], slice(*p)
        if s < 0:
            return (t[q, slice(b - 1, a - 1 if a else None, s)], [(name, (p[0], p[1], a, b, 1))], len(range(a, b, -s)), name)
        return (t[q, a:b:s] if s != 1 else t[q, a:b], [(name, (p[0], p[1], a, b, s))], len(range(a, b, s)), name)

    def rows16(name, first, last, a, b):
        return (T[name][first:last:16, a:b], [(name, (first, last, a, b, 1))])

    def codes(name, a, b):
        return (T[name][:, a:b].bitcast(dt.uint8), [(name, (0, 128, a, b, 1))])

    def inp(ap):
        return (ap, [])

    def ind(win, off):
        return (win[0].indirect(off[0]), win[1] + off[1], 16 * off[2], None)

    def price(out, in_):
        if in_[3] is None:
            return 60, in_[2]
        narrow = all(SCRATCH[e[3]][2] in ("bfloat16", "uint16", "float16") for e in (out, in_))
        return (in_[2] / 2 if narrow else in_[2]), 0

    def copy(out, in_):
        run("V", lambda: g.vector.tensor_copy(out[0], in_[0]), [out], [in_], *price(out, in_))

    def act(out, in_, scale=1.0):
        if isinstance(scale, tuple):
            run("A", lambda: g.scalar.activation(out[0], in_[0], SAME, scale=scale[0]), [out], [in_, scale], in_[2])
        else:
            run("A", lambda: g.scalar.activation(out[0], in_[0], COPY, scale=scale) if scale != 1.0 else g.scalar.activation(out[0], in_[0], COPY), [out], [in_],
                *((in_[2], 0) if in_[3] else (78, in_[2])))

    def count(out, in_, total):
        run("A", lambda: g.scalar.activation(out[0], in_[0], COPY, accum_out=total[0]), [out, total], [in_], 100, in_[2])

    def line(out, in_, scale, bias, func=SAME):
        x, y = [e[0] if isinstance(e, tuple) else e for e in (scale, bias)]
        run("A", lambda: g.scalar.activation(out[0], in_[0], func, bias=y, scale=x), [out], [in_] + [e for e in (scale, bias) if isinstance(e, tuple)], in_[2])

    def scaled(q, out, in_, scale):
        if q == "A":
            act(out, in_, scale)
        else:
            ts(out, in_, scale, MUL)

    def tt(out, a, b, op):
        run("V", lambda: g.vector.tensor_tensor(out[0], a[0], b[0], op), [out], [a, b],
            *(price(out, a) if a[3] is None else (a[2] * (1 if a[3] in PSUM or b[3] in PSUM else 2), 0)))

    def ts(out, a, s1, op0, s2=None, op1=None):
        ins = [a] + [s for s in (s1, s2) if isinstance(s, tuple)]
        x1 = s1[0] if isinstance(s1, tuple) else s1
        x2 = s2[0] if isinstance(s2, tuple) else s2
        if op1 is None:
            run("V", lambda: g.vector.tensor_scalar(out[0], a[0], x1, None, op0), [out], ins, *price(out, a))
        else:
            run("V", lambda: g.vector.tensor_scalar(out[0], a[0], x1, x2, op0, op1), [out], ins, *price(out, a))

    def scan(out, a, b, first, op0, op1):
        more = [first] if isinstance(first, tuple) else []
        run("V", lambda: g.vector.tensor_tensor_scan(out[0], a[0], b[0], first[0] if more else first, op0, op1), [out], [a, b] + more, *price(out, a))

    def fill(out, c):
        run("V", lambda: g.vector.memset(out[0], c), [out], [], *price(out, out))

    def quant(c, s, in_):
        run("V", lambda: g.vector.quantize_mx(c[0], s[0], in_[0]), [c, s], [in_], 15 + 0.265 * in_[2])

    def mx(out, lc, ls, rc, rs, start=True, stop=True):
        run("T", lambda: g.tensor.matmul_mx(out[0], lc[0], ls[0], rc[0], rs[0], start, stop), [out], [lc, ls, rc, rs], rc[2] + 16)

    def pair(c, s, a, b):
        return v(c, a, b), v(s, a, b)

    def turn(out, in_):
        run("V", lambda: g.vector.transpose(out[0], in_[0]), [out], [in_], *price(out, in_))

    def iota(out, pattern, base, cm=0):
        if SCRATCH[out[3]][2] == "int32":
            run("P", lambda: g.iota(out[0], pattern, base, cm), [out], [], 160 + 2 * out[2])
        else:
            run("P", lambda: g.iota(out[0], pattern, base, cm, allow_small_or_imprecise_dtypes=True), [out], [], 160 + 2 * out[2])

    def const(q, out, c=0):
        if q == "A":
            z = v("zero", 0, out[2])
            run("A", lambda: g.scalar.activation(out[0], z[0], COPY, bias=float(c)) if c else g.scalar.activation(out[0], z[0], COPY), [out], [z], out[2])
        elif q == "V":
            fill(out, float(c))
        else:
            iota(out, [[0, out[2]]], c)

    def col(k, n=1):
        return v("col", k, k + n)

    iota(v("flr", 0, 32), [[1, 32]], 0)
    pri[0] = 9.0
    dma("S", "dta", v("tia", 0, 32, p=(0, 64)), inp(T.ti[0:2, :]), 8192, 64)
    pri[0] = 0.0
    dma("S", "du", v("ut", 0, 512), inp(T.u[:]), 131072, 128)
    for b in range(2):
        dma("S", "dx%d" % b, v("xt", 896 * b, 896 * b + 768), inp(T.x[:, 4 * AT[b]:4 * AT[b] + 768]), 196608, 128)
    for G in range(6):
        dma("S", "dfr", v("flr", 0, 32, p=(16 * G, 16 * G + 7)), inp(T.fl[0:7, :]), 896, 7)

    def later(names, after):
        for c in names:
            if c == "s":
                dma("S", "dtc", v("tia", 0, 32, p=(64, 128)), inp(T.ti[2:4, :]), 8192, 64, after)
            elif c == "t":
                dma("S", "dtb", v("tib", 0, 32, p=(0, 96)), inp(T.ti[4:7, :]), 12288, 96, after)
            else:
                dma("S", "dfl", v("flw", 0, 2), inp(T.fl[:]), 1024, 128, after)
    later(OPT["ahead"], ())

    fill(v("zero", 0, 1128), 0.0)
    iota(v("pidx", 0, 1), [[0, 1]], 0, 1)
    iota(v("s16", 0, 2), [[1, 2]], 0)
    iota(v("bw", 0, 32), [[1, 32]], 0)
    const(OPT["few"][2], v("bw", 32, 64), -1)
    const(OPT["few"][2], v("clr", 0, 32))
    iota(v("clr", 0, 12), [[1, 2], [2, 6]], 0)
    iota(v("clr", 16, 28), [[2, 2], [4, 3], [1, 2]], 0)
    copy(v("clr", 16, 28, p=(96, 128)), v("clr", 0, 12, p=(96, 128)))
    turn(v("clt", 0, 32), v("clr", 0, 32))
    copy(v("cl", 0, 1), v("clt", 0, 1))
    ts(v("pint", 0, 1), v("pidx", 0, 1), 15, AND)
    ts(v("pint", 1, 2), v("pidx", 0, 1), 4, SHR)
    copy(v("pf", 0, 2), v("pint", 0, 2))
    i15 = v("pf", 0, 1)
    ts(col(2, 2), v("pf", 0, 2), 6.0, GE, 31.0, MUL)
    line(col(0, 2), col(2, 2), 1.0, 1.0)
    dead = col(1)
    ts(col(4), i15, 7.0, LT)
    act(col(5), col(0), col(4))
    line(col(6), col(4), -1.0, 1.0)
    line(col(7), col(5), -1.0, col(6))
    line(col(8), dead, -2.0 * BIG, BIG)
    ts(col(9), i15, 8.0, GE, -24.0, MUL)
    ts(col(10), i15, 8.0, GE, -27.0, MUL)
    iota(v("c32", 0, 8), [[0, 2], [-32, 4]], 112)
    ts(v("ul", 0, 8), v("c32", 0, 8), i15, ADD, col(9), ADD)
    ts(v("ul", 3, 8, 4), v("c32", 3, 8, 4), i15, ADD, col(10), ADD)
    q = OPT["few"]
    const(q[0], v("horn", 0, 160), 2)
    const(q[0], v("horn", 0, 160, 8))
    const(q[0], v("horn", 4, 160, 80))
    const(q[0], v("horn", 67, 160, 80))
    const(q[0], v("horn", 72, 160, 80), 1)
    const(q[1], v("bits", 0, 320), 66)
    const(q[1], v("bits", 4, 320, 80), -2)
    for b in range(2):
        const("P", v("xt", 896 * b + 768, 896 * b + 896))
        const(q[2], v("stg%d" % b, 0, 32))
        const(q[2], v("stt%d" % b, 0, 32))
    WIN = [(32, 1122)] * 2 + [(0, 2146)] * 2 + [(2176, 3266)] * 3
    SOON, LATE = 34, 2178

    def rows(G, h, k, a, n):
        return v("win", a, a + n, p=(16 * G + h, 16 * G + k))
    for q, (a, z) in zip(OPT["fills"], ((0, 1128), (1128, 2176), (2176, 3280))):
        const(q, v("win", a, z))
    for a in (SOON, LATE):
        line(v("win", a + 32, a + 64), v("zero", 0, 32), 1.0, col(0))
        ops[-1]["outs"] = v("win", a + 30, a + 70)[1]
        ts(v("win", a, a + 32), v("flr", 0, 32), col(7), MUL, col(5), ADD)

    def tables(name, a, p, k):
        for q, c in zip(p, k):
            ts(v("tab", a, a + 32, p=q), v(name, 0, 32, p=q), c, ADD)
        q = (p[0][0], p[-1][1])
        turn(v("tat", a, a + 32, p=q), v("tab", a, a + 32, p=q))

    def staged(a, b):
        return (T.tdr[a:b, :, :], [("tdr", (a, b, 0, 1, 1))])
    tables("tia", 0, ((0, 32), (32, 64)), (2.0, 34.0))
    for G in range(6):
        k = dma("S", "dw0", rows(G, 0, 2, 98, 1024), v("tat", 0, 32, p=(0, 64)), 4096, 64)
    later([c for c in "stf" if c not in OPT["ahead"]], (k,))
    tables("tia", 0, ((64, 96), (96, 128)), (34.0, 2.0))
    dma("S", "dt0", staged(0, 2), v("tat", 0, 32, p=(64, 128)), 4096, 64)
    tables("tib", 32, ((0, 64), (64, 96)), (2.0, 0.0))
    dma("S", "dt1", staged(2, 5), v("tat", 32, 64, p=(0, 96)), 6144, 96)
    for G in range(6):
        dma("S", "dw2", rows(G, 2, 4, 1122, 1024), staged(0, 2), 4096)
    for G in range(6):
        k = dma("S", "dw4", rows(G, 4, 7, LATE + 64, 1024), staged(2, 5), 6144)
    dma("S", "dtr", v("trp", 384, 512), inp(T.tr[:]), 32768, 128, (k,))
    for a in (0, 256):
        dma("S", "dw", codes("wq", a, a + 256), inp(T.wc[:, 4 * a:4 * a + 1024]), 131072, 128, (k,))
    dma("S", "dw", v("wp", 0, 512), inp(T.ws[:]), 65536, 128, (k,))
    pri[0] = OPT["tell"]
    ts(v("me", 0, 2), v("flw", 0, 2), 0.0, EQ, dead, MUL)
    pri[0] = 0.0
    quant(*pair("quc", "qus", 0, 128), v("ut", 0, 512))
    ul = v("ul", 0, 8)
    run("V", lambda: g.vector.tensor_copy(T.qpc[:, 0:128].bitcast(dt.uint32), T.quc[:, 0:128].bitcast(dt.uint32).indirect(ul[0])), [v("qpc", 0, 128)], [v("quc", 0, 128), ul], 60, 128)
    act(v("qps", 0, 128), ind(v("qus", 0, 128), ul))
    pri[0] = OPT["diag"]
    const(OPT["few"][4], v("et", 0, 516), 2.0 ** -6)
    run("P", lambda: g.affine_select(T.et[:], T.et[:], [[1, 516]], EQ, 0.0, -3, -4), [v("et", 0, 516)], [v("et", 0, 516)], 200 + 2 * 516)
    for b in range(4):
        quant(*pair("ec", "es", 128 * b, 128 * b + 128), v("et", 3 - b, 515 - b))
    pri[0] = 0.0
    const(OPT["more"][0], v("trp", 0, 384))
    quant(*pair("lc", "ls", 0, 128), v("trp", 0, 512))
    const(OPT["more"][1], v("ctl", 128, 512))
    const(OPT["more"][2], v("tw", 0, 768))
    const(OPT["more"][3], v("up", 0, 384), 1)
    const(OPT["more"][4], v("down", 0, 384), -1)
    for t in range(4):
        const("P", v("zp", 400 * t + 384, 400 * t + 400))
        const("P", v("fs", 400 * t + 384, 400 * t + 400))
    ts(v("l16", 0, 2), v("s16", 0, 2), i15, ADD, i15, ADD)
    for s in range(2):
        ts(v("mwb", 64 * s, 64 * s + 64), v("bw", 0, 64), v("l16", s, s + 1), EQ, -1.0, MUL)

    elist = topo.engines(core, nxt)
    n = 1
    while n * 2 <= len(elist) and n < 8:
        n *= 2
    elist = elist[:n]
    full_mask = sum(1 << e for e in elist)
    half = len(elist) // 2
    halves = [sum(1 << e for e in elist[:half]), sum(1 << e for e in elist[half:])]
    rid, pid, _ = topo.addr(nxt)

    def send(ins, cnt, fn, where, sem, hold=0.3):
        k = add("P", "r", fn, [], ins, "loc", cnt, hold)
        add("R", "a", None, [(None, where)], [], sem, cnt, after=(k,))

    ridb, pidb, _b = topo.addr(prv)
    maskb = sum(1 << e for e in topo.engines(core, prv)[:half])
    pri[0] = OPT["tell"]
    send([v("me", 0, 2)], half, lambda: g.remote_dma(T.nx[:], T.me[:], T.sem.rn, T.sem.loc, pidb, ridb, maskb), [("nx", (0, 128, 0, 2, 1))], "rn", 1.8)

    def bank(b, t, a=0, z=H, s=1):
        return v("pb%d" % (4 * b + t), a, z, s)

    def theirs(r):
        return v("nx", 0, 2) if r == 0 else v("lim", 4 * r - 2, 4 * r)

    def unpack(r):
        for t in range(4):
            b, k = t % 2, t // 2
            for j in range(r + 2):
                mx(bank(b, k, 0, 128), *pair("ec", "es", 128 * t, 128 * t + 128), *pair("lc", "ls", 32 * j, 32 * j + 128), j == 0, j == r + 1)
            a = 256 * r + 256 + 64 * t
            act(v("tw", a, a + 32), bank(b, k, 96, 128), -1.0)

    def keys(r):
        line(v("far", 0, 2), theirs(r), BIG, col(8))
        for s in range(2):
            a = 2 * r - 2 + s
            line(v("key", s, s + 1), v("me", s, s + 1) if r == 0 else v("lw", a, a + 1), BIG, v("far", s, s + 1), RELU)
            line(v("mw", 64 * s, 64 * s + 64), v("mwb", 64 * s, 64 * s + 64), v("key", s, s + 1), BIG)
        if r < ROUNDS - 1:
            line(v("far", 2, 4), theirs(r), 1.0, -C * BIG)
        else:
            line(v("full", 2, 4), theirs(r), -1.0, 1.0, RELU)
            tt(v("mw", 128, 192), v("mw", 0, 64), v("mw", 64, 128), SUB)

    def tell(r, e):
        tag, k = "%d%d" % (r, e), 4 * r + 2 * e
        for s in range(2):
            got = v("got", 2 * e + s, 2 * e + s + 1)
            count(v(("jnk", "mm")[e], C * s, C * s + C), ind(v("mw", 64 * s, 64 * s + 64), v(("oe", "ol")[e], 0, 24)), got)
            ts(v("lim", k + s, k + s + 1), got, v("far", 2 + s, 3 + s), ADD, 0.0, MAX)
        lim, fe, where, sem = v("lim", k, k + 2), T["fe" + tag], [("fe" + tag, (0, 128, 0, 2, 1))], T.sem["re" + tag]
        if e:
            tr = [RemoteDMATransfer(dst_ids=[DstId(rid=rid, pnc=pid)], dma_engine_mask=halves[j], remote_sem=sem, src=lim[0], dst=d) for j, d in enumerate((fe[:], T.lw[:, 2 * r:2 * r + 2]))]
            send([lim], n, lambda: g.remote_dma_fused(tr, local_sem=T.sem.loc), where + [("lw", (0, 128, 2 * r, 2 * r + 2, 1))], "re" + tag)
        else:
            send([lim], n, lambda: g.remote_dma(fe[:], lim[0], sem, T.sem.loc, pid, rid, full_mask), where, "re" + tag)
        for G in range(6):
            k = dma("S", "der" + tag, rows(G, 4 * e, 4 + 3 * e, (SOON, LATE)[e], 32), (fe[64 * e:64 + 48 * e, :], where), 256, 4)
        if r == 0 and e == 0:
            dma("S", "dv", v("vt", 0, 512), inp(T.v[:]), 131072, 128, (k,))

    def early(r, b):
        turn(v("stt%d" % b, 0, 32, p=(0, 64)), v("stg%d" % b, 0, 32, p=(0, 64)))
        copy(v("oe", 12 * b, 12 * b + 12), v("stt%d" % b, 0, 12))

    def claims(r):
        if r < ROUNDS - 1:
            for s in range(2):
                scan(v("pr", C * s, C * s + C), v("up", 0, C), v("mm", C * s, C * s + C, -1), 0.0, ADD, MIN)
            copy(v("clu", 0, 4, 2), v("pr", C - 1, 2 * C, C))
        else:
            scan(v("pr", 0, C), v("up", 0, C), v("mm", 0, C, -1), -BIG, ADD, MIN)
            scan(v("pr", C, 2 * C), v("down", 0, C), v("mm", 0, C, -1), BIG, ADD, MAX)
            ts(v("clu", 0, 1), v("pr", C - 1, C), BIG, ADD)
            ts(v("clu", 2, 3), v("pr", 2 * C - 1, 2 * C), -1.0, MUL, BIG, ADD)
            for s in range(2):
                ts(v("full", s, s + 1), v("clu", 2 * s, 2 * s + 1), float(C), LT, v("full", 2 + s, 3 + s), MAX)
            where = [("fin", (0, 128, 0, 2, 1))]
            send([v("full", 0, 2)], n, lambda: g.remote_dma(T.fin[:], T.full[:, 0:2], T.sem.rf, T.sem.loc, pid, rid, full_mask), where, "rf")
            dma("S", "dout", inp(T.bp[:, 384:416]), (T.fin[:], where), 1024, 8)
        for t in range(4):
            for s in range(2):
                out, at = v("ctl", 4 * s + t, 128, 8), v("clu", 2 * s, 2 * s + 1)
                if r < ROUNDS - 1:
                    act(out, ind(v("zp", 400 * t, 400 * t + 400), at))
                else:
                    scaled(OPT["ctl"][t], out, ind(v("fs", 400 * t, 400 * t + 400), at), 64.0)
        qc, qs, a = T["qcc%d" % r], T["qcs%d" % r], 128 + 32 * r
        quant(*pair("qcc%d" % r, "qcs%d" % r, 0, 128), v("ctl", 0, 512))
        send([v("qcc%d" % r, 0, 32)], n, lambda: g.remote_dma(T.lc[:, a:a + 32].bitcast(dt.uint8), qc[:, 0:32].bitcast(dt.uint8), T.sem["rc%d" % r], T.sem.loc, pid, rid, full_mask),
             [("lc", (0, 128, a, a + 32, 1))], "rc%d" % r)
        send([v("qcs%d" % r, 0, 32)], n, lambda: g.remote_dma(T.ls[:, a:a + 32], qs[:, 0:32], T.sem["rs%d" % r], T.sem.loc, pid, rid, full_mask),
             [("ls", (0, 128, a, a + 32, 1))], "rs%d" % r)

    LO = [0]
    for h in range(8):
        LO.append(LO[h] + 32 * (8 - h))

    def images(r, b):
        a = 224 * b
        k = 224 if r == 0 else H
        quant(*pair("qxc", "qxs", a, a + k), v("xt", 896 * b, 896 * b + 4 * k))
        for k in range(2):
            mx(bank(b, k, 0, 128), *pair("qxc", "qxs", a + 96 * k, a + 96 * k + 128), *pair("qpc", "qps", 0, 128))
            ts(v("bits", 160 * b + 80 * k + 8, 160 * b + 80 * k + 72), bank(b, k, 0, 64), 0.0, GT)
        ev = "ev%d" % b
        scan(v(ev, 0, 160), v("horn", 0, 160), v("bits", 160 * b, 160 * b + 160), 0.0, MUL, ADD)
        for k in range(2):
            ts(v("of%d" % b, k, 16, 2), v(ev, 80 * k + 4, 80 * k + 61, -8), 32.0, MUL, v(ev, 80 * k + 72, 80 * k + 73), ADD)

    def level(r, b, h):
        a, m, res, trb, o = LO[h], 8 - h, "res%d" % b, "trb%d" % b, "of%d" % b
        w = v("win", *WIN[h])
        k = OPT["share"][b][h]
        if k:
            copy(v(res, a, a + 32 * k), ind(w, v(o, 16 * h, 16 * h + 2 * k)))
        if k < m:
            act(v(res, a + 32 * k, a + 32 * m), ind(w, v(o, 16 * h + 2 * k, 16 * h + 2 * m)))
        z = a + 32 * m

        def stage(h, row, a):
            dma("S", "dl%d%d%d" % (r, b, h // 4), v("stg%d" % b, 16 * (h % 2), 16 * (h % 2) + 16, p=(32 * (h // 2), 32 * (h // 2) + 12)), rows16(res, row, 96, a, a + 32), 384, 12)
        stage(h, 7, z - 32)
        if h < 6:
            turn(v(trb, a, z), v(res, a, z))
            for G in range(2):
                c = a + 16 * G + h
                ts(v(o, 16 * h + 16 + G, 16 * h + 16 + 2 * (m - 1), 2), v(trb, c + 32, z, 32), 32.0, MUL, v(trb, c, c + 1), ADD)
        else:
            tt(v(res, z, z + 32), v(res, a, a + 32), v(res, a + 32, z), ADD)
            stage(7, 6, z)

    def state(r, b):
        for t in range(4):
            mx(bank(b, t), *pair("ec", "es", 128 * t, 128 * t + 128), *pair("qxc", "qxs", 224 * b, 224 * b + H))
            if t < OPT["nv"][2 * r + b] or r == ROUNDS - 1:
                act(v("fs", 400 * t + AT[b], 400 * t + AT[b] + H), bank(b, t))

    def diff(r, b):
        p = (64 * (r < ROUNDS - 1), 128)
        turn(v("stt%d" % b, 0, 32, p=p), v("stg%d" % b, 0, 32, p=p))
        copy(v("ol", 12 * b, 12 * b + 16), ind(v("stt%d" % b, 0, 32), v("cl", 0, 1)))
        ol, zt = v("ol", 12 * b, 12 * b + 12), "zt%d" % b
        if r == ROUNDS - 1:
            act(v("mm", AT[b], AT[b] + H), ind(v("mw", 128, 192), ol))
        for t in range(4):
            w = ind(v("tw", 256 * r + 64 * t, 256 * r + 64 * t + 64), ol)
            if t < OPT["nv"][2 * r + b]:
                tt(v(zt, t, 768, 4), w, v("fs", 400 * t + AT[b], 400 * t + AT[b] + H), ADD)
            else:
                act(v("gt%d" % b, H * t, H * t + H), w)
                tt(v(zt, t, 768, 4), bank(b, t), v("gt%d" % b, H * t, H * t + H), ADD)
            scaled(OPT["full" if r < ROUNDS - 1 else "fin"][4 * b + t], v("zp", 400 * t + AT[b], 400 * t + AT[b] + H), v(zt, t, 768, 4), 64.0)
        if r == ROUNDS - 1:
            act(v("bpt", AT[b], AT[b] + H), ind(v("bw", 0, 64), ol))

    def layer(r, b):
        qz = pair("qzc", "qzs", H * b, H * b + H)
        quant(*qz, v("zt%d" % b, 0, 768))
        for t in range(4):
            mx(bank(b, t), *pair("wq", "wp", 128 * t, 128 * t + 128), *qz)
            tt(v("xt", 896 * b + t, 896 * b + 768, 4), bank(b, t), v("zp", 400 * t + AT[b], 400 * t + AT[b] + H), ADD)

    def both(fn, *args):
        for b in range(2):
            pri[0], mark = 0.0, len(ops)
            fn(args[0], b, *args[1:])
            for o in ops[mark:]:
                o["first"] = 1 - b

    calm = []
    for r in range(ROUNDS):
        both(images, r)
        both(state, r)
        unpack(r - 1)
        keys(r)
        for h in range(7):
            both(level, r, h)
            calm.append(len(ops) - 1)
            if h == 3 and r < ROUNDS - 1:
                both(early, r)
                pri[0] = OPT["soon"]
                tell(r, 0)
        both(diff, r)
        if r < ROUNDS - 1:
            tell(r, 1)
        pri[0] = OPT["claim"] + OPT["last"] * (r == ROUNDS - 1)
        claims(r)
        both(layer, r)
    r = ROUNDS - 1
    quant(*pair("qvc", "qvs", 0, 128), v("vt", 0, 512))
    dma("S", "dout", inp(T.bp[:, 0:384]), rows16("bpt", 0, 128, 0, 384), 12288, 24)
    for b in range(2):
        a = AT[b]
        qf = pair("qfc", "qfs", a, a + H)
        quant(*qf, v("xt", 896 * b, 896 * b + 768))
        mx(bank(b, 0), *pair("qvc", "qvs", 0, 128), *qf)
        dma("S", "dout", inp(T.oc[:, 4 * a:4 * a + 768]), codes("qfc", a, a + H), 98304, 128)
        act(v("yt", a, a + H), bank(b, 0))
        k = dma("S", "dout", inp(T.y[:, a:a + H]), v("yt", a, a + H), 98304, 128)
        ops[k]["tail"] = OPT["lead"] * (1 - b)
    for k in range(4):
        dma("S", "dout", inp(T.osc[4 * k:4 * k + 4, :]), v("qfs", 0, 384, p=(32 * k, 32 * k + 4)))
    act(v("et1", 0, 516), v("et", 0, 516), 64.0)
    ops[-1]["after"] = (calm[OPT["calm"]],)
    for t in range(4):
        quant(*pair("ec", "es", 512 + 128 * t, 640 + 128 * t), v("et1", 3 - t, 515 - t))
        act(v("rto", t, 128, 4), v("tw", 256 * r + 64 * t, 256 * r + 64 * t + 32), -64.0)
    for t in range(4):
        b, k = 0, (t + 1) % 4
        mx(bank(b, k, 0, 128), *pair("ec", "es", 512 + 128 * t, 640 + 128 * t), *pair("lc", "ls", 32 + 32 * r, 160 + 32 * r))
        tt(v("rtt", t, 128, 4), v("rto", t, 128, 4), bank(b, k, 96, 128), ADD)
    dma("S", "dout", inp(T.rt[:]), v("rtt", 0, 128), 65536, 128)

    if not ORDER:
        ORDER.extend(arrange(ops))
    total = {}
    known = {q: {} for q in eng}
    clock = {}
    wr, rd = {}, {}

    def learn(q, sem, val):
        k = known[q]
        if k.get(sem, 0) >= val:
            return
        if sem in DMAS or sem == "loc":
            val = total[sem]
        eng[q].wait_ge(T.sem[sem], val)
        k[sem] = val
        for x, c in clock.get(sem, {}).items():
            if x == val or (sem in DMAS and x < val):
                for s2, x2 in c.items():
                    if k.get(s2, 0) < x2:
                        k[s2] = x2

    for k in ORDER:
        o = ops[k]
        q, sem, toks = o["q"], o["sem"], {}
        if o["kind"] != "a":
            for name, reg in o["ins"]:
                for e in [e for e in wr.get(name, []) if hit(reg, e[0])] + [e for e in rd.get(name, []) if name in PSUM and e[1] != q]:
                    toks[e[2]] = max(toks.get(e[2], 0), e[3])
            for name, reg in o["outs"]:
                for e in wr.get(name, []) + rd.get(name, []):
                    if name in PSUM or hit(reg, e[0]):
                        toks[e[2]] = max(toks.get(e[2], 0), e[3])
            for s in sorted(toks):
                learn(q, s, toks[s])
        total[sem] = total.get(sem, 0) + o["cnt"]
        if o["kind"] in "cd":
            clock.setdefault(sem, {})[total[sem]] = dict(known[q])
            o["fn"]().then_inc(T.sem[sem], o["cnt"])
        elif o["kind"] == "r":
            o["fn"]()
        for name, reg in o["outs"]:
            wr[name] = [e for e in wr.get(name, []) if not covers(reg, e[0])] + [(reg, q, sem, total[sem])]
            rd[name] = [e for e in rd.get(name, []) if not covers(reg, e[0])]
        for name, reg in o["ins"]:
            rd.setdefault(name, []).append((reg, q, sem, total[sem]))
    for s in sorted(total):
        if known["P"].get(s, 0) < total[s]:
            g.wait_ge(T.sem[s], total[s])
